import numpy as np, ml_dtypes
CORES = [35,38,43,46]
N = 4
import mx_ref
BF = ml_dtypes.bfloat16
def gcols(t, e):
    v = np.concatenate([t.reshape(8, 16, -1, 4), np.zeros((8, 16, 1, 4), BF)], axis=2)
    return np.ascontiguousarray(np.stack([v[g][:, e[g]] for g in range(8)])).reshape(128, -1)
def tile(rs):
    return np.stack(rs, axis=2).reshape(128, -1).astype(BF)
def pick(q, e):
    c = np.concatenate([q[0].reshape(128, -1, 4), np.zeros((128, 1, 4), np.uint8)], axis=1); s = np.concatenate([q[1], np.ones((16, 1), np.uint8)], axis=1)
    return (np.ascontiguousarray(c[:, e].reshape(128, -1)), np.ascontiguousarray(s[:, e]))
def join(*qs):
    return (np.concatenate([q[0] for q in qs], axis=1), np.concatenate([q[1] for q in qs], axis=1))
def put(q, e, v):
    c, s = q[0].reshape(128, -1, 4).copy(), q[1].copy(); c[:, e] = v[0].reshape(128, -1, 4); s[:, e] = v[1]
    return (c.reshape(128, -1), s)
def pk(c, s):
    return (np.ascontiguousarray(c), mx_ref.live(s))
def emit(q):
    return q[0], q[1]
def packed(v, rng):
    q = [mx_ref.quantize(np.ascontiguousarray(v[r])) for r in range(N)]
    return np.stack([a for a, b in q]), np.stack([mx_ref.plane(b, rng) for a, b in q])
def values_of_codes():
    e, c = np.zeros((128, 128, 4), np.float32), np.zeros((128, 2, 4), np.uint8)
    e[np.arange(128), np.arange(128), 0] = 1
    c[:127, :, 0] = np.arange(256).reshape(2, 128).T[:127]
    return mx_ref.matmul(mx_ref.quantize(e.reshape(128, 512).astype(BF)), (c.reshape(128, 8), np.full((16, 2), 127, np.uint8))).T.reshape(-1).astype(np.float64)
CODE_VALUE, SCALE_VALUE = values_of_codes(), 2.0 ** (np.arange(256) - 127.0)
def decode(q):
    return (CODE_VALUE[q[0]].reshape(16, 8, -1, 4) * SCALE_VALUE[q[1]][:, None, :, None] + 0.0).reshape(128, -1).astype(np.float32)
def f(rng, *shape):
    return mx_ref.flush((rng.standard_normal(shape, dtype=np.float32) * np.exp2(rng.integers(-2, 3, shape[:-1] + (1,)))).astype(BF))
def wide(rng, *shape, cols=0):
    v = rng.standard_normal(shape, dtype=np.float32) * np.exp2(rng.integers(-12, 13, shape)).astype(np.float32)
    if cols: v *= np.repeat(np.exp2(rng.integers(-cols, cols + 1, shape[:-2] + (1, shape[-1] // 4))) * (rng.random(shape[:-2] + (1, shape[-1] // 4)) > 0.0625), 4, axis=-1).astype(np.float32)
    return mx_ref.flush(v.astype(BF))
J, K, R = 12, 6, 3
def cycle(t, o):
    i = np.arange(len(t))
    a, b = o[:, 0], o[:, 1]
    c = np.where(t[i, a, b] == o[:, 2], o[:, 3], o[:, 2])
    m = np.zeros((len(t), 16), bool)
    for k in range(6):
        m[i, c] = True
        c = t[i, a, c]
        m[i, c] = True
        c = t[i, b, c]
    return m
def switched(t, o):
    i = np.arange(len(t))
    a, b = o[:, 0], o[:, 1]
    m = cycle(t, o)
    inside = m[:, :, None] & m[:, None, :]
    aa, bb = a[:, None, None], b[:, None, None]
    new = np.where(inside & (t == aa), bb, np.where(inside & (t == bb), aa, t))
    ra, rb = np.where(m, t[i, b], t[i, a]), np.where(m, t[i, a], t[i, b])
    new[i, a] = ra
    new[i, :, a] = ra
    new[i, b] = rb
    new[i, :, b] = rb
    return new
def numbered(e):
    return (e.reshape(N, 8, 16, J).transpose(0, 1, 3, 2) + 16 * np.arange(16)).reshape(N, 8, 16 * J)
FIELD = (((np.arange(16) + 1) % 16)[:, None] ^ ((np.arange(16) + 1) % 16)[None, :]) + 15
FIELD = FIELD % 16
def orders(rng, n):
    return np.argsort(rng.random((n, 15)), axis=1)
def renamed(rng, t):
    n = len(t)
    s = np.concatenate([orders(rng, n), np.full((n, 1), 15)], axis=1)
    k = np.argsort(s, axis=1)
    i = np.arange(n)[:, None, None]
    return s[i, t[i, k[:, :, None], k[:, None, :]]]
def systems(rng):
    t = renamed(rng, np.stack([FIELD] * (N * 128)))
    for k in range(16): t = switched(t, orders(rng, N * 128))
    return t
def stored(t):
    return t.astype(np.int32).reshape(N, 128, 256)
def big(v):
    v = v.astype(np.float32)
    v[np.abs(v) < np.float32(2.0 ** -16)] = 0
    return v.astype(BF)
def odd(rng):
    s = (N, 8, 8, 16, 16, 4)
    k = rng.integers(8, 15, s)
    k[:, :, 1, :, :, 0] = 13 + k[:, :, 1, :, :, 0] % 2
    v = (1.0 + (2 * rng.integers(0, 64, s) + 1) * 2.0 ** -7) * 2.0 ** -k.astype(float)
    v[:, :, 0, :, :, 0] = 1.96875
    return (v * (rng.integers(0, 2, s) * 2.0 - 1.0)).astype(np.float32).astype(BF)
def numbers_of(rng):
    return {"x": big(f(rng, N, 128, 1024)), "u": np.array(f(rng, N, 128, 512)), "v": np.array(f(rng, N, 128, 512))}
def weights(rng, still=[]):
    w = big(f(rng, N, 128, 2048)).reshape(N, 8, 16, 4, 8, 16, 4)
    for i in still:
        w[:, :, i] = 0
        w[:, :, :, :, :, i] = 0
    c, p = packed(w.reshape(N, 128, 2048), rng)
    return {"wc": c, "ws": p}
def setup_inputs(rng):
    return {**numbers_of(rng), "tri": stored(systems(rng)), **weights(rng)}
def setup_inputs_ties(rng):
    d = numbers_of(rng)
    x = d["x"].reshape(N, 8, 16, 16, 16, 4)
    k = rng.integers(0, 3, (N, 8, 16, 16)) - 4 * rng.integers(0, 2, (N, 8, 16, 1))
    k = np.where(rng.random((N, 8, 16, 1)) < 0.25, k[:, :, :, :1], k)
    x[:, :, 0] = 0
    x[:, :, 0, :, :, 0] = k.astype(np.float32).astype(BF)
    x[:, :, 8:] = odd(rng)
    u = d["u"].reshape(N, 128, 128, 4)
    u[:, :, ::16] = 0
    o = rng.permutation(N)
    for r in range(N):
        e = 16 * rng.permutation(8)[:2]
        for h in range(0, 128, 16): u[r, h + 9 if h in e else h, h, 0] = 0.0 if r == o[0] else -1.0 if r == o[1] else 1.0
    return {"x": x.reshape(N, 128, 1024), "u": u.reshape(N, 128, 512), "v": d["v"], "tri": stored(systems(rng)), **weights(rng, [0])}
def setup_inputs_near(rng):
    d = numbers_of(rng)
    x = d["x"].astype(np.float32).reshape(N, 8, 16, 16, 16, 4)
    x[:, :, 0] = 0
    x[:, :, 8:] = 0
    x[:, :, 0, :, :, 0] = rng.integers(0, 2, (N, 8, 16, 1)) * 2.0 - 1.0
    s = rng.integers(0, 16, (N, 8, 16, 16))
    x[:, :, 8] = ((s[..., None] >> np.arange(4)) & 1) * np.exp2(np.arange(4) - 23.0)
    u = d["u"].reshape(N, 128, 128, 4)
    u[:, :, ::16] = 0
    o = rng.permutation(N) % 4
    for r in range(N):
        k = 1.0 if o[r] == 0 else 2.0 ** -30
        if o[r] < 2: x[r, :, 11, :, :, 0] = 2.0 ** -10
        if o[r] == 2:
            a = np.zeros((8, 16, 16), np.float32)
            e = np.argsort(rng.random((8, 16, 15)), axis=2)
            np.put_along_axis(a, e[:, :, :1], 1.0, axis=2)
            np.put_along_axis(a, e[:, :, 1:2], -1.0, axis=2)
            x[r, :, 0, :, :, 0] = a
        if o[r] == 3:
            x[r, :, 8] = 0
            x[r, :, 10, :, :, 0] = rng.integers(-7, 8, (8, 16, 16)) * 2.0 ** -27
        for h in range(0, 128, 16):
            if o[r] < 2:
                u[r, h, h, 0] = k
                u[r, h + 11, h, 0] = k
            if o[r] == 2: u[r, h, h, 0] = 1.0
            if o[r] < 3: u[r, h + 8, h] = k
            else: u[r, h + 10, h, 0] = k
    return {"x": x.reshape(N, 128, 1024).astype(BF), "u": u.reshape(N, 128, 512), "v": d["v"], "tri": stored(systems(rng)), **weights(rng, [0, 8, 9, 10, 11, 12, 13, 14, 15])}
def setup_inputs_late(rng):
    d = numbers_of(rng)
    n = N * 128
    o = rng.permutation(N)
    t = systems(rng)
    for r in o[:N // 2]: t[128 * r:128 * r + 128] = renamed(rng, np.stack([FIELD] * 128))
    best = orders(rng, n)
    most = np.count_nonzero(cycle(t, best), axis=1)
    for j in range(60):
        e = orders(rng, n)
        m = np.count_nonzero(cycle(t, e), axis=1)
        best[m > most] = e[m > most]
        most = np.maximum(most, m)
    i = np.arange(n)
    third = t[i, best[:, 0], best[:, 1]]
    c = np.where(third == best[:, 2], best[:, 3], best[:, 2])
    k = np.argsort(best, axis=1).astype(float)
    k[i, c] = 1.6
    k[i[::2], third[::2]] = 1.3
    p = np.argsort(np.argsort(k, axis=1), axis=1).reshape(N, 8, 16, 15)
    s = 15.0 - p
    s[o[::2]] -= 16.0
    x = d["x"].reshape(N, 8, 16, 16, 16, 4)
    x[:, :, 0, :, :15, 0] = s.astype(np.float32).astype(BF)
    x[:, :, 8:] = odd(rng)
    u = d["u"].reshape(N, 128, 128, 4)
    u[:, :, ::16] = 0
    for h in range(0, 128, 16): u[:, h, h, 0] = 1
    return {"x": x.reshape(N, 128, 1024), "u": u.reshape(N, 128, 512), "v": d["v"], "tri": stored(t), **weights(rng)}
def setup_inputs_huge(rng):
    d = numbers_of(rng)
    q = int(rng.integers(N))
    c = rng.integers(0, 2, (N, 1, 1, 16, 16, 1)) * 2.0 - 1.0
    c[:, :, :, ::2] = c[:, :, :, ::2, :1]
    x = (0.6 + 0.06 * rng.random((N, 8, 1, 16, 16, 1)) + 0.03 * rng.random((N, 8, 16, 16, 16, 4))) * c
    s = -np.ones((16, 16))
    np.put_along_axis(s, np.argsort(rng.random((16, 15)), axis=1)[:, :3], 1.0, axis=1)
    x[q] = 0.875 * s[None, None, :, :, None]
    h = rng.integers(0, 8, (1, 16, 16, 1))
    x[q, 0, :2] *= np.where(4 * np.arange(2)[:, None, None, None] + np.arange(4) < h, 0.5, 1.0)
    a = 2.0 ** 29 * (1.0 - 0.1 * rng.random((N, 8, 16, 8, 4)))
    for g in range(8): a[:, g, :, g] *= 2.0
    a *= rng.integers(0, 2, (N, 1, 1, 8, 1)) * 2.0 - 1.0
    a[q] = 2.0 ** 30
    u = d["u"].reshape(N, 128, 128, 4)
    u[:, :, ::16] = a.reshape(N, 128, 8, 4).astype(np.float32).astype(BF)
    w = np.zeros((N, 128, 4, 128, 4), np.float32)
    i = np.arange(128)
    for b in range(4): w[:, i, b, i, b] = -1
    wc, ws = packed(w.reshape(N, 128, 2048).astype(BF), rng)
    return {"x": (2.0 ** 30 * x).astype(np.float32).reshape(N, 128, 1024).astype(BF), "u": u.reshape(N, 128, 512), "v": d["v"], "tri": stored(systems(rng)), "wc": wc, "ws": ws}
def setup_inputs_spread(rng):
    d = setup_inputs(rng)
    d["x"] = big(wide(rng, N, 128, 1024, cols=6))
    return d
def check_inputs(d):
    b = []
    for k in ("x", "u", "v"):
        a = np.abs(d[k].astype(np.float32))
        if not (np.isfinite(a).all() and ((a == 0) | (a >= 2.0 ** -30) & (a <= 2.0 ** 30)).all()): b.append("a value of " + k)
    if not ((d["tri"] >= 0) & (d["tri"] <= 15)).all(): b.append("an entry of tri")
    t = np.clip(d["tri"], 0, 15).astype(np.int64).reshape(-1, 16, 16)
    i = np.arange(16)
    if (t != t.transpose(0, 2, 1)).any() or (t[:, i, i] != 15).any() or (t[:, :, 15] != i).any() or (np.take_along_axis(t, t, axis=2) != i).any(): b.append("a table of tri that isn't one of triples")
    none, least, most = [emit(mx_ref.quantize(np.full((128, 16), k, np.float32).astype(BF)))[1][0, 0] for k in (0.0, 2.0 ** -30, 2.0 ** 30)]
    for r in range(N):
        if ((d["wc"][r] & 0x7F) == 0x7F).any(): b.append("wc: a code that is no number")
        s = mx_ref.live(d["ws"][r])
        if ((s != none) & ((s < least) | (s > most))).any(): b.append("ws: a scale out of range")
    return b
def reference(x, u, v, tri, wc, ws):
    qu = [mx_ref.quantize(u[r]) for r in range(N)]
    lay = [pk(wc[r], ws[r]) for r in range(N)]
    now = [x[r] for r in range(N)]
    t = tri.astype(np.int64).reshape(N * 128, 16, 16)
    i = np.arange(N * 128)[:, None]
    for h in range(R):
        q = [mx_ref.quantize(now[r]) for r in range(N)]
        own = [decode(q[r]).astype(BF) for r in range(N)]
        s = np.concatenate([(mx_ref.matmul(qu[r], q[r])[::16] + np.float32(0.0)).reshape(128, 16)[:, :15] for r in range(N)])
        o = np.argsort(-s, axis=1, kind="stable")
        first, second = numbered(o[:, :J]), numbered(o[:, 1:J + 1])
        third = numbered(t[i, o[:, :J], o[:, 1:J + 1]])
        z = [((gcols(own[r], second[r]).astype(np.float32) + gcols(own[r], third[r]).astype(np.float32)) * np.float32(0.5)).astype(BF) for r in range(N)]
        zq = [mx_ref.quantize(z[r]) for r in range(N)]
        for r in range(N):
            w = join(pick(zq[(r - 1) % N], np.arange(16 * K)), pick(zq[r], np.arange(16 * K, 16 * J)))
            made = tile([mx_ref.matmul(pick(lay[r], np.arange(128 * b, 128 * b + 128)), w) * np.float32(0.03125) + z[r][:, b::4].astype(np.float32) for b in range(4)]).reshape(8, 16, 16 * J, 4)
            new = np.array(own[r]).reshape(8, 16, 256, 4)
            for g in range(8): new[g][:, first[r, g]] = made[g]
            now[r] = new.reshape(128, 1024)
        t = switched(t, o)
    y, ot = np.zeros((N, 128, 256), np.float32), t.reshape(N, 128, 256).astype(np.float32)
    oc, osc = np.zeros((N, 128, 1024), np.uint8), np.zeros((N, 16, 256), np.uint8)
    for r in range(N):
        q = mx_ref.quantize(now[r])
        y[r] = mx_ref.matmul(mx_ref.quantize(v[r]), q)
        oc[r], osc[r] = emit(q)
    return {"y": y, "ot": ot, "oc": oc, "osc": osc}

@@ -1,0 +1,544 @@
+from concourse.mybir import dt, AluOpType, ActivationFunctionType
+
+A = AluOpType
+F = ActivationFunctionType
+ROUNDS = 3
+C4, U8, BF, F32, I32, U16 = "float8_e4m3fn_x4", "uint8", "bfloat16", "float32", "int32", "uint16"
+X_ON_ACT = 3
+SB = {
+    BF: dict(xin=1024, uin=512, vin=512, et=1032, idn=128, ones=512, xt=1024, ioc=192, d0r=240, kjp=240, d1o=240,
+             mk=192, nm=192, r7=224, r4=448, gg=240, rs=240, ne=240, osn=240, o16=16, ix=16, lk=192, ms=192,
+             fh=1024, a1=384, a2=576, zt=896, z32=896, yw=1024, tab=256, sq=512, ab=512, df=32, do=4, t2=2,
+             nw=224, wk=64, nc=224, ncm=16, amb=16, cd=32, pp=128, pq=128, re=128, rx=336, pa=512, pb=512),
+    F32: dict(pc=16, iop=16, w1=32, w3=32, w4=80, w5=64, lf=72, tf=67, tt=512, ap=240, rk=16, rv=32, rvt=32,
+              tabo=256, dof=2, yo=256),
+    I32: dict(trii=256, pi=4, w2=32),
+    U16: dict(lu=72, tu=67, ixu=16, offo=18, offm=12, offr=16),
+    C4: dict(wq=512, qu=128, qv=128, qe=512, qn=256, qp=272, qx=256, qs0=128, qs1=128, qs2=128, qa0=224, qa1=224, qa2=224),
+    U8: dict(wsc=512, su=128, sv=128, se=512, sn=256, sp=272, sx=256, ss0=128, ss1=128, ss2=128, sa0=224, sa1=224, sa2=224),
+}
+SCRATCH = {name: ("sbuf", [128, n], t) for t, d in SB.items() for name, n in d.items()}
+SCRATCH.update({"psS": ("psum", [128, 512], F32), "psF": ("psum", [128, 2048], F32), "psY": ("psum", [128, 1536], F32)})
+SEMAPHORES = ["cv", "cs", "ct", "cg", "sent"] + ["arr%d" % r for r in range(ROUNDS)] + ["dm%d" % k for k in range(16)]
+COUNTER = {"v": "cv", "s": "cs", "t": "ct", "g": "cg"}
+
+
+def V(name, a=0, b=None, s=1):
+    return (name, a, SCRATCH[name][1][1] if b is None else b, s)
+
+
+def C(name, a):
+    return (name, a, a + 1, 1)
+
+
+def I(win, off):
+    return ("@", win, off)
+
+
+def is_view(x):
+    return isinstance(x, tuple)
+
+
+def schedule(ops, g, T):
+    queue = {"v": g.vector, "s": g.scalar, "t": g.tensor, "g": g, "y": g.sync}
+    writer, readers = {}, {}
+
+    def cells(v):
+        name, a, b, s = v
+        if SCRATCH[name][0] == "psum":
+            return [(name, k) for k in range(a // 512, (b - 1) // 512 + 1)]
+        return [(name, k) for k in range(a, b, s)]
+
+    deps = []
+    for i, op in enumerate(ops):
+        d = set()
+        rd = [c for v in op["r"] for c in cells(v)]
+        wr = [c for v in op["w"] for c in cells(v)]
+        for c in rd:
+            if c in writer:
+                d.add(writer[c])
+            if SCRATCH[c[0]][0] == "psum":
+                d.update(j for j in readers.get(c, ()) if ops[j]["q"] != op["q"])
+        for c in wr:
+            if c in writer:
+                d.add(writer[c])
+            d.update(readers.get(c, ()))
+        for c in rd:
+            readers.setdefault(c, set()).add(i)
+        for c in wr:
+            writer[c] = i
+            readers[c] = set()
+        d.discard(i)
+        deps.append(d)
+    known = {q: set() for q in queue}
+    clock, waits = [], []
+    for i, op in enumerate(ops):
+        if op["kind"] == "arrive":
+            clock.append(set())
+            waits.append([])
+            continue
+        k = known[op["q"]]
+        mine = []
+        for j in sorted(deps[i], reverse=True):
+            if j in k:
+                continue
+            mine.append(j)
+            k.add(j)
+            k.update(clock[j])
+            if ops[j]["kind"] == "compute":
+                for e in range(j):
+                    if ops[e]["kind"] == "compute" and ops[e]["q"] == ops[j]["q"] and e not in k:
+                        k.add(e)
+                        k.update(clock[e])
+        waits.append(mine)
+        clock.append(set(k))
+    needed = set(j for w in waits for j in w)
+    token, count, ndma, open_dma = {}, {q: 0 for q in COUNTER}, [0], []
+    for i, op in enumerate(ops):
+        if op["kind"] == "arrive":
+            token[i] = (op["sem"], op["n"])
+        elif op["kind"] == "compute" and i in needed:
+            count[op["q"]] += 1
+            token[i] = (COUNTER[op["q"]], count[op["q"]])
+        elif op["kind"] == "dma":
+            token[i] = ("dm%d" % ndma[0], 16)
+            ndma[0] += 1
+            if i not in needed:
+                open_dma.append(i)
+    for i, op in enumerate(ops):
+        if op["kind"] == "arrive":
+            continue
+        q = queue[op["q"]]
+        for j in waits[i]:
+            q.wait_ge(T.sem[token[j][0]], token[j][1])
+        ins = op["f"](q)
+        if i in token:
+            ins.then_inc(T.sem[token[i][0]], 16 if op["kind"] == "dma" else 1)
+    for i in open_dma:
+        queue[ops[i]["q"]].wait_ge(T.sem[token[i][0]], 16)
+
+
+def rank_program(g, core, T, topo):
+    rank = T.rank_of(core)
+    if rank is None:
+        return
+    n = len(T.cores)
+    nxt, prv = T.cores[(rank + 1) % n], T.cores[(rank - 1) % n]
+    rid, pid, _ = topo.addr(nxt)
+    mask = topo.mask(core, nxt)
+    n_out, n_in = len(topo.engines(core, nxt)), len(topo.engines(prv, core))
+    ops = []
+
+    def ap(x, word=None):
+        if not is_view(x):
+            return x
+        if x[0] == "@":
+            return ap(x[1], word).indirect(ap(x[2]))
+        name, a, b, s = x
+        v = T[name][:, a:b] if s == 1 else T[name][:, a:b:s]
+        return v.bitcast(word) if word is not None else v
+
+    def flat(xs):
+        out = []
+        for x in xs:
+            if is_view(x):
+                out += [x[1], x[2]] if x[0] == "@" else [x]
+        return out
+
+    def rec(q, f, r, w, kind="compute"):
+        ops.append({"q": q, "f": f, "r": flat(r), "w": flat(w), "kind": kind})
+
+    def cp(o, i, word=None):
+        rec("v", lambda q: q.tensor_copy(ap(o, word), ap(i, word)), [i], [o])
+
+    def tt(o, a, b, op):
+        rec("v", lambda q: q.tensor_tensor(ap(o), ap(a), ap(b), op), [a, b], [o])
+
+    def ts(o, a, s1, op0, s2=None, op1=None):
+        if op1 is None:
+            rec("v", lambda q: q.tensor_scalar(ap(o), ap(a), ap(s1), None, op0), [a, s1], [o])
+        else:
+            rec("v", lambda q: q.tensor_scalar(ap(o), ap(a), ap(s1), ap(s2), op0, op1), [a, s1, s2], [o])
+
+    def scan(o, d0, d1, op0, op1):
+        rec("v", lambda q: q.tensor_tensor_scan(ap(o), ap(d0), ap(d1), 0.0, op0, op1), [d0, d1], [o])
+
+    def mset(o, c):
+        rec("v", lambda q: q.memset(ap(o), c), [], [o])
+
+    def tr(o, i):
+        rec("v", lambda q: q.transpose(ap(o), ap(i)), [i], [o])
+
+    def quant(qc, sc, i):
+        rec("v", lambda q: q.quantize_mx(ap(qc), ap(sc), ap(i)), [i], [qc, sc])
+
+    def act(o, i, scale=None, func=F.Copy, bias=None):
+        kw = {}
+        if scale is not None:
+            kw["scale"] = ap(scale)
+        if bias is not None:
+            kw["bias"] = ap(bias)
+        rec("s", lambda q: q.activation(ap(o), ap(i), func, **kw), [i, bias, scale], [o])
+
+    def lin(o, i, scale, bias):
+        act(o, i, scale, F.Identity, bias)
+
+    def mm(o, lq, ls, rq, rsc):
+        rec("t", lambda q: q.matmul_mx(ap(o), ap(lq), ap(ls), ap(rq), ap(rsc), True, True), [lq, ls, rq, rsc], [o])
+
+    def iota(o, pattern, base, cm, small=True):
+        if small:
+            rec("g", lambda q: q.iota(ap(o), pattern, base, cm, allow_small_or_imprecise_dtypes=True), [], [o])
+        else:
+            rec("g", lambda q: q.iota(ap(o), pattern, base, cm), [], [o])
+
+    def select(o, i, pattern, op, fill, base=0, cm=0):
+        rec("g", lambda q: q.affine_select(ap(o), ap(i), pattern, op, fill, base, cm), [i], [o])
+
+    def load(q, o, src, word=None, after=()):
+        rec(q, lambda e: e.dma_start(ap(o, word), src), list(after), [o], "dma")
+
+    def store(q, dst, src, reads):
+        rec(q, lambda e: e.dma_start(dst, src), reads, [], "dma")
+
+    def send(dst, src, sem, word=None):
+        rec("g", lambda q: q.remote_dma(ap(dst, word), ap(src, word), T.sem[sem], T.sem.sent, pid, rid, mask),
+            [src], [], "remote")
+
+    load("y", V("xin"), T.x[:])
+    load("s", V("uin"), T.u[:])
+    load("y", V("trii"), T.tri[:], None, [C("xin", 0)])
+    load("y", V("wq"), T.wc[:], dt.uint8)
+    load("y", V("wsc"), T.ws[:])
+    load("y", V("vin"), T.v[:])
+
+    q_, h_, p32, c16, c16q = C("pc", 0), C("pc", 1), C("pc", 2), C("pc", 3), C("pc", 4)
+    iota(C("pi", 0), [[0, 1]], 0, 1, False)
+    iota(V("iop"), [[1, 16]], 0, 0)
+    mset(V("ones"), 1.0)
+    select(V("idn"), V("ones", 0, 128), [[-1, 128]], A.is_equal, 0.0, 0, 1)
+    iota(V("ioc"), [[0, 12], [1, 16]], 0, 0)
+    select(V("d0r"), V("ones", 0, 240), [[1, 15], [-1, 16]], A.not_equal, -1.0)
+    select(V("d0r"), V("d0r"), [[0, 15], [1, 16]], A.is_gt, 0.0)
+    iota(V("kjp"), [[1, 15], [-1, 16]], 0, 0)
+    select(V("kjp"), V("kjp"), [[0, 15], [-1, 16]], A.is_gt, 99.0, 15)
+    select(V("nm"), V("ones", 0, 192), [[0, 12], [1, 16]], A.is_gt, 0.0)
+    iota(V("zt", 384, 512), [[0, 128]], 0, 0)
+    iota(V("pa", 0, 64), [[1, 16], [0, 4]], 0, 0)
+    iota(V("sq", 240, 256), [[256, 16]], 0, 0)
+    iota(V("sq", 496, 512), [[256, 16]], 0, 0)
+    act(V("et", 0, 512), V("ones"), 0.0)
+    act(V("et", 512, 1024), V("ones"), 0.0)
+    mset(V("et", 1024, 1032), 0.0)
+    ts(C("pi", 1), C("pi", 0), 15, A.bitwise_and)
+    ts(C("pi", 2), C("pi", 0), 4, A.arith_shift_right, 1, A.bitwise_and)
+    ts(C("pi", 3), C("pi", 0), 31, A.bitwise_and)
+    mset(V("lf"), 0.0)
+    cp(V("pc", 0, 3), V("pi", 1, 4))
+    mset(V("w1", 15, 32, 16), 0.0)
+    ts(V("w1", 0, 15), V("iop", 0, 15), q_, A.max, 1.0, A.add)
+    ts(V("w1", 16, 31), V("iop", 0, 15), q_, A.min, 1.0, A.add)
+    ts(c16q, q_, 16.0, A.mult)
+    mset(C("lf", 68), 30.0)
+    ts(V("w2"), V("w1"), h_, A.add)
+    ts(V("lf", 1, 16), V("iop", 0, 15), c16q, A.add)
+    ts(C("lf", 0), c16q, 15.0, A.add)
+    ts(V("w2"), V("w2"), 1, A.bitwise_and)
+    ts(C("pc", 5), c16q, 14.0, A.add, 238.0, A.min)
+    mset(C("lf", 69), 14.0)
+    ts(V("w3"), V("w2"), 15.0, A.mult)
+    ts(V("lf", 50, 65), V("iop", 0, 15), 0.0, A.mult, C("pc", 5), A.add)
+    cp(C("lf", 66), p32)
+    tt(V("w3"), V("w3"), V("w1"), A.add)
+    ts(c16, q_, 16.0, A.add)
+    ts(V("lf", 18, 50), V("w3"), 16.0, A.mult)
+    mset(V("d1o"), -1.0)
+    cp(V("lu"), V("lf"))
+    l_pick, l_a, l_b, l_n = V("lu", 0, 17), V("lu", 18, 33), V("lu", 34, 49), V("lu", 50, 65)
+    l_32, l_w = V("lu", 66, 67), V("lu", 68, 70)
+    act(V("et", 2, 514, 4), V("idn"))
+    act(V("et", 519, 1031, 4), V("idn"))
+    mset(V("d1o", 15, 240, 16), 15.0)
+    for b in range(4):
+        o = 516 * (b % 2) + (2 if b < 2 else 0)
+        quant(V("qe", 128 * b, 128 * b + 128), V("se", 128 * b, 128 * b + 128), V("et", o, o + 512))
+    lin(C("pc", 6), q_, 1.0, 1.0)
+    lin(C("pc", 7), q_, 64.0, 0.0)
+    lin(C("pc", 8), q_, 4.0, 963.0)
+    lin(C("pc", 9), q_, 1.0, 240.0)
+    lin(V("w4", 0, 7), V("iop", 0, 7), 1.0, C("pc", 6))
+    lin(V("w4", 16, 32), V("iop"), -64.0, C("pc", 7))
+    lin(V("w4", 32, 48), V("iop"), 4.0, 3.0)
+    lin(V("tf", 0, 8), V("iop", 0, 8), 0.0, q_)
+    lin(V("tf", 14, 24), V("iop", 0, 10), 0.0, q_)
+    lin(V("tf", 31, 44), V("iop", 0, 13), 0.0, c16)
+    lin(V("rv", 15, 32, 16), V("iop", 0, 2), 0.0, C("pc", 9))
+    lin(C("tf", 59), q_, 4.0, 3.0)
+    quant(V("qu"), V("su"), V("uin"))
+    quant(V("qn"), V("sn"), V("xin"))
+    cp(V("qp"), I(V("qn"), l_pick), dt.uint32)
+    act(V("sp"), I(V("sn"), l_pick))
+
+    def constants_1():
+        ts(V("w4", 8, 15), V("w4", 0, 7), 15.0, A.is_ge, -15.0, A.mult)
+        ts(V("w5", 0, 16), V("w4", 16, 32), 0.0, A.is_lt, 960.0, A.mult)
+        ts(C("pc", 10), q_, 15.0, A.is_equal)
+        tt(V("tf", 7, 14), V("w4", 0, 7), V("w4", 8, 15), A.add)
+        tt(V("w5", 0, 16), V("w5", 0, 16), V("w4", 16, 32), A.add)
+        lin(V("w5", 32, 48), V("w4", 32, 48), C("pc", 10), 0.0)
+        lin(V("tf", 24, 31), V("tf", 7, 14), 1.0, 16.0)
+        lin(V("w5", 16, 32), V("w5", 0, 16), -1.0, C("pc", 8))
+        lin(V("tf", 60, 67), V("tf", 7, 14), 1.0, c16q)
+
+    def constants_2():
+        tt(V("w4", 48, 64), V("w5", 0, 16), V("w4", 32, 48), A.add)
+        ts(C("pc", 11), q_, 15.0, A.not_equal)
+        tt(V("w4", 48, 64), V("w4", 48, 64), V("w5", 16, 32), A.min)
+        ts(V("mk"), V("ioc"), q_, A.is_equal)
+        ts(V("w4", 48, 64), V("w4", 48, 64), 63.0, A.max, C("pc", 11), A.mult)
+        cp(C("offo", 16), q_)
+        tt(V("tf", 44, 59), V("w4", 48, 63), V("w5", 32, 47), A.add)
+
+    l_exy, l_exp = V("tu", 0, 14), V("tu", 44, 60)
+    l_term = [V("tu", 16, 23), V("tu", 24, 31), V("tu", 32, 39)]
+
+    def o_(j):
+        return C("osn", 16 * j + 15)
+
+    def walk(s):
+        if s == 0:
+            ts(V("nw", 0, 224, 7), V("ioc", 0, 32), C("t2", 0), A.add, o_(2), A.not_equal)
+        else:
+            k = 32 * ((s - 1) % 2)
+            tt(V("nw", s, 224, 7), I(V("wk", k, k + 32), l_w), V("ioc", 0, 32), A.not_equal)
+
+    def step(s):
+        k = 32 * (s % 2)
+        scan(V("wk", k, k + 32), V("nw", s, 224, 7), V("df"), A.mult, A.add)
+
+    def cycle_done():
+        scan(V("nc"), V("r7"), V("nw"), A.max, A.min)
+        tt(V("ncm"), V("nc", 6, 112, 7), V("nc", 118, 224, 7), A.min)
+        ts(V("cd", 0, 16), V("ncm"), -1.0, A.add)
+        tt(V("cd", 16, 32), V("cd", 0, 16), V("amb"), A.mult)
+
+    def term(r, t):
+        tt(V("pb" if r % 2 else "pa", 64 + t, 512, 4), I(V("cd"), l_term[t]), V("rx", 112 * t, 112 * t + 112), A.mult)
+
+    def table_sum(r):
+        old, new = ("pb", "pa") if r % 2 else ("pa", "pb")
+        scan(V(new, 64, 512), V("r4"), V(old, 64, 512), A.mult, A.add)
+
+    ybank = [V("psS"), V("psY", 0, 512), V("psY", 512, 1024), V("psY", 1024, 1536)]
+
+    for r in range(ROUNDS):
+        last = r == ROUNDS - 1
+        qs, ss, qa, sa = "qs%d" % r, "ss%d" % r, "qa%d" % r, "sa%d" % r
+        qx, sx, ns = ("qp", "sp", 272) if r == 0 else ("qx", "sx", 256)
+        table = V("trii") if r == 0 else V("tab")
+        cur = "pb" if r % 2 else "pa"
+
+        def plane(b):
+            return V("fh", 256 * b, 256 * b + 256)
+
+        def evac(b):
+            act(plane(b), V("psF", 512 * b, 512 * b + 256), 0.5)
+
+        def squares():
+            act(V("sq", 0, 240), V("tab", 0, 240), -16.0, F.Square, C("o16", 0))
+            act(V("sq", 256, 496), V("tab", 0, 240), -16.0, F.Square, C("o16", 1))
+
+        def second():
+            for b in range(4):
+                act(V("a2", 144 * b, 144 * b + 144), I(plane(b), V("offo", 8, 17)))
+
+        def is_point(o, j):
+            ts(V(o), V(cur, 3, 512, 4), o_(j), A.is_equal)
+
+        def rows():
+            scan(V("ab"), V("sq"), V("ones"), A.min, A.add)
+
+        def signs():
+            tt(V("re"), V("pp"), V("pq"), A.subtract)
+
+        def diffs():
+            tt(V("df", 0, 31), V("ab", 31, 512, 16), V("ab", 15, 496, 16), A.subtract)
+            tt(V("amb"), V("ab", 271, 512, 16), V("ab", 15, 256, 16), A.subtract)
+
+        def blend2(b):
+            tt(V("zt", 512 + b, 896, 4), I(plane(b), V("offm", 6, 12)), V("a2", 144 * b, 144 * b + 96), A.add)
+
+        def own(b):
+            tt(V("yw", 256 * b + 96, 256 * b + 192), (ybank[b][0], ybank[b][1] + 32, ybank[b][1] + 128, 1),
+               V("z32", 512 + b, 896, 4), A.add)
+
+        def after_blend():
+            quant(V(qa, 96, 224), V(sa, 96, 224), V("zt", 384, 896))
+            act(V("z32", 512, 896), V("zt", 512, 896), 32.0)
+            for b in range(4):
+                mm((ybank[b][0], ybank[b][1], ybank[b][1] + 128, 1), V("wq", 128 * b, 128 * b + 128),
+                   V("wsc", 128 * b, 128 * b + 128), V(qa, 96, 224), V(sa, 96, 224))
+
+        def kept():
+            act(V("z32", 0, 384), V("zt", 0, 384), 32.0)
+            for b in range(4):
+                act(V("yw", 256 * b + 192, 256 * b + 256), V("a2", 144 * b + 80, 144 * b + 144), 64.0)
+
+        def factors():
+            act(C("dof", 0), C("do", 0))
+            act(V("rx", 112, 336), I(V("re", 0, 16), l_exy))
+            act(V("rx", 0, 112), V("re", 16, 128), C("dof", 0), F.Identity)
+
+        mm(V("psS", 0, ns), V("qu"), V("su"), V(qx, 0, ns), V(sx, 0, ns))
+        for b in range(4):
+            mm(V("psF", 512 * b, 512 * b + 256), V("qe", 128 * b, 128 * b + 128), V("se", 128 * b, 128 * b + 128),
+               V(qx, 0, 256), V(sx, 0, 256))
+        if r == 0:
+            constants_1()
+        else:
+            term(r - 1, 1)
+        tr(V("tt", 0, 256), V("psS", 0, 256))
+        tr(V("tt", 256, 512), V("psS", 16, 272))
+        if r > 0:
+            evac(0)
+        act(V("ap"), I(V("tt"), l_a))
+        if r == 0:
+            constants_2()
+            evac(0)
+            evac(1)
+        else:
+            term(r - 1, 2)
+            table_sum(r - 1)
+            evac(1)
+            act(V("tab"), I(V(cur), l_exp))
+        evac(2)
+        evac(3)
+        if r == 0:
+            act(V("pa", 64, 512), V("ones", 0, 448), 0.0)
+        tt(V("gg"), I(V("tt"), l_b), V("ap"), A.is_lt)
+        if r == 0:
+            cp(V("tu"), V("tf"))
+        scan(V("rs"), V("d0r"), V("gg"), A.mult, A.add)
+        if r == 0:
+            cp(C("offr", 0), C("pc", 9))
+        tt(V("ne"), I(V("rs"), l_n), V("kjp"), A.not_equal)
+        if r == 0:
+            mset(C("df", 31), 0.0)
+        scan(V("osn"), V("ne"), V("d1o"), A.mult, A.add)
+        ts(V("o16", 0, 15), V("osn", 15, 240, 16), 16.0, A.mult)
+        ts(V("offo", 1, 16), V("osn", 15, 240, 16), 16.0, A.mult, c16, A.add)
+        tt(V("ix", 0, 12), V("o16", 0, 12), V("osn", 31, 208, 16), A.add)
+        tt(V("rk", 0, 15), V("rs", 14, 240, 16), V("iop", 0, 15), A.add)
+        cp(V("ixu", 0, 12), V("ix", 0, 12))
+        tt(V("do", 0, 3), V("osn", 15, 48, 16), V("osn", 31, 64, 16), A.subtract)
+        tt(V("lk"), I(table, V("ixu", 0, 12)), V("mk"), A.mult)
+        if last:
+            ts(V("rv", 0, 15), V("rk", 0, 15), 16.0, A.mult, q_, A.add)
+        else:
+            ts(V("offr", 1, 16), V("rk", 0, 15), 16.0, A.mult, q_, A.add)
+        scan(V("ms"), V("nm"), V("lk"), A.mult, A.add)
+        if r > 0:
+            is_point("pp", 0)
+        ts(V("offm"), V("ms", 15, 192, 16), 16.0, A.mult, c16, A.add)
+        ts(C("t2", 0), C("ms", 15), o_(2), A.is_equal, C("do", 2), A.mult)
+        for b in range(4):
+            act(V("a1", 96 * b, 96 * b + 96), I(plane(b), V("offo", 2, 8)))
+        for b in range(4):
+            tt(V("zt", b, 384, 4), I(plane(b), V("offm", 0, 6)), V("a1", 96 * b, 96 * b + 96), A.add)
+        walk(0)
+        quant(V(qs), V(ss), V("zt", 0, 512))
+        send(V(qa, 0, 96), V(qs, 0, 96), "arr%d" % r, dt.uint8)
+        send(V(sa, 0, 96), V(ss, 0, 96), "arr%d" % r)
+        ops.append({"kind": "arrive", "q": None, "r": [], "w": [V(qa, 0, 96), V(sa, 0, 96)], "sem": "arr%d" % r, "n": 2 * n_in})
+        if r == 0:
+            select(V("r7"), V("ones", 0, 224), [[0, 32], [1, 7]], A.is_equal, 0.0)
+            iota(V("pb", 0, 64), [[1, 16], [0, 4]], 0, 0)
+            select(V("r4"), V("ones", 0, 448), [[0, 112], [1, 4]], A.is_gt, 0.0)
+            second()
+            cp(V("pa", 67, 512, 4), I(V("trii"), V("tu", 60, 67)))
+            act(V("tab"), I(V(cur), l_exp))
+            squares()
+            for b in range(4):
+                blend2(b)
+            after_blend()
+            kept()
+            is_point("pp", 0)
+            is_point("pq", 1)
+            rows()
+            signs()
+            factors()
+            diffs()
+            quant(V("qv"), V("sv"), V("vin"))
+            for s in range(6):
+                step(s)
+                if s < 4:
+                    own(s)
+                walk(s + 1)
+        else:
+            squares()
+            second()
+            is_point("pq", 1)
+            rows()
+            signs()
+            diffs()
+            kept()
+            if last:
+                ts(V("rv", 16, 31), V("rk", 0, 15), 16.0, A.mult, q_, A.add)
+            step(0)
+            blend2(0)
+            walk(1)
+            blend2(1)
+            step(1)
+            blend2(2)
+            walk(2)
+            blend2(3)
+            step(2)
+            after_blend()
+            factors()
+            walk(3)
+            if last:
+                tr(V("rvt"), V("rv"))
+            step(3)
+            if last:
+                cp(V("offr"), I(V("rvt"), l_32))
+            walk(4)
+            own(0)
+            step(4)
+            own(1)
+            walk(5)
+            own(2)
+            step(5)
+            own(3)
+            walk(6)
+        for b in range(4):
+            mm(V("psF", 512 * b, 512 * b + 128), V("wq", 128 * b, 128 * b + 128), V("wsc", 128 * b, 128 * b + 128),
+               V(qa, 0, 128), V(sa, 0, 128))
+        for b in range(4):
+            tt(V("yw", 256 * b, 256 * b + 96), V("psF", 512 * b, 512 * b + 96), V("z32", b, 384, 4), A.add)
+        for b in range(4):
+            src = I(V("yw", 256 * b, 256 * b + 256), V("offr"))
+            if b < X_ON_ACT or last:
+                act(V("xt", b, 1024, 4), src, 0.03125)
+            else:
+                ts(V("xt", b, 1024, 4), src, 0.03125, A.mult)
+        cycle_done()
+        term(r, 0)
+        if last:
+            term(r, 1)
+            term(r, 2)
+            table_sum(r)
+            act(V("tabo"), I(V("pa" if r % 2 else "pb"), l_exp))
+        quant(V("qx"), V("sx"), V("xt"))
+
+    mm(V("psS", 0, 128), V("qv"), V("sv"), V("qx", 0, 128), V("sx", 0, 128))
+    mm(V("psY", 0, 128), V("qv"), V("sv"), V("qx", 128, 256), V("sx", 128, 256))
+    store("y", T.oc[:], T.qx[:].bitcast(dt.uint8), [V("qx")])
+    store("y", T.ot[:], T.tabo[:], [V("tabo")])
+    cp(V("yo", 0, 128), V("psS", 0, 128))
+    act(V("yo", 128, 256), V("psY", 0, 128))
+    store("s", T.y[:], T.yo[:], [V("yo")])
+    for k in range(4):
+        store("y", T.osc[4 * k:4 * k + 4, :], T.sx[32 * k:32 * k + 4, :], [V("sx")])
+
+    schedule(ops, g, T)
+    g.wait_ge(T.sem.sent, 2 * ROUNDS * n_out)

@@ -4,7 +4,7 @@ A = AluOpType
 F = ActivationFunctionType
 ROUNDS = 3
 C4, U8, BF, F32, I32, U16 = "float8_e4m3fn_x4", "uint8", "bfloat16", "float32", "int32", "uint16"
-X_ON_ACT = 3
+X_ON_ACT = (2, 2, 3)
 SB = {
     BF: dict(xin=1024, uin=512, vin=512, et=1032, idn=128, ones=512, xt=1024, ioc=192, d0r=240, kjp=240, d1o=240,
              mk=192, nm=192, r7=224, r4=448, gg=240, rs=240, ne=240, osn=240, o16=16, ix=16, lk=192, ms=192,
@@ -219,14 +219,14 @@ def rank_program(g, core, T, topo):
     select(V("idn"), V("ones", 0, 128), [[-1, 128]], A.is_equal, 0.0, 0, 1)
     iota(V("ioc"), [[0, 12], [1, 16]], 0, 0)
     select(V("d0r"), V("ones", 0, 240), [[1, 15], [-1, 16]], A.not_equal, -1.0)
-    select(V("d0r"), V("d0r"), [[0, 15], [1, 16]], A.is_gt, 0.0)
     iota(V("kjp"), [[1, 15], [-1, 16]], 0, 0)
+    select(V("d0r"), V("d0r"), [[0, 15], [1, 16]], A.is_gt, 0.0)
     select(V("kjp"), V("kjp"), [[0, 15], [-1, 16]], A.is_gt, 99.0, 15)
-    select(V("nm"), V("ones", 0, 192), [[0, 12], [1, 16]], A.is_gt, 0.0)
-    iota(V("zt", 384, 512), [[0, 128]], 0, 0)
     iota(V("pa", 0, 64), [[1, 16], [0, 4]], 0, 0)
+    select(V("nm"), V("ones", 0, 192), [[0, 12], [1, 16]], A.is_gt, 0.0)
     iota(V("sq", 240, 256), [[256, 16]], 0, 0)
     iota(V("sq", 496, 512), [[256, 16]], 0, 0)
+    iota(V("zt", 384, 512), [[0, 128]], 0, 0)
     act(V("et", 0, 512), V("ones"), 0.0)
     act(V("et", 512, 1024), V("ones"), 0.0)
     mset(V("et", 1024, 1032), 0.0)
@@ -234,41 +234,47 @@ def rank_program(g, core, T, topo):
     ts(C("pi", 2), C("pi", 0), 4, A.arith_shift_right, 1, A.bitwise_and)
     ts(C("pi", 3), C("pi", 0), 31, A.bitwise_and)
     mset(V("lf"), 0.0)
-    cp(V("pc", 0, 3), V("pi", 1, 4))
     mset(V("w1", 15, 32, 16), 0.0)
+    cp(V("pc", 0, 3), V("pi", 1, 4))
+    mset(V("d1o"), -1.0)
+    mset(C("lf", 68), 30.0)
     ts(V("w1", 0, 15), V("iop", 0, 15), q_, A.max, 1.0, A.add)
     ts(V("w1", 16, 31), V("iop", 0, 15), q_, A.min, 1.0, A.add)
     ts(c16q, q_, 16.0, A.mult)
-    mset(C("lf", 68), 30.0)
+    mset(C("lf", 69), 14.0)
+    ts(c16, q_, 16.0, A.add)
     ts(V("w2"), V("w1"), h_, A.add)
     ts(V("lf", 1, 16), V("iop", 0, 15), c16q, A.add)
     ts(C("lf", 0), c16q, 15.0, A.add)
-    ts(V("w2"), V("w2"), 1, A.bitwise_and)
     ts(C("pc", 5), c16q, 14.0, A.add, 238.0, A.min)
-    mset(C("lf", 69), 14.0)
+    ts(V("w2"), V("w2"), 1, A.bitwise_and)
+    cp(C("lf", 66), p32)
+    mset(V("d1o", 15, 240, 16), 15.0)
     ts(V("w3"), V("w2"), 15.0, A.mult)
     ts(V("lf", 50, 65), V("iop", 0, 15), 0.0, A.mult, C("pc", 5), A.add)
-    cp(C("lf", 66), p32)
-    tt(V("w3"), V("w3"), V("w1"), A.add)
-    ts(c16, q_, 16.0, A.add)
-    ts(V("lf", 18, 50), V("w3"), 16.0, A.mult)
-    mset(V("d1o"), -1.0)
-    cp(V("lu"), V("lf"))
     l_pick, l_a, l_b, l_n = V("lu", 0, 17), V("lu", 18, 33), V("lu", 34, 49), V("lu", 50, 65)
     l_32, l_w = V("lu", 66, 67), V("lu", 68, 70)
     act(V("et", 2, 514, 4), V("idn"))
     act(V("et", 519, 1031, 4), V("idn"))
-    mset(V("d1o", 15, 240, 16), 15.0)
-    for b in range(4):
+
+    def unit(b):
         o = 516 * (b % 2) + (2 if b < 2 else 0)
         quant(V("qe", 128 * b, 128 * b + 128), V("se", 128 * b, 128 * b + 128), V("et", o, o + 512))
+
+    tt(V("w3"), V("w3"), V("w1"), A.add)
+    unit(0)
+    ts(V("lf", 18, 50), V("w3"), 16.0, A.mult)
+    unit(2)
+    cp(V("lu"), V("lf"))
+    unit(1)
+    unit(3)
     lin(C("pc", 6), q_, 1.0, 1.0)
     lin(C("pc", 7), q_, 64.0, 0.0)
     lin(C("pc", 8), q_, 4.0, 963.0)
     lin(C("pc", 9), q_, 1.0, 240.0)
+    lin(V("w4", 32, 48), V("iop"), 4.0, 3.0)
     lin(V("w4", 0, 7), V("iop", 0, 7), 1.0, C("pc", 6))
     lin(V("w4", 16, 32), V("iop"), -64.0, C("pc", 7))
-    lin(V("w4", 32, 48), V("iop"), 4.0, 3.0)
     lin(V("tf", 0, 8), V("iop", 0, 8), 0.0, q_)
     lin(V("tf", 14, 24), V("iop", 0, 10), 0.0, q_)
     lin(V("tf", 31, 44), V("iop", 0, 13), 0.0, c16)
@@ -278,11 +284,13 @@ def rank_program(g, core, T, topo):
     quant(V("qn"), V("sn"), V("xin"))
     cp(V("qp"), I(V("qn"), l_pick), dt.uint32)
     act(V("sp"), I(V("sn"), l_pick))
+    act(V("pa", 64, 512), V("ones", 0, 448), 0.0)
 
     def constants_1():
         ts(V("w4", 8, 15), V("w4", 0, 7), 15.0, A.is_ge, -15.0, A.mult)
         ts(V("w5", 0, 16), V("w4", 16, 32), 0.0, A.is_lt, 960.0, A.mult)
         ts(C("pc", 10), q_, 15.0, A.is_equal)
+        ts(C("pc", 11), q_, 15.0, A.not_equal)
         tt(V("tf", 7, 14), V("w4", 0, 7), V("w4", 8, 15), A.add)
         tt(V("w5", 0, 16), V("w5", 0, 16), V("w4", 16, 32), A.add)
         lin(V("w5", 32, 48), V("w4", 32, 48), C("pc", 10), 0.0)
@@ -292,14 +300,14 @@ def rank_program(g, core, T, topo):
 
     def constants_2():
         tt(V("w4", 48, 64), V("w5", 0, 16), V("w4", 32, 48), A.add)
-        ts(C("pc", 11), q_, 15.0, A.not_equal)
-        tt(V("w4", 48, 64), V("w4", 48, 64), V("w5", 16, 32), A.min)
         ts(V("mk"), V("ioc"), q_, A.is_equal)
-        ts(V("w4", 48, 64), V("w4", 48, 64), 63.0, A.max, C("pc", 11), A.mult)
         cp(C("offo", 16), q_)
-        tt(V("tf", 44, 59), V("w4", 48, 63), V("w5", 32, 47), A.add)
+        tt(V("w4", 48, 64), V("w4", 48, 64), V("w5", 16, 32), A.min)
+        cp(C("offr", 0), C("pc", 9))
+        mset(C("df", 31), 0.0)
+        ts(V("w4", 48, 64), V("w4", 48, 64), 63.0, A.max, C("pc", 11), A.mult)
 
-    l_exy, l_exp = V("tu", 0, 14), V("tu", 44, 60)
+    l_exy = V("tu", 0, 14)
     l_term = [V("tu", 16, 23), V("tu", 24, 31), V("tu", 32, 39)]
 
     def o_(j):
@@ -316,10 +324,10 @@ def rank_program(g, core, T, topo):
         k = 32 * (s % 2)
         scan(V("wk", k, k + 32), V("nw", s, 224, 7), V("df"), A.mult, A.add)
 
-    def cycle_done():
-        scan(V("nc"), V("r7"), V("nw"), A.max, A.min)
-        tt(V("ncm"), V("nc", 6, 112, 7), V("nc", 118, 224, 7), A.min)
+    def cd1():
         ts(V("cd", 0, 16), V("ncm"), -1.0, A.add)
+
+    def cd2():
         tt(V("cd", 16, 32), V("cd", 0, 16), V("amb"), A.mult)
 
     def term(r, t):
@@ -344,26 +352,8 @@ def rank_program(g, core, T, topo):
         def evac(b):
             act(plane(b), V("psF", 512 * b, 512 * b + 256), 0.5)
 
-        def squares():
-            act(V("sq", 0, 240), V("tab", 0, 240), -16.0, F.Square, C("o16", 0))
-            act(V("sq", 256, 496), V("tab", 0, 240), -16.0, F.Square, C("o16", 1))
-
-        def second():
-            for b in range(4):
-                act(V("a2", 144 * b, 144 * b + 144), I(plane(b), V("offo", 8, 17)))
-
         def is_point(o, j):
             ts(V(o), V(cur, 3, 512, 4), o_(j), A.is_equal)
-
-        def rows():
-            scan(V("ab"), V("sq"), V("ones"), A.min, A.add)
-
-        def signs():
-            tt(V("re"), V("pp"), V("pq"), A.subtract)
-
-        def diffs():
-            tt(V("df", 0, 31), V("ab", 31, 512, 16), V("ab", 15, 496, 16), A.subtract)
-            tt(V("amb"), V("ab", 271, 512, 16), V("ab", 15, 256, 16), A.subtract)
 
         def blend2(b):
             tt(V("zt", 512 + b, 896, 4), I(plane(b), V("offm", 6, 12)), V("a2", 144 * b, 144 * b + 96), A.add)
@@ -372,23 +362,6 @@ def rank_program(g, core, T, topo):
             tt(V("yw", 256 * b + 96, 256 * b + 192), (ybank[b][0], ybank[b][1] + 32, ybank[b][1] + 128, 1),
                V("z32", 512 + b, 896, 4), A.add)
 
-        def after_blend():
-            quant(V(qa, 96, 224), V(sa, 96, 224), V("zt", 384, 896))
-            act(V("z32", 512, 896), V("zt", 512, 896), 32.0)
-            for b in range(4):
-                mm((ybank[b][0], ybank[b][1], ybank[b][1] + 128, 1), V("wq", 128 * b, 128 * b + 128),
-                   V("wsc", 128 * b, 128 * b + 128), V(qa, 96, 224), V(sa, 96, 224))
-
-        def kept():
-            act(V("z32", 0, 384), V("zt", 0, 384), 32.0)
-            for b in range(4):
-                act(V("yw", 256 * b + 192, 256 * b + 256), V("a2", 144 * b + 80, 144 * b + 144), 64.0)
-
-        def factors():
-            act(C("dof", 0), C("do", 0))
-            act(V("rx", 112, 336), I(V("re", 0, 16), l_exy))
-            act(V("rx", 0, 112), V("re", 16, 128), C("dof", 0), F.Identity)
-
         mm(V("psS", 0, ns), V("qu"), V("su"), V(qx, 0, ns), V(sx, 0, ns))
         for b in range(4):
             mm(V("psF", 512 * b, 512 * b + 256), V("qe", 128 * b, 128 * b + 128), V("se", 128 * b, 128 * b + 128),
@@ -396,7 +369,8 @@ def rank_program(g, core, T, topo):
         if r == 0:
             constants_1()
         else:
-            term(r - 1, 1)
+            cd1()
+            cd2()
         tr(V("tt", 0, 256), V("psS", 0, 256))
         tr(V("tt", 256, 512), V("psS", 16, 272))
         if r > 0:
@@ -405,47 +379,66 @@ def rank_program(g, core, T, topo):
         if r == 0:
             constants_2()
             evac(0)
-            evac(1)
         else:
-            term(r - 1, 2)
-            table_sum(r - 1)
-            evac(1)
-            act(V("tab"), I(V(cur), l_exp))
+            for t in range(3):
+                term(r - 1, t)
+        evac(1)
         evac(2)
-        evac(3)
-        if r == 0:
-            act(V("pa", 64, 512), V("ones", 0, 448), 0.0)
         tt(V("gg"), I(V("tt"), l_b), V("ap"), A.is_lt)
         if r == 0:
-            cp(V("tu"), V("tf"))
+            tt(V("tf", 44, 59), V("w4", 48, 63), V("w5", 32, 47), A.add)
+        else:
+            table_sum(r - 1)
+            act(V("tab"), I(V(cur), V("tu", 44, 60)))
+        evac(3)
         scan(V("rs"), V("d0r"), V("gg"), A.mult, A.add)
         if r == 0:
-            cp(C("offr", 0), C("pc", 9))
+            cp(V("tu"), V("tf"))
         tt(V("ne"), I(V("rs"), l_n), V("kjp"), A.not_equal)
         if r == 0:
-            mset(C("df", 31), 0.0)
+            cp(V("pa", 67, 512, 4), I(V("trii"), V("tu", 60, 67)))
+            act(V("tab"), I(V(cur), V("tu", 44, 60)))
+        else:
+            tt(V("rk", 0, 15), V("rs", 14, 240, 16), V("iop", 0, 15), A.add)
         scan(V("osn"), V("ne"), V("d1o"), A.mult, A.add)
-        ts(V("o16", 0, 15), V("osn", 15, 240, 16), 16.0, A.mult)
-        ts(V("offo", 1, 16), V("osn", 15, 240, 16), 16.0, A.mult, c16, A.add)
-        tt(V("ix", 0, 12), V("o16", 0, 12), V("osn", 31, 208, 16), A.add)
-        tt(V("rk", 0, 15), V("rs", 14, 240, 16), V("iop", 0, 15), A.add)
-        cp(V("ixu", 0, 12), V("ix", 0, 12))
-        tt(V("do", 0, 3), V("osn", 15, 48, 16), V("osn", 31, 64, 16), A.subtract)
-        tt(V("lk"), I(table, V("ixu", 0, 12)), V("mk"), A.mult)
-        if last:
+        if r == 0:
+            tt(V("rk", 0, 15), V("rs", 14, 240, 16), V("iop", 0, 15), A.add)
+        elif last:
             ts(V("rv", 0, 15), V("rk", 0, 15), 16.0, A.mult, q_, A.add)
+            ts(V("rv", 16, 31), V("rk", 0, 15), 16.0, A.mult, q_, A.add)
         else:
             ts(V("offr", 1, 16), V("rk", 0, 15), 16.0, A.mult, q_, A.add)
+        ts(V("o16", 0, 15), V("osn", 15, 240, 16), 16.0, A.mult)
+        ts(V("offo", 1, 16), V("osn", 15, 240, 16), 16.0, A.mult, c16, A.add)
+        tt(V("do", 0, 3), V("osn", 15, 48, 16), V("osn", 31, 64, 16), A.subtract)
+        tt(V("ix", 0, 12), V("o16", 0, 12), V("osn", 31, 208, 16), A.add)
+        is_point("pp", 0)
+        is_point("pq", 1)
+        cp(V("ixu", 0, 12), V("ix", 0, 12))
+        if last:
+            tr(V("rvt"), V("rv"))
+        if r == 0:
+            ts(V("offr", 1, 16), V("rk", 0, 15), 16.0, A.mult, q_, A.add)
+        act(V("sq", 0, 240), V("tab", 0, 240), -16.0, F.Square, C("o16", 0))
+        act(V("sq", 256, 496), V("tab", 0, 240), -16.0, F.Square, C("o16", 1))
+        tt(V("lk"), I(table, V("ixu", 0, 12)), V("mk"), A.mult)
+        tt(V("re"), V("pp"), V("pq"), A.subtract)
         scan(V("ms"), V("nm"), V("lk"), A.mult, A.add)
-        if r > 0:
-            is_point("pp", 0)
+        if last:
+            cp(V("offr"), I(V("rvt"), l_32))
         ts(V("offm"), V("ms", 15, 192, 16), 16.0, A.mult, c16, A.add)
         ts(C("t2", 0), C("ms", 15), o_(2), A.is_equal, C("do", 2), A.mult)
+        scan(V("ab"), V("sq"), V("ones"), A.min, A.add)
         for b in range(4):
             act(V("a1", 96 * b, 96 * b + 96), I(plane(b), V("offo", 2, 8)))
         for b in range(4):
             tt(V("zt", b, 384, 4), I(plane(b), V("offm", 0, 6)), V("a1", 96 * b, 96 * b + 96), A.add)
-        walk(0)
+            if b == 0:
+                walk(0)
+            if b == 1:
+                tt(V("df", 0, 31), V("ab", 31, 512, 16), V("ab", 15, 496, 16), A.subtract)
+        step(0)
+        tt(V("amb"), V("ab", 271, 512, 16), V("ab", 15, 256, 16), A.subtract)
         quant(V(qs), V(ss), V("zt", 0, 512))
         send(V(qa, 0, 96), V(qs, 0, 96), "arr%d" % r, dt.uint8)
         send(V(sa, 0, 96), V(ss, 0, 96), "arr%d" % r)
@@ -454,91 +447,74 @@ def rank_program(g, core, T, topo):
             select(V("r7"), V("ones", 0, 224), [[0, 32], [1, 7]], A.is_equal, 0.0)
             iota(V("pb", 0, 64), [[1, 16], [0, 4]], 0, 0)
             select(V("r4"), V("ones", 0, 448), [[0, 112], [1, 4]], A.is_gt, 0.0)
-            second()
-            cp(V("pa", 67, 512, 4), I(V("trii"), V("tu", 60, 67)))
-            act(V("tab"), I(V(cur), l_exp))
-            squares()
-            for b in range(4):
-                blend2(b)
-            after_blend()
-            kept()
-            is_point("pp", 0)
-            is_point("pq", 1)
-            rows()
-            signs()
-            factors()
-            diffs()
+        for b in range(4):
+            act(V("a2", 144 * b, 144 * b + 144), I(plane(b), V("offo", 8, 17)))
+        act(V("z32", 0, 384), V("zt", 0, 384), 32.0)
+        for b in range(4):
+            act(V("yw", 256 * b + 192, 256 * b + 256), V("a2", 144 * b + 80, 144 * b + 144), 64.0)
+        walk(1)
+        blend2(0)
+        step(1)
+        blend2(1)
+        walk(2)
+        blend2(2)
+        step(2)
+        blend2(3)
+        walk(3)
+        quant(V(qa, 96, 224), V(sa, 96, 224), V("zt", 384, 896))
+        act(V("z32", 512, 896), V("zt", 512, 896), 32.0)
+        for b in range(4):
+            mm((ybank[b][0], ybank[b][1], ybank[b][1] + 128, 1), V("wq", 128 * b, 128 * b + 128),
+               V("wsc", 128 * b, 128 * b + 128), V(qa, 96, 224), V(sa, 96, 224))
+        act(C("dof", 0), C("do", 0))
+        act(V("rx", 112, 336), I(V("re", 0, 16), l_exy))
+        act(V("rx", 0, 112), V("re", 16, 128), C("dof", 0), F.Identity)
+        step(3)
+        if r == 0:
             quant(V("qv"), V("sv"), V("vin"))
-            for s in range(6):
-                step(s)
-                if s < 4:
-                    own(s)
-                walk(s + 1)
-        else:
-            squares()
-            second()
-            is_point("pq", 1)
-            rows()
-            signs()
-            diffs()
-            kept()
-            if last:
-                ts(V("rv", 16, 31), V("rk", 0, 15), 16.0, A.mult, q_, A.add)
-            step(0)
-            blend2(0)
-            walk(1)
-            blend2(1)
-            step(1)
-            blend2(2)
-            walk(2)
-            blend2(3)
-            step(2)
-            after_blend()
-            factors()
-            walk(3)
-            if last:
-                tr(V("rvt"), V("rv"))
-            step(3)
-            if last:
-                cp(V("offr"), I(V("rvt"), l_32))
-            walk(4)
-            own(0)
-            step(4)
-            own(1)
-            walk(5)
-            own(2)
-            step(5)
-            own(3)
+        walk(4)
+        step(4)
+        own(0)
+        own(1)
+        walk(5)
+        own(2)
+        own(3)
+        step(5)
+        if r == 0:
             walk(6)
         for b in range(4):
             mm(V("psF", 512 * b, 512 * b + 128), V("wq", 128 * b, 128 * b + 128), V("wsc", 128 * b, 128 * b + 128),
                V(qa, 0, 128), V(sa, 0, 128))
         for b in range(4):
             tt(V("yw", 256 * b, 256 * b + 96), V("psF", 512 * b, 512 * b + 96), V("z32", b, 384, 4), A.add)
+            if b == 1 and r > 0:
+                walk(6)
+        scan(V("nc"), V("r7"), V("nw"), A.max, A.min)
         for b in range(4):
             src = I(V("yw", 256 * b, 256 * b + 256), V("offr"))
-            if b < X_ON_ACT or last:
+            if b < X_ON_ACT[r]:
                 act(V("xt", b, 1024, 4), src, 0.03125)
             else:
                 ts(V("xt", b, 1024, 4), src, 0.03125, A.mult)
-        cycle_done()
-        term(r, 0)
+        tt(V("ncm"), V("nc", 6, 112, 7), V("nc", 118, 224, 7), A.min)
         if last:
-            term(r, 1)
-            term(r, 2)
-            table_sum(r)
-            act(V("tabo"), I(V("pa" if r % 2 else "pb"), l_exp))
+            cd1()
+            cd2()
         quant(V("qx"), V("sx"), V("xt"))
 
-    mm(V("psS", 0, 128), V("qv"), V("sv"), V("qx", 0, 128), V("sx", 0, 128))
-    mm(V("psY", 0, 128), V("qv"), V("sv"), V("qx", 128, 256), V("sx", 128, 256))
+    mm(V("psS", 0, 256), V("qv"), V("sv"), V("qx"), V("sx"))
     store("y", T.oc[:], T.qx[:].bitcast(dt.uint8), [V("qx")])
-    store("y", T.ot[:], T.tabo[:], [V("tabo")])
-    cp(V("yo", 0, 128), V("psS", 0, 128))
-    act(V("yo", 128, 256), V("psY", 0, 128))
+    for t in range(3):
+        term(ROUNDS - 1, t)
+    act(V("yo"), V("psS", 0, 256))
     store("s", T.y[:], T.yo[:], [V("yo")])
+    table_sum(ROUNDS - 1)
+    new = V("pa" if (ROUNDS - 1) % 2 else "pb")
+    cp(V("tabo", 0, 128), I(new, V("tu", 44, 52)))
+    act(V("tabo", 128, 256), I(new, V("tu", 52, 60)))
     for k in range(4):
         store("y", T.osc[4 * k:4 * k + 4, :], T.sx[32 * k:32 * k + 4, :], [V("sx")])
+    store("y", T.ot[:], T.tabo[:], [V("tabo")])
 
     schedule(ops, g, T)
     g.wait_ge(T.sem.sent, 2 * ROUNDS * n_out)

@@ -4,12 +4,11 @@ A = AluOpType
 F = ActivationFunctionType
 ROUNDS = 3
 C4, U8, BF, F32, I32, U16 = "float8_e4m3fn_x4", "uint8", "bfloat16", "float32", "int32", "uint16"
-X_ON_ACT = (2, 2, 3)
 SB = {
     BF: dict(xin=1024, uin=512, vin=512, et=1032, idn=128, ones=512, xt=1024, ioc=192, d0r=240, kjp=240, d1o=240,
-             mk=192, nm=192, r7=224, r4=448, gg=240, rs=240, ne=240, osn=240, o16=16, ix=16, lk=192, ms=192,
+             mk=192, nm=192, r8=256, d1s=240, r4=448, gg=240, rs=240, ne=240, osn=240, o16=240, ix=16, lk=192, ms=192,
              fh=1024, a1=384, a2=576, zt=896, z32=896, yw=1024, tab=256, sq=512, ab=512, df=32, do=4, t2=2,
-             nw=224, wk=64, nc=224, ncm=16, amb=16, cd=32, pp=128, pq=128, re=128, rx=336, pa=512, pb=512),
+             nw=256, wk=64, nc=256, amb=16, cd=32, pp=128, pq=128, re=128, rx=336, pa=512, pb=512),
     F32: dict(pc=16, iop=16, w1=32, w3=32, w4=80, w5=64, lf=72, tf=67, tt=512, ap=240, rk=16, rv=32, rvt=32,
               tabo=256, dof=2, yo=256),
     I32: dict(trii=256, pi=4, w2=32),
@@ -206,7 +205,7 @@ def rank_program(g, core, T, topo):
             [src], [], "remote")
 
     load("y", V("xin"), T.x[:])
-    load("s", V("uin"), T.u[:])
+    load("y", V("uin"), T.u[:])
     load("y", V("trii"), T.tri[:], None, [C("xin", 0)])
     load("y", V("wq"), T.wc[:], dt.uint8)
     load("y", V("wsc"), T.ws[:])
@@ -235,23 +234,24 @@ def rank_program(g, core, T, topo):
     ts(C("pi", 3), C("pi", 0), 31, A.bitwise_and)
     mset(V("lf"), 0.0)
     mset(V("w1", 15, 32, 16), 0.0)
-    cp(V("pc", 0, 3), V("pi", 1, 4))
     mset(V("d1o"), -1.0)
+    cp(V("pc", 0, 3), V("pi", 1, 4))
     mset(C("lf", 68), 30.0)
+    mset(C("lf", 69), 14.0)
+    mset(V("d1o", 15, 240, 16), 15.0)
     ts(V("w1", 0, 15), V("iop", 0, 15), q_, A.max, 1.0, A.add)
     ts(V("w1", 16, 31), V("iop", 0, 15), q_, A.min, 1.0, A.add)
     ts(c16q, q_, 16.0, A.mult)
-    mset(C("lf", 69), 14.0)
     ts(c16, q_, 16.0, A.add)
+    cp(C("lf", 66), p32)
     ts(V("w2"), V("w1"), h_, A.add)
     ts(V("lf", 1, 16), V("iop", 0, 15), c16q, A.add)
     ts(C("lf", 0), c16q, 15.0, A.add)
     ts(C("pc", 5), c16q, 14.0, A.add, 238.0, A.min)
     ts(V("w2"), V("w2"), 1, A.bitwise_and)
-    cp(C("lf", 66), p32)
-    mset(V("d1o", 15, 240, 16), 15.0)
-    ts(V("w3"), V("w2"), 15.0, A.mult)
+    cp(V("lu", 0, 18), V("lf", 0, 18))
     ts(V("lf", 50, 65), V("iop", 0, 15), 0.0, A.mult, C("pc", 5), A.add)
+    ts(V("w3"), V("w2"), 15.0, A.mult)
     l_pick, l_a, l_b, l_n = V("lu", 0, 17), V("lu", 18, 33), V("lu", 34, 49), V("lu", 50, 65)
     l_32, l_w = V("lu", 66, 67), V("lu", 68, 70)
     act(V("et", 2, 514, 4), V("idn"))
@@ -263,11 +263,11 @@ def rank_program(g, core, T, topo):
 
     tt(V("w3"), V("w3"), V("w1"), A.add)
     unit(0)
-    ts(V("lf", 18, 50), V("w3"), 16.0, A.mult)
     unit(2)
-    cp(V("lu"), V("lf"))
+    ts(V("lf", 18, 50), V("w3"), 16.0, A.mult)
     unit(1)
     unit(3)
+    cp(V("lu", 18, 72), V("lf", 18, 72))
     lin(C("pc", 6), q_, 1.0, 1.0)
     lin(C("pc", 7), q_, 64.0, 0.0)
     lin(C("pc", 8), q_, 4.0, 963.0)
@@ -280,32 +280,26 @@ def rank_program(g, core, T, topo):
     lin(V("tf", 31, 44), V("iop", 0, 13), 0.0, c16)
     lin(V("rv", 15, 32, 16), V("iop", 0, 2), 0.0, C("pc", 9))
     lin(C("tf", 59), q_, 4.0, 3.0)
-    quant(V("qu"), V("su"), V("uin"))
+    act(V("d1s"), V("d1o"), 16.0)
     quant(V("qn"), V("sn"), V("xin"))
+    ts(C("pc", 10), q_, 15.0, A.is_equal)
+    ts(C("pc", 11), q_, 15.0, A.not_equal)
+    cp(C("offo", 16), q_)
     cp(V("qp"), I(V("qn"), l_pick), dt.uint32)
     act(V("sp"), I(V("sn"), l_pick))
-    act(V("pa", 64, 512), V("ones", 0, 448), 0.0)
+    quant(V("qu"), V("su"), V("uin"))
 
     def constants_1():
         ts(V("w4", 8, 15), V("w4", 0, 7), 15.0, A.is_ge, -15.0, A.mult)
         ts(V("w5", 0, 16), V("w4", 16, 32), 0.0, A.is_lt, 960.0, A.mult)
-        ts(C("pc", 10), q_, 15.0, A.is_equal)
-        ts(C("pc", 11), q_, 15.0, A.not_equal)
+        cp(C("offr", 0), C("pc", 9))
+        mset(C("df", 31), 0.0)
         tt(V("tf", 7, 14), V("w4", 0, 7), V("w4", 8, 15), A.add)
         tt(V("w5", 0, 16), V("w5", 0, 16), V("w4", 16, 32), A.add)
         lin(V("w5", 32, 48), V("w4", 32, 48), C("pc", 10), 0.0)
-        lin(V("tf", 24, 31), V("tf", 7, 14), 1.0, 16.0)
         lin(V("w5", 16, 32), V("w5", 0, 16), -1.0, C("pc", 8))
+        lin(V("tf", 24, 31), V("tf", 7, 14), 1.0, 16.0)
         lin(V("tf", 60, 67), V("tf", 7, 14), 1.0, c16q)
-
-    def constants_2():
-        tt(V("w4", 48, 64), V("w5", 0, 16), V("w4", 32, 48), A.add)
-        ts(V("mk"), V("ioc"), q_, A.is_equal)
-        cp(C("offo", 16), q_)
-        tt(V("w4", 48, 64), V("w4", 48, 64), V("w5", 16, 32), A.min)
-        cp(C("offr", 0), C("pc", 9))
-        mset(C("df", 31), 0.0)
-        ts(V("w4", 48, 64), V("w4", 48, 64), 63.0, A.max, C("pc", 11), A.mult)
 
     l_exy = V("tu", 0, 14)
     l_term = [V("tu", 16, 23), V("tu", 24, 31), V("tu", 32, 39)]
@@ -315,17 +309,26 @@ def rank_program(g, core, T, topo):
 
     def walk(s):
         if s == 0:
-            ts(V("nw", 0, 224, 7), V("ioc", 0, 32), C("t2", 0), A.add, o_(2), A.not_equal)
+            ts(V("nw", 0, 256, 8), V("ioc", 0, 32), C("t2", 0), A.add, o_(2), A.not_equal)
         else:
             k = 32 * ((s - 1) % 2)
-            tt(V("nw", s, 224, 7), I(V("wk", k, k + 32), l_w), V("ioc", 0, 32), A.not_equal)
+            tt(V("nw", s, 256, 8), I(V("wk", k, k + 32), l_w), V("ioc", 0, 32), A.not_equal)
 
     def step(s):
         k = 32 * (s % 2)
-        scan(V("wk", k, k + 32), V("nw", s, 224, 7), V("df"), A.mult, A.add)
+        scan(V("wk", k, k + 32), V("nw", s, 256, 8), V("df"), A.mult, A.add)
+
+    def rows():
+        scan(V("ab"), V("sq"), V("ones"), A.min, A.add)
+
+    def diffs():
+        tt(V("df", 0, 31), V("ab", 31, 512, 16), V("ab", 15, 496, 16), A.subtract)
+
+    def met():
+        scan(V("nc"), V("r8"), V("nw"), A.add, A.min)
 
     def cd1():
-        ts(V("cd", 0, 16), V("ncm"), -1.0, A.add)
+        tt(V("cd", 0, 16), V("nc", 7, 128, 8), V("nc", 135, 256, 8), A.min)
 
     def cd2():
         tt(V("cd", 16, 32), V("cd", 0, 16), V("amb"), A.mult)
@@ -362,6 +365,16 @@ def rank_program(g, core, T, topo):
             tt(V("yw", 256 * b + 96, 256 * b + 192), (ybank[b][0], ybank[b][1] + 32, ybank[b][1] + 128, 1),
                V("z32", 512 + b, 896, 4), A.add)
 
+        def came(b):
+            tt(V("yw", 256 * b, 256 * b + 96), V("psF", 512 * b, 512 * b + 96), V("z32", b, 384, 4), A.add)
+
+        def place(b):
+            src = I(V("yw", 256 * b, 256 * b + 256), V("offr"))
+            if b in (0, 2):
+                act(V("xt", b, 1024, 4), src, 0.03125)
+            else:
+                ts(V("xt", b, 1024, 4), src, 0.03125, A.mult)
+
         mm(V("psS", 0, ns), V("qu"), V("su"), V(qx, 0, ns), V(sx, 0, ns))
         for b in range(4):
             mm(V("psF", 512 * b, 512 * b + 256), V("qe", 128 * b, 128 * b + 128), V("se", 128 * b, 128 * b + 128),
@@ -369,37 +382,50 @@ def rank_program(g, core, T, topo):
         if r == 0:
             constants_1()
         else:
+            met()
             cd1()
-            cd2()
         tr(V("tt", 0, 256), V("psS", 0, 256))
+        if r > 0:
+            cd2()
+        else:
+            tt(V("w4", 48, 64), V("w5", 0, 16), V("w4", 32, 48), A.add)
         tr(V("tt", 256, 512), V("psS", 16, 272))
         if r > 0:
             evac(0)
-        act(V("ap"), I(V("tt"), l_a))
+        act(V("ap", 0, 128), I(V("tt"), V("lu", 18, 26)))
         if r == 0:
-            constants_2()
+            tt(V("w4", 48, 64), V("w4", 48, 64), V("w5", 16, 32), A.min)
+            ts(V("mk"), V("ioc"), q_, A.is_equal)
+        else:
+            term(r - 1, 0)
+        cp(V("ap", 128, 240), I(V("tt"), V("lu", 26, 33)))
+        if r == 0:
+            ts(V("w4", 48, 64), V("w4", 48, 64), 63.0, A.max, C("pc", 11), A.mult)
+            act(V("pa", 64, 512), V("ones", 0, 448), 0.0)
             evac(0)
         else:
-            for t in range(3):
-                term(r - 1, t)
+            term(r - 1, 1)
         evac(1)
         evac(2)
         tt(V("gg"), I(V("tt"), l_b), V("ap"), A.is_lt)
         if r == 0:
             tt(V("tf", 44, 59), V("w4", 48, 63), V("w5", 32, 47), A.add)
         else:
-            table_sum(r - 1)
-            act(V("tab"), I(V(cur), V("tu", 44, 60)))
+            term(r - 1, 2)
         evac(3)
         scan(V("rs"), V("d0r"), V("gg"), A.mult, A.add)
         if r == 0:
             cp(V("tu"), V("tf"))
+        else:
+            table_sum(r - 1)
+            act(V("tab"), I(V(cur), V("tu", 44, 60)))
         tt(V("ne"), I(V("rs"), l_n), V("kjp"), A.not_equal)
         if r == 0:
             cp(V("pa", 67, 512, 4), I(V("trii"), V("tu", 60, 67)))
             act(V("tab"), I(V(cur), V("tu", 44, 60)))
         else:
             tt(V("rk", 0, 15), V("rs", 14, 240, 16), V("iop", 0, 15), A.add)
+        scan(V("o16"), V("ne"), V("d1s"), A.mult, A.add)
         scan(V("osn"), V("ne"), V("d1o"), A.mult, A.add)
         if r == 0:
             tt(V("rk", 0, 15), V("rs", 14, 240, 16), V("iop", 0, 15), A.add)
@@ -408,110 +434,141 @@ def rank_program(g, core, T, topo):
             ts(V("rv", 16, 31), V("rk", 0, 15), 16.0, A.mult, q_, A.add)
         else:
             ts(V("offr", 1, 16), V("rk", 0, 15), 16.0, A.mult, q_, A.add)
-        ts(V("o16", 0, 15), V("osn", 15, 240, 16), 16.0, A.mult)
+        tt(V("ix", 0, 12), V("o16", 15, 192, 16), V("osn", 31, 208, 16), A.add)
         ts(V("offo", 1, 16), V("osn", 15, 240, 16), 16.0, A.mult, c16, A.add)
-        tt(V("do", 0, 3), V("osn", 15, 48, 16), V("osn", 31, 64, 16), A.subtract)
-        tt(V("ix", 0, 12), V("o16", 0, 12), V("osn", 31, 208, 16), A.add)
         is_point("pp", 0)
         is_point("pq", 1)
         cp(V("ixu", 0, 12), V("ix", 0, 12))
+        tt(V("do", 0, 3), V("osn", 15, 48, 16), V("osn", 31, 64, 16), A.subtract)
         if last:
             tr(V("rvt"), V("rv"))
         if r == 0:
             ts(V("offr", 1, 16), V("rk", 0, 15), 16.0, A.mult, q_, A.add)
-        act(V("sq", 0, 240), V("tab", 0, 240), -16.0, F.Square, C("o16", 0))
-        act(V("sq", 256, 496), V("tab", 0, 240), -16.0, F.Square, C("o16", 1))
+        act(V("sq", 0, 240), V("tab", 0, 240), -16.0, F.Square, C("o16", 15))
+        act(V("sq", 256, 496), V("tab", 0, 240), -16.0, F.Square, C("o16", 31))
         tt(V("lk"), I(table, V("ixu", 0, 12)), V("mk"), A.mult)
         tt(V("re"), V("pp"), V("pq"), A.subtract)
         scan(V("ms"), V("nm"), V("lk"), A.mult, A.add)
-        if last:
-            cp(V("offr"), I(V("rvt"), l_32))
+        if r > 0:
+            rows()
+        else:
+            quant(V("qv"), V("sv"), V("vin"))
         ts(V("offm"), V("ms", 15, 192, 16), 16.0, A.mult, c16, A.add)
         ts(C("t2", 0), C("ms", 15), o_(2), A.is_equal, C("do", 2), A.mult)
-        scan(V("ab"), V("sq"), V("ones"), A.min, A.add)
+        if r == 0:
+            rows()
+        if last:
+            cp(V("offr"), I(V("rvt"), l_32))
+        if r > 0:
+            diffs()
         for b in range(4):
             act(V("a1", 96 * b, 96 * b + 96), I(plane(b), V("offo", 2, 8)))
         for b in range(4):
             tt(V("zt", b, 384, 4), I(plane(b), V("offm", 0, 6)), V("a1", 96 * b, 96 * b + 96), A.add)
             if b == 0:
                 walk(0)
-            if b == 1:
-                tt(V("df", 0, 31), V("ab", 31, 512, 16), V("ab", 15, 496, 16), A.subtract)
-        step(0)
+                if r == 0:
+                    diffs()
+            if b == 2:
+                step(0)
         tt(V("amb"), V("ab", 271, 512, 16), V("ab", 15, 256, 16), A.subtract)
+        walk(1)
         quant(V(qs), V(ss), V("zt", 0, 512))
         send(V(qa, 0, 96), V(qs, 0, 96), "arr%d" % r, dt.uint8)
         send(V(sa, 0, 96), V(ss, 0, 96), "arr%d" % r)
         ops.append({"kind": "arrive", "q": None, "r": [], "w": [V(qa, 0, 96), V(sa, 0, 96)], "sem": "arr%d" % r, "n": 2 * n_in})
         if r == 0:
-            select(V("r7"), V("ones", 0, 224), [[0, 32], [1, 7]], A.is_equal, 0.0)
+            iota(V("r8"), [[0, 256]], 0, 0)
+            iota(V("nw", 7, 256, 8), [[0, 32]], 2, 0)
             iota(V("pb", 0, 64), [[1, 16], [0, 4]], 0, 0)
+            iota(V("r8", 7, 256, 8), [[0, 32]], -1, 0)
+            iota(V("r8", 0, 256, 8), [[0, 32]], 2, 0)
             select(V("r4"), V("ones", 0, 448), [[0, 112], [1, 4]], A.is_gt, 0.0)
         for b in range(4):
             act(V("a2", 144 * b, 144 * b + 144), I(plane(b), V("offo", 8, 17)))
         act(V("z32", 0, 384), V("zt", 0, 384), 32.0)
         for b in range(4):
             act(V("yw", 256 * b + 192, 256 * b + 256), V("a2", 144 * b + 80, 144 * b + 144), 64.0)
-        walk(1)
-        blend2(0)
-        step(1)
-        blend2(1)
-        walk(2)
-        blend2(2)
-        step(2)
-        blend2(3)
-        walk(3)
-        quant(V(qa, 96, 224), V(sa, 96, 224), V("zt", 384, 896))
-        act(V("z32", 512, 896), V("zt", 512, 896), 32.0)
-        for b in range(4):
-            mm((ybank[b][0], ybank[b][1], ybank[b][1] + 128, 1), V("wq", 128 * b, 128 * b + 128),
-               V("wsc", 128 * b, 128 * b + 128), V(qa, 96, 224), V(sa, 96, 224))
         act(C("dof", 0), C("do", 0))
         act(V("rx", 112, 336), I(V("re", 0, 16), l_exy))
         act(V("rx", 0, 112), V("re", 16, 128), C("dof", 0), F.Identity)
-        step(3)
-        if r == 0:
-            quant(V("qv"), V("sv"), V("vin"))
-        walk(4)
-        step(4)
-        own(0)
-        own(1)
-        walk(5)
-        own(2)
-        own(3)
-        step(5)
-        if r == 0:
-            walk(6)
+        blend2(0)
+        step(1)
+        blend2(1)
+        if last:
+            walk(2)
+            blend2(2)
+            step(2)
+            blend2(3)
+            walk(3)
+        else:
+            blend2(2)
+            walk(2)
+            blend2(3)
+            step(2)
+        quant(V(qa, 96, 224), V(sa, 96, 224), V("zt", 384, 896))
+        for b in range(4):
+            mm((ybank[b][0], ybank[b][1], ybank[b][1] + 128, 1), V("wq", 128 * b, 128 * b + 128),
+               V("wsc", 128 * b, 128 * b + 128), V(qa, 96, 224), V(sa, 96, 224))
         for b in range(4):
             mm(V("psF", 512 * b, 512 * b + 128), V("wq", 128 * b, 128 * b + 128), V("wsc", 128 * b, 128 * b + 128),
                V(qa, 0, 128), V(sa, 0, 128))
-        for b in range(4):
-            tt(V("yw", 256 * b, 256 * b + 96), V("psF", 512 * b, 512 * b + 96), V("z32", b, 384, 4), A.add)
-            if b == 1 and r > 0:
-                walk(6)
-        scan(V("nc"), V("r7"), V("nw"), A.max, A.min)
-        for b in range(4):
-            src = I(V("yw", 256 * b, 256 * b + 256), V("offr"))
-            if b < X_ON_ACT[r]:
-                act(V("xt", b, 1024, 4), src, 0.03125)
-            else:
-                ts(V("xt", b, 1024, 4), src, 0.03125, A.mult)
-        tt(V("ncm"), V("nc", 6, 112, 7), V("nc", 118, 224, 7), A.min)
         if last:
+            step(3)
+            ts(V("z32", 512, 896), V("zt", 512, 896), 32.0, A.mult)
+            walk(4)
+            step(4)
+            own(0)
+            own(1)
+            walk(5)
+            own(2)
+            own(3)
+            step(5)
+            walk(6)
+            came(0)
+            came(1)
+            met()
+            came(2)
+            came(3)
             cd1()
+            place(0)
+            place(1)
             cd2()
+            place(2)
+            place(3)
+            term(r, 0)
+        else:
+            walk(3)
+            ts(V("z32", 512, 896), V("zt", 512, 896), 32.0, A.mult)
+            step(3)
+            own(0)
+            own(1)
+            walk(4)
+            own(2)
+            own(3)
+            step(4)
+            came(0)
+            came(1)
+            came(2)
+            came(3)
+            place(0)
+            place(2)
+            walk(5)
+            place(1)
+            step(5)
+            place(3)
+            walk(6)
         quant(V("qx"), V("sx"), V("xt"))
 
     mm(V("psS", 0, 256), V("qv"), V("sv"), V("qx"), V("sx"))
     store("y", T.oc[:], T.qx[:].bitcast(dt.uint8), [V("qx")])
-    for t in range(3):
+    for t in (1, 2):
         term(ROUNDS - 1, t)
     act(V("yo"), V("psS", 0, 256))
     store("s", T.y[:], T.yo[:], [V("yo")])
     table_sum(ROUNDS - 1)
     new = V("pa" if (ROUNDS - 1) % 2 else "pb")
-    cp(V("tabo", 0, 128), I(new, V("tu", 44, 52)))
-    act(V("tabo", 128, 256), I(new, V("tu", 52, 60)))
+    cp(V("tabo"), I(new, V("tu", 44, 60)))
     for k in range(4):
         store("y", T.osc[4 * k:4 * k + 4, :], T.sx[32 * k:32 * k + 4, :], [V("sx")])
     store("y", T.ot[:], T.tabo[:], [V("tabo")])

@@ -5,14 +5,14 @@ F = ActivationFunctionType
 ROUNDS = 3
 C4, U8, BF, F32, I32, U16 = "float8_e4m3fn_x4", "uint8", "bfloat16", "float32", "int32", "uint16"
 SB = {
-    BF: dict(xin=1024, uin=512, vin=512, et=1032, idn=128, ones=512, xt=1024, ioc=192, d0r=240, kjp=240, d1o=240,
-             mk=192, nm=192, r8=256, d1s=240, r4=448, gg=240, rs=240, ne=240, osn=240, o16=240, ix=16, lk=192, ms=192,
-             fh=1024, a1=384, a2=576, zt=896, z32=896, yw=1024, tab=256, sq=512, ab=512, df=32, do=4, t2=2,
-             nw=256, wk=64, nc=256, amb=16, cd=32, pp=128, pq=128, re=128, rx=336, pa=512, pb=512),
-    F32: dict(pc=16, iop=16, w1=32, w3=32, w4=80, w5=64, lf=72, tf=67, tt=512, ap=240, rk=16, rv=32, rvt=32,
+    BF: dict(xin=1024, uin=512, vin=512, et=1032, idn=128, ones=560, xt=1024, ioc=96, d0r=240, kjp=240, d1o=128,
+             mk=96, nm=96, d1s=128, gg=240, rs=240, ne=240, osn=240, o16=240, ix=12, lk=192, ms=192,
+             fh=1024, a1=384, a2=576, zt=896, z32=896, yw=1024, tab=256, sq=512, ab=512, df=16, t2=2, rk=16,
+             nw=288, md=288, nc=288, do=4, wk=80, r2=32, ev=16, hm=560, pa=640, pb=640),
+    F32: dict(pc=16, iop=16, w1=32, w3=32, w4=64, w5=48, lf=60, tf=64, tt=512, ap=240, rv=32, rvt=32,
               tabo=256, dof=2, yo=256),
     I32: dict(trii=256, pi=4, w2=32),
-    U16: dict(lu=72, tu=67, ixu=16, offo=18, offm=12, offr=16),
+    U16: dict(lu=60, tu=64, ixu=12, offo=16, offm=12, offr=16),
     C4: dict(wq=512, qu=128, qv=128, qe=512, qn=256, qp=272, qx=256, qs0=128, qs1=128, qs2=128, qa0=224, qa1=224, qa2=224),
     U8: dict(wsc=512, su=128, sv=128, se=512, sn=256, sp=272, sx=256, ss0=128, ss1=128, ss2=128, sa0=224, sa1=224, sa2=224),
 }
@@ -20,6 +20,10 @@ SCRATCH = {name: ("sbuf", [128, n], t) for t, d in SB.items() for name, n in d.i
 SCRATCH.update({"psS": ("psum", [128, 512], F32), "psF": ("psum", [128, 2048], F32), "psY": ("psum", [128, 1536], F32)})
 SEMAPHORES = ["cv", "cs", "ct", "cg", "sent"] + ["arr%d" % r for r in range(ROUNDS)] + ["dm%d" % k for k in range(16)]
 COUNTER = {"v": "cv", "s": "cs", "t": "ct", "g": "cg"}
+BIG = 1024.0
+LIFT = 128.0
+CFG = dict(WAIT=180, FLIGHT=1500, LOCAL=1300, ISSUE=350, FIRST=1500, SLACK=100, GUARD=300, ACT=180)
+ORDER = []
 
 
 def V(name, a=0, b=None, s=1):
@@ -38,9 +42,12 @@ def is_view(x):
     return isinstance(x, tuple)
 
 
-def schedule(ops, g, T):
-    queue = {"v": g.vector, "s": g.scalar, "t": g.tensor, "g": g, "y": g.sync}
-    writer, readers = {}, {}
+def size(v):
+    return 16 * size(v[2]) if v[0] == "@" else len(range(v[1], v[2], v[3]))
+
+
+def depends(ops):
+    writer, readers, deps = {}, {}, []
 
     def cells(v):
         name, a, b, s = v
@@ -48,7 +55,6 @@ def schedule(ops, g, T):
             return [(name, k) for k in range(a // 512, (b - 1) // 512 + 1)]
         return [(name, k) for k in range(a, b, s)]
 
-    deps = []
     for i, op in enumerate(ops):
         d = set()
         rd = [c for v in op["r"] for c in cells(v)]
@@ -69,6 +75,47 @@ def schedule(ops, g, T):
             readers[c] = set()
         d.discard(i)
         deps.append(d)
+    return deps
+
+
+def arrange(ops):
+    deps = depends(ops)
+    for i, op in enumerate(ops):
+        deps[i].update(op.get("after", ()))
+    n = len(ops)
+    succ = [[] for _ in ops]
+    for i in range(n):
+        for j in deps[i]:
+            succ[j].append(i)
+    behind = [0.0] * n
+    for i in reversed(range(n)):
+        behind[i] = ops[i]["len"] + max([CFG["WAIT"] + behind[k] for k in succ[i]] + [0])
+    done, free, order = {}, {op["q"]: 0.0 for op in ops}, []
+    todo = list(range(n))
+    while todo:
+        start = {}
+        for i in todo:
+            start[i] = max([free[ops[i]["q"]]] + [(done[j] if j in done else start[j] + ops[j]["len"]) + CFG["WAIT"]
+                                                  for j in deps[i]])
+        end = max(start[i] + behind[i] for i in todo)
+
+        def fits(i):
+            stop = start[i] + ops[i]["hold"]
+            return all(stop <= max(start[j], end - behind[j] - CFG["GUARD"]) + CFG["SLACK"] for j in todo
+                       if behind[j] > behind[i] and ops[j]["q"] == ops[i]["q"] and start[j] < stop)
+
+        ready = sorted((i for i in todo if all(j in done for j in deps[i])), key=lambda i: (start[i], -behind[i]))
+        i = next((i for i in ready if fits(i)), ready[0])
+        todo.remove(i)
+        order.append(i)
+        free[ops[i]["q"]] = start[i] + ops[i]["hold"]
+        done[i] = start[i] + ops[i]["len"]
+    return order
+
+
+def issue(ops, g, T):
+    queue = {"v": g.vector, "s": g.scalar, "t": g.tensor, "g": g, "y": g.sync}
+    deps = depends(ops)
     known = {q: set() for q in queue}
     clock, waits = [], []
     for i, op in enumerate(ops):
@@ -144,8 +191,14 @@ def rank_program(g, core, T, topo):
                 out += [x[1], x[2]] if x[0] == "@" else [x]
         return out
 
-    def rec(q, f, r, w, kind="compute"):
-        ops.append({"q": q, "f": f, "r": flat(r), "w": flat(w), "kind": kind})
+    def rec(q, f, r, w, kind="compute", hold=None, more=0):
+        if hold is None:
+            narrow = q == "v" and all(SCRATCH[x[0]][2] in (BF, U16) for x in flat([r[0], w[0]] if r else w))
+            if r and is_view(r[0]) and r[0][0] == "@":
+                hold = 70 + 1.56 * size(r[0])
+            else:
+                hold = max(64, size(w[0]) * (0.5 if narrow else 1)) if q == "v" else CFG["ACT"] + size(w[0])
+        ops.append({"q": q, "f": f, "r": flat(r), "w": flat(w), "kind": kind, "hold": hold, "len": hold + more})
 
     def cp(o, i, word=None):
         rec("v", lambda q: q.tensor_copy(ap(o, word), ap(i, word)), [i], [o])
@@ -169,7 +222,7 @@ def rank_program(g, core, T, topo):
         rec("v", lambda q: q.transpose(ap(o), ap(i)), [i], [o])
 
     def quant(qc, sc, i):
-        rec("v", lambda q: q.quantize_mx(ap(qc), ap(sc), ap(i)), [i], [qc, sc])
+        rec("v", lambda q: q.quantize_mx(ap(qc), ap(sc), ap(i)), [i], [qc, sc], hold=15 + 0.27 * size(i))
 
     def act(o, i, scale=None, func=F.Copy, bias=None):
         kw = {}
@@ -180,398 +233,267 @@ def rank_program(g, core, T, topo):
         rec("s", lambda q: q.activation(ap(o), ap(i), func, **kw), [i, bias, scale], [o])
 
     def lin(o, i, scale, bias):
-        act(o, i, scale, F.Identity, bias)
+        if i[0] == "@":
+            act(o, i, scale, F.Identity, bias)
+        else:
+            ts(o, i, scale, A.mult, bias, A.add)
 
     def mm(o, lq, ls, rq, rsc):
-        rec("t", lambda q: q.matmul_mx(ap(o), ap(lq), ap(ls), ap(rq), ap(rsc), True, True), [lq, ls, rq, rsc], [o])
+        rec("t", lambda q: q.matmul_mx(ap(o), ap(lq), ap(ls), ap(rq), ap(rsc), True, True), [lq, ls, rq, rsc], [o],
+            hold=0.7 * (size(o) + 16))
 
     def iota(o, pattern, base, cm, small=True):
-        if small:
-            rec("g", lambda q: q.iota(ap(o), pattern, base, cm, allow_small_or_imprecise_dtypes=True), [], [o])
-        else:
-            rec("g", lambda q: q.iota(ap(o), pattern, base, cm), [], [o])
+        kw = {"allow_small_or_imprecise_dtypes": True} if small else {}
+        rec("g", lambda q: q.iota(ap(o), pattern, base, cm, **kw), [], [o], hold=160 + 2 * size(o))
 
     def select(o, i, pattern, op, fill, base=0, cm=0):
-        rec("g", lambda q: q.affine_select(ap(o), ap(i), pattern, op, fill, base, cm), [i], [o])
+        rec("g", lambda q: q.affine_select(ap(o), ap(i), pattern, op, fill, base, cm), [i], [o], hold=200 + 2 * size(o))
 
     def load(q, o, src, word=None, after=()):
-        rec(q, lambda e: e.dma_start(ap(o, word), src), list(after), [o], "dma")
+        rec(q, lambda e: e.dma_start(ap(o, word), src), list(after), [o], "dma", 60, CFG["LOCAL"])
 
     def store(q, dst, src, reads):
-        rec(q, lambda e: e.dma_start(dst, src), reads, [], "dma")
+        rec(q, lambda e: e.dma_start(dst, src), reads, [], "dma", 60, CFG["LOCAL"])
 
-    def send(dst, src, sem, word=None):
+    def send(dst, src, sem, word=None, first=0):
         rec("g", lambda q: q.remote_dma(ap(dst, word), ap(src, word), T.sem[sem], T.sem.sent, pid, rid, mask),
-            [src], [], "remote")
+            [src], [], "remote", CFG["ISSUE"] + first)
 
     load("y", V("xin"), T.x[:])
     load("y", V("uin"), T.u[:])
     load("y", V("trii"), T.tri[:], None, [C("xin", 0)])
-    load("y", V("wq"), T.wc[:], dt.uint8)
-    load("y", V("wsc"), T.ws[:])
-    load("y", V("vin"), T.v[:])
+    load("y", V("wq"), T.wc[:], dt.uint8, [C("xin", 0)])
+    load("y", V("wsc"), T.ws[:], None, [C("xin", 0)])
+    load("y", V("vin"), T.v[:], None, [C("xin", 0)])
 
     q_, h_, p32, c16, c16q = C("pc", 0), C("pc", 1), C("pc", 2), C("pc", 3), C("pc", 4)
     iota(C("pi", 0), [[0, 1]], 0, 1, False)
     iota(V("iop"), [[1, 16]], 0, 0)
     mset(V("ones"), 1.0)
     select(V("idn"), V("ones", 0, 128), [[-1, 128]], A.is_equal, 0.0, 0, 1)
-    iota(V("ioc"), [[0, 12], [1, 16]], 0, 0)
+    iota(V("ioc"), [[0, 6], [1, 16]], 0, 0)
     select(V("d0r"), V("ones", 0, 240), [[1, 15], [-1, 16]], A.not_equal, -1.0)
     iota(V("kjp"), [[1, 15], [-1, 16]], 0, 0)
-    select(V("d0r"), V("d0r"), [[0, 15], [1, 16]], A.is_gt, 0.0)
-    select(V("kjp"), V("kjp"), [[0, 15], [-1, 16]], A.is_gt, 99.0, 15)
-    iota(V("pa", 0, 64), [[1, 16], [0, 4]], 0, 0)
-    select(V("nm"), V("ones", 0, 192), [[0, 12], [1, 16]], A.is_gt, 0.0)
+    select(V("d0r", 0, 240, 16), V("d0r", 0, 240, 16), [[0, 15]], A.is_gt, 0.0)
+    select(V("kjp", 15, 240, 16), V("kjp", 15, 240, 16), [[0, 15]], A.is_gt, 99.0)
+    select(V("nm"), V("ones", 0, 96), [[0, 6], [1, 16]], A.is_gt, 0.0)
     iota(V("sq", 240, 256), [[256, 16]], 0, 0)
     iota(V("sq", 496, 512), [[256, 16]], 0, 0)
     iota(V("zt", 384, 512), [[0, 128]], 0, 0)
-    act(V("et", 0, 512), V("ones"), 0.0)
-    act(V("et", 512, 1024), V("ones"), 0.0)
-    mset(V("et", 1024, 1032), 0.0)
+    iota(V("r2", 1, 32, 2), [[1, 16]], 0, 0)
+    for p in ("pa", "pb"):
+        iota(V(p, 0, 80), [[1, 16], [0, 5]], int(LIFT), 0)
+    select(V("md"), V("ones", 0, 288), [[0, 16], [1, 18]], A.is_equal, 0.0)
+    iota(V("md", 16, 288, 18), [[0, 16]], -1, 0)
+    select(V("nw"), V("ones", 0, 288), [[0, 16], [1, 18]], A.not_equal, 0.0)
     ts(C("pi", 1), C("pi", 0), 15, A.bitwise_and)
     ts(C("pi", 2), C("pi", 0), 4, A.arith_shift_right, 1, A.bitwise_and)
     ts(C("pi", 3), C("pi", 0), 31, A.bitwise_and)
-    mset(V("lf"), 0.0)
-    mset(V("w1", 15, 32, 16), 0.0)
-    mset(V("d1o"), -1.0)
     cp(V("pc", 0, 3), V("pi", 1, 4))
-    mset(C("lf", 68), 30.0)
-    mset(C("lf", 69), 14.0)
-    mset(V("d1o", 15, 240, 16), 15.0)
-    ts(V("w1", 0, 15), V("iop", 0, 15), q_, A.max, 1.0, A.add)
-    ts(V("w1", 16, 31), V("iop", 0, 15), q_, A.min, 1.0, A.add)
     ts(c16q, q_, 16.0, A.mult)
-    ts(c16, q_, 16.0, A.add)
-    cp(C("lf", 66), p32)
-    ts(V("w2"), V("w1"), h_, A.add)
+    lin(c16, q_, 1.0, 16.0)
+    mset(V("lf", 16, 18), 0.0)
     ts(V("lf", 1, 16), V("iop", 0, 15), c16q, A.add)
     ts(C("lf", 0), c16q, 15.0, A.add)
-    ts(C("pc", 5), c16q, 14.0, A.add, 238.0, A.min)
-    ts(V("w2"), V("w2"), 1, A.bitwise_and)
     cp(V("lu", 0, 18), V("lf", 0, 18))
-    ts(V("lf", 50, 65), V("iop", 0, 15), 0.0, A.mult, C("pc", 5), A.add)
+    ts(V("w1", 0, 16), V("iop"), q_, A.max, 1.0, A.add)
+    ts(V("w1", 16, 32), V("iop"), q_, A.min, 1.0, A.add)
+    ts(V("w2"), V("w1"), h_, A.add)
+    ts(V("w2"), V("w2"), 1, A.bitwise_and)
     ts(V("w3"), V("w2"), 15.0, A.mult)
-    l_pick, l_a, l_b, l_n = V("lu", 0, 17), V("lu", 18, 33), V("lu", 34, 49), V("lu", 50, 65)
-    l_32, l_w = V("lu", 66, 67), V("lu", 68, 70)
+    tt(V("w3"), V("w3"), V("w1"), A.add)
+    ts(V("lu", 18, 50), V("w3"), 16.0, A.mult)
+    ts(C("pc", 5), c16q, 14.0, A.add, 238.0, A.min)
+    ts(V("lu", 50, 58), V("iop", 0, 8), 0.0, A.mult, C("pc", 5), A.add)
+    cp(C("lu", 58), p32)
+    l_pick, l_b, l_32 = V("lu", 0, 17), V("lu", 34, 49), V("lu", 58, 59)
+    mset(V("d1o"), -1.0)
+    mset(V("d1o", 15, 128, 16), 15.0)
+    lin(V("d1s"), V("d1o"), 16.0, 0.0)
+    ts(V("mk"), V("ioc"), q_, A.is_equal)
+    act(V("et", 0, 516), V("ones", 0, 516), 0.0)
+    act(V("et", 516, 1032), V("ones", 0, 516), 0.0)
     act(V("et", 2, 514, 4), V("idn"))
     act(V("et", 519, 1031, 4), V("idn"))
-
-    def unit(b):
+    for b in range(4):
         o = 516 * (b % 2) + (2 if b < 2 else 0)
         quant(V("qe", 128 * b, 128 * b + 128), V("se", 128 * b, 128 * b + 128), V("et", o, o + 512))
-
-    tt(V("w3"), V("w3"), V("w1"), A.add)
-    unit(0)
-    unit(2)
-    ts(V("lf", 18, 50), V("w3"), 16.0, A.mult)
-    unit(1)
-    unit(3)
-    cp(V("lu", 18, 72), V("lf", 18, 72))
     lin(C("pc", 6), q_, 1.0, 1.0)
-    lin(C("pc", 7), q_, 64.0, 0.0)
-    lin(C("pc", 8), q_, 4.0, 963.0)
+    lin(C("pc", 7), q_, 80.0, 0.0)
+    lin(C("pc", 8), q_, 5.0, 1204.0)
     lin(C("pc", 9), q_, 1.0, 240.0)
-    lin(V("w4", 32, 48), V("iop"), 4.0, 3.0)
-    lin(V("w4", 0, 7), V("iop", 0, 7), 1.0, C("pc", 6))
-    lin(V("w4", 16, 32), V("iop"), -64.0, C("pc", 7))
-    lin(V("tf", 0, 8), V("iop", 0, 8), 0.0, q_)
-    lin(V("tf", 14, 24), V("iop", 0, 10), 0.0, q_)
-    lin(V("tf", 31, 44), V("iop", 0, 13), 0.0, c16)
-    lin(V("rv", 15, 32, 16), V("iop", 0, 2), 0.0, C("pc", 9))
-    lin(C("tf", 59), q_, 4.0, 3.0)
-    act(V("d1s"), V("d1o"), 16.0)
-    quant(V("qn"), V("sn"), V("xin"))
+    lin(C("pc", 12), q_, 18.0, 16.0)
+    lin(C("pc", 13), q_, 18.0, 17.0)
     ts(C("pc", 10), q_, 15.0, A.is_equal)
     ts(C("pc", 11), q_, 15.0, A.not_equal)
-    cp(C("offo", 16), q_)
+    lin(V("w4", 0, 8), V("iop", 0, 8), 1.0, C("pc", 6))
+    ts(V("w4", 8, 16), V("w4", 0, 8), 15.0, A.is_ge, -15.0, A.mult)
+    tt(V("tf", 8, 16), V("w4", 0, 8), V("w4", 8, 16), A.add)
+    lin(V("tf", 0, 8), V("iop", 0, 8), 0.0, q_)
+    lin(V("tf", 16, 24), V("iop", 0, 8), 0.0, C("pc", 12))
+    lin(V("tf", 24, 32), V("iop", 0, 8), 0.0, C("pc", 13))
+    lin(V("tf", 32, 40), V("tf", 8, 16), 18.0, 17.0)
+    lin(V("tf", 40, 48), V("tf", 8, 16), 1.0, c16q)
+    lin(V("w4", 32, 48), V("iop"), 5.0, 4.0)
+    lin(V("w4", 16, 32), V("iop"), -80.0, C("pc", 7))
+    ts(V("w5", 0, 16), V("w4", 16, 32), 0.0, A.is_lt, 1200.0, A.mult)
+    tt(V("w5", 0, 16), V("w5", 0, 16), V("w4", 16, 32), A.add)
+    lin(V("w5", 32, 48), V("w4", 32, 48), C("pc", 10), 0.0)
+    lin(V("w5", 16, 32), V("w5", 0, 16), -1.0, C("pc", 8))
+    tt(V("w4", 48, 64), V("w5", 0, 16), V("w4", 32, 48), A.add)
+    tt(V("w4", 48, 64), V("w4", 48, 64), V("w5", 16, 32), A.min)
+    ts(V("w4", 48, 64), V("w4", 48, 64), 79.0, A.max, C("pc", 11), A.mult)
+    tt(V("tf", 48, 63), V("w4", 48, 63), V("w5", 32, 47), A.add)
+    lin(C("tf", 63), q_, 5.0, 4.0)
+    cp(V("tu", 0, 48), V("tf", 0, 48))
+    cp(V("tu", 48, 64), V("tf", 48, 64))
+    l_x, l_y, l_cx, l_wx, l_wy, l_xy, l_tab = [V("tu", 8 * k, 8 * k + 7) for k in range(6)] + [V("tu", 48, 64)]
+    act(V("hm", 0, 560, 5), V("ones", 0, 112), 0.0)
+    act(V("hm", 1, 560, 5), V("ones", 0, 112), -1.0)
+    act(V("pa", 80, 640), V("ones"), 0.0)
+    lin(V("rv", 15, 32, 16), V("iop", 0, 2), 0.0, C("pc", 9))
+    cp(C("offo", 14), q_)
+    cp(C("offr", 0), C("pc", 9))
+
+    quant(V("qn"), V("sn"), V("xin"))
     cp(V("qp"), I(V("qn"), l_pick), dt.uint32)
     act(V("sp"), I(V("sn"), l_pick))
     quant(V("qu"), V("su"), V("uin"))
-
-    def constants_1():
-        ts(V("w4", 8, 15), V("w4", 0, 7), 15.0, A.is_ge, -15.0, A.mult)
-        ts(V("w5", 0, 16), V("w4", 16, 32), 0.0, A.is_lt, 960.0, A.mult)
-        cp(C("offr", 0), C("pc", 9))
-        mset(C("df", 31), 0.0)
-        tt(V("tf", 7, 14), V("w4", 0, 7), V("w4", 8, 15), A.add)
-        tt(V("w5", 0, 16), V("w5", 0, 16), V("w4", 16, 32), A.add)
-        lin(V("w5", 32, 48), V("w4", 32, 48), C("pc", 10), 0.0)
-        lin(V("w5", 16, 32), V("w5", 0, 16), -1.0, C("pc", 8))
-        lin(V("tf", 24, 31), V("tf", 7, 14), 1.0, 16.0)
-        lin(V("tf", 60, 67), V("tf", 7, 14), 1.0, c16q)
-
-    l_exy = V("tu", 0, 14)
-    l_term = [V("tu", 16, 23), V("tu", 24, 31), V("tu", 32, 39)]
+    quant(V("qv"), V("sv"), V("vin"))
+    ts(V("pa", 84, 640, 5), I(V("trii"), l_xy), LIFT, A.add)
+    lin(V("tab"), I(V("pa"), l_tab), 1.0, -LIFT)
 
     def o_(j):
         return C("osn", 16 * j + 15)
 
-    def walk(s):
-        if s == 0:
-            ts(V("nw", 0, 256, 8), V("ioc", 0, 32), C("t2", 0), A.add, o_(2), A.not_equal)
-        else:
-            k = 32 * ((s - 1) % 2)
-            tt(V("nw", s, 256, 8), I(V("wk", k, k + 32), l_w), V("ioc", 0, 32), A.not_equal)
-
-    def step(s):
-        k = 32 * (s % 2)
-        scan(V("wk", k, k + 32), V("nw", s, 256, 8), V("df"), A.mult, A.add)
-
-    def rows():
-        scan(V("ab"), V("sq"), V("ones"), A.min, A.add)
-
-    def diffs():
-        tt(V("df", 0, 31), V("ab", 31, 512, 16), V("ab", 15, 496, 16), A.subtract)
-
-    def met():
-        scan(V("nc"), V("r8"), V("nw"), A.add, A.min)
-
-    def cd1():
-        tt(V("cd", 0, 16), V("nc", 7, 128, 8), V("nc", 135, 256, 8), A.min)
-
-    def cd2():
-        tt(V("cd", 16, 32), V("cd", 0, 16), V("amb"), A.mult)
-
-    def term(r, t):
-        tt(V("pb" if r % 2 else "pa", 64 + t, 512, 4), I(V("cd"), l_term[t]), V("rx", 112 * t, 112 * t + 112), A.mult)
-
-    def table_sum(r):
-        old, new = ("pb", "pa") if r % 2 else ("pa", "pb")
-        scan(V(new, 64, 512), V("r4"), V(old, 64, 512), A.mult, A.add)
-
-    ybank = [V("psS"), V("psY", 0, 512), V("psY", 512, 1024), V("psY", 1024, 1536)]
+    ybank = [("psS", 0), ("psY", 0), ("psY", 512), ("psY", 1024)]
 
     for r in range(ROUNDS):
         last = r == ROUNDS - 1
         qs, ss, qa, sa = "qs%d" % r, "ss%d" % r, "qa%d" % r, "sa%d" % r
         qx, sx, ns = ("qp", "sp", 272) if r == 0 else ("qx", "sx", 256)
         table = V("trii") if r == 0 else V("tab")
-        cur = "pb" if r % 2 else "pa"
+        cur, new = ("pb", "pa") if r % 2 else ("pa", "pb")
 
         def plane(b):
             return V("fh", 256 * b, 256 * b + 256)
 
-        def evac(b):
-            act(plane(b), V("psF", 512 * b, 512 * b + 256), 0.5)
+        def w_(b):
+            return V("wq", 128 * b, 128 * b + 128), V("wsc", 128 * b, 128 * b + 128)
 
-        def is_point(o, j):
-            ts(V(o), V(cur, 3, 512, 4), o_(j), A.is_equal)
+        def order(j0, j1):
+            a, b = 16 * j0, 16 * j1
+            tt(V("ne", a, b), I(V("rs"), V("lu", 50, 50 + j1 - j0)), V("kjp", a, b), A.not_equal)
+            scan(V("o16", a, b), V("ne", a, b), V("d1s", 0, b - a), A.mult, A.add)
+            scan(V("osn", a, b), V("ne", a, b), V("d1o", 0, b - a), A.mult, A.add)
 
-        def blend2(b):
-            tt(V("zt", 512 + b, 896, 4), I(plane(b), V("offm", 6, 12)), V("a2", 144 * b, 144 * b + 96), A.add)
-
-        def own(b):
-            tt(V("yw", 256 * b + 96, 256 * b + 192), (ybank[b][0], ybank[b][1] + 32, ybank[b][1] + 128, 1),
-               V("z32", 512 + b, 896, 4), A.add)
-
-        def came(b):
-            tt(V("yw", 256 * b, 256 * b + 96), V("psF", 512 * b, 512 * b + 96), V("z32", b, 384, 4), A.add)
-
-        def place(b):
-            src = I(V("yw", 256 * b, 256 * b + 256), V("offr"))
-            if b in (0, 2):
-                act(V("xt", b, 1024, 4), src, 0.03125)
-            else:
-                ts(V("xt", b, 1024, 4), src, 0.03125, A.mult)
+        def third(j):
+            a = 16 * j
+            tt(V("ix", j, j + 6), V("o16", a + 15, a + 96, 16), V("osn", a + 31, a + 112, 16), A.add)
+            cp(V("ixu", j, j + 6), V("ix", j, j + 6))
+            tt(V("lk", a, a + 96), I(table, V("ixu", j, j + 6)), V("mk"), A.mult)
+            scan(V("ms", a, a + 96), V("nm"), V("lk", a, a + 96), A.mult, A.add)
+            ts(V("offm", j, j + 6), V("ms", a + 15, a + 96, 16), 16.0, A.mult, c16, A.add)
 
         mm(V("psS", 0, ns), V("qu"), V("su"), V(qx, 0, ns), V(sx, 0, ns))
         for b in range(4):
             mm(V("psF", 512 * b, 512 * b + 256), V("qe", 128 * b, 128 * b + 128), V("se", 128 * b, 128 * b + 128),
                V(qx, 0, 256), V(sx, 0, 256))
-        if r == 0:
-            constants_1()
-        else:
-            met()
-            cd1()
+            act(plane(b), V("psF", 512 * b, 512 * b + 256), 0.5)
         tr(V("tt", 0, 256), V("psS", 0, 256))
-        if r > 0:
-            cd2()
-        else:
-            tt(V("w4", 48, 64), V("w5", 0, 16), V("w4", 32, 48), A.add)
         tr(V("tt", 256, 512), V("psS", 16, 272))
-        if r > 0:
-            evac(0)
         act(V("ap", 0, 128), I(V("tt"), V("lu", 18, 26)))
-        if r == 0:
-            tt(V("w4", 48, 64), V("w4", 48, 64), V("w5", 16, 32), A.min)
-            ts(V("mk"), V("ioc"), q_, A.is_equal)
-        else:
-            term(r - 1, 0)
         cp(V("ap", 128, 240), I(V("tt"), V("lu", 26, 33)))
-        if r == 0:
-            ts(V("w4", 48, 64), V("w4", 48, 64), 63.0, A.max, C("pc", 11), A.mult)
-            act(V("pa", 64, 512), V("ones", 0, 448), 0.0)
-            evac(0)
-        else:
-            term(r - 1, 1)
-        evac(1)
-        evac(2)
         tt(V("gg"), I(V("tt"), l_b), V("ap"), A.is_lt)
-        if r == 0:
-            tt(V("tf", 44, 59), V("w4", 48, 63), V("w5", 32, 47), A.add)
-        else:
-            term(r - 1, 2)
-        evac(3)
         scan(V("rs"), V("d0r"), V("gg"), A.mult, A.add)
-        if r == 0:
-            cp(V("tu"), V("tf"))
-        else:
-            table_sum(r - 1)
-            act(V("tab"), I(V(cur), V("tu", 44, 60)))
-        tt(V("ne"), I(V("rs"), l_n), V("kjp"), A.not_equal)
-        if r == 0:
-            cp(V("pa", 67, 512, 4), I(V("trii"), V("tu", 60, 67)))
-            act(V("tab"), I(V(cur), V("tu", 44, 60)))
-        else:
-            tt(V("rk", 0, 15), V("rs", 14, 240, 16), V("iop", 0, 15), A.add)
-        scan(V("o16"), V("ne"), V("d1s"), A.mult, A.add)
-        scan(V("osn"), V("ne"), V("d1o"), A.mult, A.add)
-        if r == 0:
-            tt(V("rk", 0, 15), V("rs", 14, 240, 16), V("iop", 0, 15), A.add)
-        elif last:
+        order(0, 7)
+        ts(V("offo", 0, 6), V("osn", 31, 112, 16), 16.0, A.mult, c16, A.add)
+        third(0)
+        for b in range(4):
+            act(V("a1", 96 * b, 96 * b + 96), I(plane(b), V("offo", 0, 6)))
+            tt(V("zt", b, 384, 4), I(plane(b), V("offm", 0, 6)), V("a1", 96 * b, 96 * b + 96), A.add)
+        quant(V(qs), V(ss), V("zt", 0, 512))
+        send(V(qa, 0, 96), V(qs, 0, 96), "arr%d" % r, dt.uint8, CFG["FIRST"] if r == 0 else 0)
+        send(V(sa, 0, 96), V(ss, 0, 96), "arr%d" % r)
+        ops.append({"kind": "arrive", "q": "a", "r": [], "w": [V(qa, 0, 96), V(sa, 0, 96)], "sem": "arr%d" % r,
+                    "n": 2 * n_in, "after": [len(ops) - 2, len(ops) - 1], "hold": 0, "len": CFG["FLIGHT"]})
+        order(7, 15)
+        ts(V("offo", 6, 14), V("osn", 127, 240, 16), 16.0, A.mult, c16, A.add)
+        third(6)
+        for b in range(4):
+            act(V("a2", 144 * b, 144 * b + 144), I(plane(b), V("offo", 6, 15)))
+            tt(V("zt", 512 + b, 896, 4), I(plane(b), V("offm", 6, 12)), V("a2", 144 * b, 144 * b + 96), A.add)
+            act(V("yw", 256 * b + 192, 256 * b + 256), V("a2", 144 * b + 80, 144 * b + 144), 64.0)
+        quant(V(qa, 96, 224), V(sa, 96, 224), V("zt", 384, 896))
+        act(V("z32", 0, 384), V("zt", 0, 384), 32.0)
+        ts(V("z32", 512, 896), V("zt", 512, 896), 32.0, A.mult)
+        tt(V("rk", 0, 15), V("rs", 14, 240, 16), V("iop", 0, 15), A.add)
+        if last:
             ts(V("rv", 0, 15), V("rk", 0, 15), 16.0, A.mult, q_, A.add)
             ts(V("rv", 16, 31), V("rk", 0, 15), 16.0, A.mult, q_, A.add)
+            tr(V("rvt"), V("rv"))
+            cp(V("offr"), I(V("rvt"), l_32))
         else:
             ts(V("offr", 1, 16), V("rk", 0, 15), 16.0, A.mult, q_, A.add)
-        tt(V("ix", 0, 12), V("o16", 15, 192, 16), V("osn", 31, 208, 16), A.add)
-        ts(V("offo", 1, 16), V("osn", 15, 240, 16), 16.0, A.mult, c16, A.add)
-        is_point("pp", 0)
-        is_point("pq", 1)
-        cp(V("ixu", 0, 12), V("ix", 0, 12))
-        tt(V("do", 0, 3), V("osn", 15, 48, 16), V("osn", 31, 64, 16), A.subtract)
-        if last:
-            tr(V("rvt"), V("rv"))
-        if r == 0:
-            ts(V("offr", 1, 16), V("rk", 0, 15), 16.0, A.mult, q_, A.add)
+        for b in range(4):
+            name, o = ybank[b]
+            mm(V(name, o, o + 128), *w_(b), V(qa, 96, 224), V(sa, 96, 224))
+            tt(V("yw", 256 * b + 96, 256 * b + 192), V(name, o + 32, o + 128), V("z32", 512 + b, 896, 4), A.add)
+        for b in range(4):
+            mm(V("psF", 512 * b, 512 * b + 128), *w_(b), V(qa, 0, 128), V(sa, 0, 128))
+            tt(V("yw", 256 * b, 256 * b + 96), V("psF", 512 * b, 512 * b + 96), V("z32", b, 384, 4), A.add)
+        for b in range(4):
+            src = I(V("yw", 256 * b, 256 * b + 256), V("offr"))
+            if b in (0, 2):
+                act(V("xt", b, 1024, 4), src, 0.03125)
+            else:
+                ts(V("xt", b, 1024, 4), src, 0.03125, A.mult)
+        quant(V("qx"), V("sx"), V("xt"))
         act(V("sq", 0, 240), V("tab", 0, 240), -16.0, F.Square, C("o16", 15))
         act(V("sq", 256, 496), V("tab", 0, 240), -16.0, F.Square, C("o16", 31))
-        tt(V("lk"), I(table, V("ixu", 0, 12)), V("mk"), A.mult)
-        tt(V("re"), V("pp"), V("pq"), A.subtract)
-        scan(V("ms"), V("nm"), V("lk"), A.mult, A.add)
-        if r > 0:
-            rows()
-        else:
-            quant(V("qv"), V("sv"), V("vin"))
-        ts(V("offm"), V("ms", 15, 192, 16), 16.0, A.mult, c16, A.add)
+        scan(V("ab", 0, 256), V("sq", 0, 256), V("ones", 0, 256), A.min, A.add)
+        scan(V("ab", 256, 512), V("sq", 256, 512), V("ones", 0, 256), A.min, A.add)
+        lin(V("r2", 0, 32, 2), V("ab", 15, 256, 16), -1.0, 16.0)
+        tt(V("df", 0, 15), V("ab", 287, 512, 16), V("ab", 271, 496, 16), A.subtract)
+        tt(V("nw", 17, 288, 18), V("ab", 271, 512, 16), V("ab", 15, 256, 16), A.subtract)
+        tt(V("do", 0, 3), V("osn", 15, 48, 16), V("osn", 31, 64, 16), A.subtract)
         ts(C("t2", 0), C("ms", 15), o_(2), A.is_equal, C("do", 2), A.mult)
-        if r == 0:
-            rows()
-        if last:
-            cp(V("offr"), I(V("rvt"), l_32))
-        if r > 0:
-            diffs()
-        for b in range(4):
-            act(V("a1", 96 * b, 96 * b + 96), I(plane(b), V("offo", 2, 8)))
-        for b in range(4):
-            tt(V("zt", b, 384, 4), I(plane(b), V("offm", 0, 6)), V("a1", 96 * b, 96 * b + 96), A.add)
-            if b == 0:
-                walk(0)
-                if r == 0:
-                    diffs()
-            if b == 2:
-                step(0)
-        tt(V("amb"), V("ab", 271, 512, 16), V("ab", 15, 256, 16), A.subtract)
-        walk(1)
-        quant(V(qs), V(ss), V("zt", 0, 512))
-        send(V(qa, 0, 96), V(qs, 0, 96), "arr%d" % r, dt.uint8)
-        send(V(sa, 0, 96), V(ss, 0, 96), "arr%d" % r)
-        ops.append({"kind": "arrive", "q": None, "r": [], "w": [V(qa, 0, 96), V(sa, 0, 96)], "sem": "arr%d" % r, "n": 2 * n_in})
-        if r == 0:
-            iota(V("r8"), [[0, 256]], 0, 0)
-            iota(V("nw", 7, 256, 8), [[0, 32]], 2, 0)
-            iota(V("pb", 0, 64), [[1, 16], [0, 4]], 0, 0)
-            iota(V("r8", 7, 256, 8), [[0, 32]], -1, 0)
-            iota(V("r8", 0, 256, 8), [[0, 32]], 2, 0)
-            select(V("r4"), V("ones", 0, 448), [[0, 112], [1, 4]], A.is_gt, 0.0)
-        for b in range(4):
-            act(V("a2", 144 * b, 144 * b + 144), I(plane(b), V("offo", 8, 17)))
-        act(V("z32", 0, 384), V("zt", 0, 384), 32.0)
-        for b in range(4):
-            act(V("yw", 256 * b + 192, 256 * b + 256), V("a2", 144 * b + 80, 144 * b + 144), 64.0)
-        act(C("dof", 0), C("do", 0))
-        act(V("rx", 112, 336), I(V("re", 0, 16), l_exy))
-        act(V("rx", 0, 112), V("re", 16, 128), C("dof", 0), F.Identity)
-        blend2(0)
-        step(1)
-        blend2(1)
-        if last:
-            walk(2)
-            blend2(2)
-            step(2)
-            blend2(3)
-            walk(3)
-        else:
-            blend2(2)
-            walk(2)
-            blend2(3)
-            step(2)
-        quant(V(qa, 96, 224), V(sa, 96, 224), V("zt", 384, 896))
-        for b in range(4):
-            mm((ybank[b][0], ybank[b][1], ybank[b][1] + 128, 1), V("wq", 128 * b, 128 * b + 128),
-               V("wsc", 128 * b, 128 * b + 128), V(qa, 96, 224), V(sa, 96, 224))
-        for b in range(4):
-            mm(V("psF", 512 * b, 512 * b + 128), V("wq", 128 * b, 128 * b + 128), V("wsc", 128 * b, 128 * b + 128),
-               V(qa, 0, 128), V(sa, 0, 128))
-        if last:
-            step(3)
-            ts(V("z32", 512, 896), V("zt", 512, 896), 32.0, A.mult)
-            walk(4)
-            step(4)
-            own(0)
-            own(1)
-            walk(5)
-            own(2)
-            own(3)
-            step(5)
-            walk(6)
-            came(0)
-            came(1)
-            met()
-            came(2)
-            came(3)
-            cd1()
-            place(0)
-            place(1)
-            cd2()
-            place(2)
-            place(3)
-            term(r, 0)
-        else:
-            walk(3)
-            ts(V("z32", 512, 896), V("zt", 512, 896), 32.0, A.mult)
-            step(3)
-            own(0)
-            own(1)
-            walk(4)
-            own(2)
-            own(3)
-            step(4)
-            came(0)
-            came(1)
-            came(2)
-            came(3)
-            place(0)
-            place(2)
-            walk(5)
-            place(1)
-            step(5)
-            place(3)
-            walk(6)
-        quant(V("qx"), V("sx"), V("xt"))
 
+        def mark(i, k):
+            ts(V("nw", 1 + i, 288, 9), V("r2"), k, A.not_equal)
+
+        def hop(s, i, e):
+            scan(V("wk", 16 * s, 16 * s + 15), V("nw", 1 + i + 9 * e, 270, 18), V("df", 0, 15), A.mult, A.add)
+            return C("wk", 16 * s + 14)
+
+        ts(V("nw", 1, 288, 9), V("r2"), C("t2", 0), A.add, o_(2), A.not_equal)
+        mark(2, hop(1, 0, 1))
+        mark(1, hop(0, 0, 0))
+        mark(4, hop(3, 2, 0))
+        mark(3, hop(2, 1, 0))
+        mark(5, hop(4, 4, 0))
+        scan(V("nc"), V("nw"), V("md"), A.mult, A.add)
+        ts(V(cur, 1, 640, 5), V(cur, 4, 640, 5), -LIFT, A.add, o_(0), A.is_equal)
+        ts(V(cur, 0, 640, 5), V(cur, 4, 640, 5), -LIFT, A.add, o_(1), A.is_equal)
+        tt(V("ev"), V(cur, 1, 80, 5), V(cur, 0, 80, 5), A.subtract)
+        lin(V("hm", 3, 560, 5), I(V("ev"), l_y), BIG, 1.0)
+        lin(V("hm", 4, 560, 5), I(V("ev"), l_x), 1.0, 1.0 / BIG)
+        lin(C("dof", 0), C("do", 0), BIG, 0.0)
+        act(V("hm", 2, 560, 5), I(V("nc"), l_cx), C("dof", 0), F.Identity)
+        act(V(cur, 82, 640, 5), I(V("nc"), l_wx))
+        act(V(cur, 83, 640, 5), I(V("nc"), l_wy))
+        scan(V(new, 80, 640), V("hm"), V(cur, 80, 640), A.mult, A.add)
+        lin(V("tabo" if last else "tab"), I(V(new), l_tab), 1.0, -LIFT)
+
+    store("y", T.ot[:], T.tabo[:], [V("tabo")])
     mm(V("psS", 0, 256), V("qv"), V("sv"), V("qx"), V("sx"))
-    store("y", T.oc[:], T.qx[:].bitcast(dt.uint8), [V("qx")])
-    for t in (1, 2):
-        term(ROUNDS - 1, t)
     act(V("yo"), V("psS", 0, 256))
     store("s", T.y[:], T.yo[:], [V("yo")])
-    table_sum(ROUNDS - 1)
-    new = V("pa" if (ROUNDS - 1) % 2 else "pb")
-    cp(V("tabo"), I(new, V("tu", 44, 60)))
+    store("y", T.oc[:], T.qx[:].bitcast(dt.uint8), [V("qx")])
     for k in range(4):
         store("y", T.osc[4 * k:4 * k + 4, :], T.sx[32 * k:32 * k + 4, :], [V("sx")])
-    store("y", T.ot[:], T.tabo[:], [V("tabo")])
 
-    schedule(ops, g, T)
+    if not ORDER:
+        ORDER.extend(arrange(ops))
+    issue([ops[i] for i in ORDER], g, T)
     g.wait_ge(T.sem.sent, 2 * ROUNDS * n_out)

@@ -5,14 +5,14 @@ F = ActivationFunctionType
 ROUNDS = 3
 C4, U8, BF, F32, I32, U16 = "float8_e4m3fn_x4", "uint8", "bfloat16", "float32", "int32", "uint16"
 SB = {
-    BF: dict(xin=1024, uin=512, vin=512, et=1032, idn=128, ones=560, xt=1024, ioc=96, d0r=240, kjp=240, d1o=128,
-             mk=96, nm=96, d1s=128, gg=240, rs=240, ne=240, osn=240, o16=240, ix=12, lk=192, ms=192,
-             fh=1024, a1=384, a2=576, zt=896, z32=896, yw=1024, tab=256, sq=512, ab=512, df=16, t2=2, rk=16,
+    BF: dict(xin=1024, uin=512, vin=512, et=1032, idn=128, ones=516, xt=1024, ioc=96, d0r=240, kjp=240, d1o=240,
+             mk=96, nm=96, d1s=192, gg=240, rs=240, ne=240, osn=240, o16=192, ix=12, lk=192, ms=192,
+             fh=1024, a1=384, a2=576, zt=896, z32=896, yw=1024, tab=240, sq=512, ab=512, df=16, t2=2, rk=16,
              nw=288, md=288, nc=288, do=4, wk=80, r2=32, ev=16, hm=560, pa=640, pb=640),
-    F32: dict(pc=16, iop=16, w1=32, w3=32, w4=64, w5=48, lf=60, tf=64, tt=512, ap=240, rv=32, rvt=32,
+    F32: dict(pc=16, iop=18, w1=32, w3=32, w4=64, w5=32, lf=18, tf=64, tt=512, ap=240, rv=32, rvt=32,
               tabo=256, dof=2, yo=256),
     I32: dict(trii=256, pi=4, w2=32),
-    U16: dict(lu=60, tu=64, ixu=12, offo=16, offm=12, offr=16),
+    U16: dict(lu=68, tu=64, ixu=12, offo=16, offm=12, offr=16),
     C4: dict(wq=512, qu=128, qv=128, qe=512, qn=256, qp=272, qx=256, qs0=128, qs1=128, qs2=128, qa0=224, qa1=224, qa2=224),
     U8: dict(wsc=512, su=128, sv=128, se=512, sn=256, sp=272, sx=256, ss0=128, ss1=128, ss2=128, sa0=224, sa1=224, sa2=224),
 }
@@ -22,7 +22,10 @@ SEMAPHORES = ["cv", "cs", "ct", "cg", "sent"] + ["arr%d" % r for r in range(ROUN
 COUNTER = {"v": "cv", "s": "cs", "t": "ct", "g": "cg"}
 BIG = 1024.0
 LIFT = 128.0
-CFG = dict(WAIT=180, FLIGHT=1500, LOCAL=1300, ISSUE=350, FIRST=1500, SLACK=100, GUARD=300, ACT=180)
+GUESS = [dict(same=255, other=250, flight=1000, first=2000, fixed=0, least=64, act=80, gather=130),
+         dict(same=215, other=260, flight=1400, first=1500, fixed=25, least=40, act=90, gather=110)]
+CFG = dict(LOCAL=1100, DMA=200, ISSUE=240, SWEEPS=2, REACH=4,
+           PASSES=[(240, 30), (240, 30), (220, 60), (260, 0), (260, 40)])
 ORDER = []
 
 
@@ -82,35 +85,94 @@ def arrange(ops):
     deps = depends(ops)
     for i, op in enumerate(ops):
         deps[i].update(op.get("after", ()))
-    n = len(ops)
+    n, queue, above = len(ops), [op["q"] for op in ops], []
+    for d in deps:
+        implied = set().union(*[above[j] for j in d])
+        above.append(implied | d)
+        d -= implied
     succ = [[] for _ in ops]
     for i in range(n):
         for j in deps[i]:
             succ[j].append(i)
+    holds = [[op["hold"](u) for op in ops] for u in GUESS]
+    spans = [[op["hold"](u) + op["more"](u) for op in ops] for u in GUESS]
+    hold_, span_ = [[sum(x) / len(x) for x in zip(*y)] for y in (holds, spans)]
     behind = [0.0] * n
     for i in reversed(range(n)):
-        behind[i] = ops[i]["len"] + max([CFG["WAIT"] + behind[k] for k in succ[i]] + [0])
-    done, free, order = {}, {op["q"]: 0.0 for op in ops}, []
-    todo = list(range(n))
-    while todo:
-        start = {}
-        for i in todo:
-            start[i] = max([free[ops[i]["q"]]] + [(done[j] if j in done else start[j] + ops[j]["len"]) + CFG["WAIT"]
-                                                  for j in deps[i]])
-        end = max(start[i] + behind[i] for i in todo)
+        behind[i] = span_[i] + max([CFG["PASSES"][0][0] + behind[k] for k in succ[i]] + [0])
 
-        def fits(i):
-            stop = start[i] + ops[i]["hold"]
-            return all(stop <= max(start[j], end - behind[j] - CFG["GUARD"]) + CFG["SLACK"] for j in todo
-                       if behind[j] > behind[i] and ops[j]["q"] == ops[i]["q"] and start[j] < stop)
+    def lay(before, after, key, backwards, wait, slack):
+        left = [len(b) for b in before]
+        ready = [i for i in range(n) if not left[i]]
+        start, done, busy = [0.0] * n, [0.0] * n, {}
+        while ready:
+            i = min(ready, key=lambda k: (key[k], k))
+            ready.remove(i)
+            hold = hold_[i]
+            lead = span_[i] - hold if backwards else 0
+            t = max([0] + [done[j] + wait for j in before[i]]) + lead
+            taken = busy.setdefault(ops[i]["q"], [])
+            for a, b in taken:
+                if b > t:
+                    if t < a and t + hold <= a + slack:
+                        break
+                    t = b
+            taken.append((t, t + hold))
+            taken.sort()
+            start[i], done[i] = t - lead, t - lead + span_[i]
+            for k in after[i]:
+                left[k] -= 1
+                if not left[k]:
+                    ready.append(k)
+        return start, done
 
-        ready = sorted((i for i in todo if all(j in done for j in deps[i])), key=lambda i: (start[i], -behind[i]))
-        i = next((i for i in ready if fits(i)), ready[0])
-        todo.remove(i)
-        order.append(i)
-        free[ops[i]["q"]] = start[i] + ops[i]["hold"]
-        done[i] = start[i] + ops[i]["len"]
-    return order
+    def ends(order, k):
+        same, other, hold, span = GUESS[k]["same"], GUESS[k]["other"], holds[k], spans[k]
+        free, done = {}, [0.0] * n
+        for i in order:
+            q = queue[i]
+            t = free.get(q, 0.0)
+            for j in deps[i]:
+                e = done[j] + (same if queue[j] == q else other)
+                if e > t:
+                    t = e
+            free[q] = t + hold[i]
+            done[i] = t + span[i]
+        return done
+
+    def length(order):
+        return sum(max(done) + sum(done) / n for done in (ends(order, k) for k in range(len(GUESS))))
+
+    def polish(order):
+        now = length(order)
+        for _ in range(CFG["SWEEPS"]):
+            for i in range(n):
+                p, better = order.index(i), None
+                for step, stop in ((-1, deps[i]), (1, succ[i])):
+                    k, passed = p, 0
+                    while passed < CFG["REACH"] and 0 <= k + step < n and order[k + step] not in stop:
+                        k += step
+                        if queue[order[k]] == queue[i]:
+                            passed += 1
+                            moved = order[:p] + order[p + 1:]
+                            moved.insert(k, i)
+                            t = length(moved)
+                            if t < now - 1e-6:
+                                now, better = t, moved
+                order = better or order
+        return order
+
+    best, key = None, [-b for b in behind]
+    for wait, slack in CFG["PASSES"]:
+        if best:
+            done = [a + b for a, b in zip(ends(best[1], 0), ends(best[1], 1))]
+            key = [-d for d in lay(succ, deps, [-d for d in done], True, wait, slack)[1]]
+        start = lay(deps, succ, key, False, wait, slack)[0]
+        order = polish(sorted(range(n), key=lambda i: (start[i], i)))
+        end = sum(max(ends(order, k)) for k in range(len(GUESS)))
+        if best is None or end < best[0]:
+            best = (end, order)
+    return best[1]
 
 
 def issue(ops, g, T):
@@ -191,20 +253,23 @@ def rank_program(g, core, T, topo):
                 out += [x[1], x[2]] if x[0] == "@" else [x]
         return out
 
-    def rec(q, f, r, w, kind="compute", hold=None, more=0):
-        if hold is None:
-            narrow = q == "v" and all(SCRATCH[x[0]][2] in (BF, U16) for x in flat([r[0], w[0]] if r else w))
-            if r and is_view(r[0]) and r[0][0] == "@":
-                hold = 70 + 1.56 * size(r[0])
-            else:
-                hold = max(64, size(w[0]) * (0.5 if narrow else 1)) if q == "v" else CFG["ACT"] + size(w[0])
-        ops.append({"q": q, "f": f, "r": flat(r), "w": flat(w), "kind": kind, "hold": hold, "len": hold + more})
+    def rec(q, f, r, w, kind="compute", hold=None, more=0, slow=1, first=False):
+        def cycles(u):
+            if hold is not None:
+                return hold + (u["first"] if first else 0)
+            if r and r[0][0] == "@":
+                return (60 if q == "v" else u["gather"]) + 1.6 * size(r[0])
+            if q == "s":
+                return u["act"] + size(w[0])
+            narrow = all(SCRATCH[x[0]][2] in (BF, U16) for x in flat([r[0], w[0]] if r else w))
+            return u["fixed"] + max(u["least"], size(w[0]) * (0.5 if narrow else 1) * slow)
+        ops.append({"q": q, "f": f, "r": flat(r), "w": flat(w), "kind": kind, "hold": cycles, "more": lambda u: more})
 
     def cp(o, i, word=None):
         rec("v", lambda q: q.tensor_copy(ap(o, word), ap(i, word)), [i], [o])
 
     def tt(o, a, b, op):
-        rec("v", lambda q: q.tensor_tensor(ap(o), ap(a), ap(b), op), [a, b], [o])
+        rec("v", lambda q: q.tensor_tensor(ap(o), ap(a), ap(b), op), [a, b], [o], slow=1 if a[0][:2] == "ps" else 2)
 
     def ts(o, a, s1, op0, s2=None, op1=None):
         if op1 is None:
@@ -232,8 +297,8 @@ def rank_program(g, core, T, topo):
             kw["bias"] = ap(bias)
         rec("s", lambda q: q.activation(ap(o), ap(i), func, **kw), [i, bias, scale], [o])
 
-    def lin(o, i, scale, bias):
-        if i[0] == "@":
+    def lin(o, i, scale, bias, q="v"):
+        if q == "s":
             act(o, i, scale, F.Identity, bias)
         else:
             ts(o, i, scale, A.mult, bias, A.add)
@@ -249,18 +314,18 @@ def rank_program(g, core, T, topo):
     def select(o, i, pattern, op, fill, base=0, cm=0):
         rec("g", lambda q: q.affine_select(ap(o), ap(i), pattern, op, fill, base, cm), [i], [o], hold=200 + 2 * size(o))
 
-    def load(q, o, src, word=None, after=()):
-        rec(q, lambda e: e.dma_start(ap(o, word), src), list(after), [o], "dma", 60, CFG["LOCAL"])
+    def load(q, o, src, word=None, after=(), more=500):
+        rec(q, lambda e: e.dma_start(ap(o, word), src), list(after), [o], "dma", CFG["DMA"], CFG["LOCAL"] + more)
 
-    def store(q, dst, src, reads):
-        rec(q, lambda e: e.dma_start(dst, src), reads, [], "dma", 60, CFG["LOCAL"])
+    def store(q, dst, src, reads, more=400):
+        rec(q, lambda e: e.dma_start(dst, src), reads, [], "dma", CFG["DMA"], CFG["LOCAL"] + more)
 
-    def send(dst, src, sem, word=None, first=0):
+    def send(dst, src, sem, word=None, first=False):
         rec("g", lambda q: q.remote_dma(ap(dst, word), ap(src, word), T.sem[sem], T.sem.sent, pid, rid, mask),
-            [src], [], "remote", CFG["ISSUE"] + first)
+            [src], [], "remote", CFG["ISSUE"], first=first)
 
-    load("y", V("xin"), T.x[:])
-    load("y", V("uin"), T.u[:])
+    load("y", V("xin"), T.x[:], more=600)
+    load("y", V("uin"), T.u[:], more=1100)
     load("y", V("trii"), T.tri[:], None, [C("xin", 0)])
     load("y", V("wq"), T.wc[:], dt.uint8, [C("xin", 0)])
     load("y", V("wsc"), T.ws[:], None, [C("xin", 0)])
@@ -268,14 +333,14 @@ def rank_program(g, core, T, topo):
 
     q_, h_, p32, c16, c16q = C("pc", 0), C("pc", 1), C("pc", 2), C("pc", 3), C("pc", 4)
     iota(C("pi", 0), [[0, 1]], 0, 1, False)
-    iota(V("iop"), [[1, 16]], 0, 0)
+    iota(V("iop"), [[1, 18]], 0, 0)
     mset(V("ones"), 1.0)
     select(V("idn"), V("ones", 0, 128), [[-1, 128]], A.is_equal, 0.0, 0, 1)
     iota(V("ioc"), [[0, 6], [1, 16]], 0, 0)
     select(V("d0r"), V("ones", 0, 240), [[1, 15], [-1, 16]], A.not_equal, -1.0)
     iota(V("kjp"), [[1, 15], [-1, 16]], 0, 0)
-    select(V("d0r", 0, 240, 16), V("d0r", 0, 240, 16), [[0, 15]], A.is_gt, 0.0)
-    select(V("kjp", 15, 240, 16), V("kjp", 15, 240, 16), [[0, 15]], A.is_gt, 99.0)
+    iota(V("d0r", 0, 240, 16), [[0, 15]], 0, 0)
+    iota(V("kjp", 15, 240, 16), [[0, 15]], 99, 0)
     select(V("nm"), V("ones", 0, 96), [[0, 6], [1, 16]], A.is_gt, 0.0)
     iota(V("sq", 240, 256), [[256, 16]], 0, 0)
     iota(V("sq", 496, 512), [[256, 16]], 0, 0)
@@ -286,30 +351,31 @@ def rank_program(g, core, T, topo):
     select(V("md"), V("ones", 0, 288), [[0, 16], [1, 18]], A.is_equal, 0.0)
     iota(V("md", 16, 288, 18), [[0, 16]], -1, 0)
     select(V("nw"), V("ones", 0, 288), [[0, 16], [1, 18]], A.not_equal, 0.0)
+    iota(V("tabo", 240, 256), [[1, 16]], 0, 0)
+    iota(V("w4", 32, 48), [[5, 16]], 4, 0)
+    select(V("lf"), V("iop"), [[1, 18]], A.is_gt, 16.0)
     ts(C("pi", 1), C("pi", 0), 15, A.bitwise_and)
     ts(C("pi", 2), C("pi", 0), 4, A.arith_shift_right, 1, A.bitwise_and)
     ts(C("pi", 3), C("pi", 0), 31, A.bitwise_and)
     cp(V("pc", 0, 3), V("pi", 1, 4))
     ts(c16q, q_, 16.0, A.mult)
-    lin(c16, q_, 1.0, 16.0)
-    mset(V("lf", 16, 18), 0.0)
-    ts(V("lf", 1, 16), V("iop", 0, 15), c16q, A.add)
-    ts(C("lf", 0), c16q, 15.0, A.add)
-    cp(V("lu", 0, 18), V("lf", 0, 18))
-    ts(V("w1", 0, 16), V("iop"), q_, A.max, 1.0, A.add)
-    ts(V("w1", 16, 32), V("iop"), q_, A.min, 1.0, A.add)
+    lin(c16, q_, 1.0, 16.0, "s")
+    ts(V("lu", 0, 16), V("lf", 0, 16), c16q, A.add, -1.0, A.add)
+    mset(V("lu", 16, 18), 0)
+    ts(V("w1", 0, 16), V("iop", 0, 16), q_, A.max, 1.0, A.add)
+    ts(V("w1", 16, 32), V("iop", 0, 16), q_, A.min, 1.0, A.add)
     ts(V("w2"), V("w1"), h_, A.add)
     ts(V("w2"), V("w2"), 1, A.bitwise_and)
     ts(V("w3"), V("w2"), 15.0, A.mult)
     tt(V("w3"), V("w3"), V("w1"), A.add)
     ts(V("lu", 18, 50), V("w3"), 16.0, A.mult)
     ts(C("pc", 5), c16q, 14.0, A.add, 238.0, A.min)
-    ts(V("lu", 50, 58), V("iop", 0, 8), 0.0, A.mult, C("pc", 5), A.add)
-    cp(C("lu", 58), p32)
-    l_pick, l_b, l_32 = V("lu", 0, 17), V("lu", 34, 49), V("lu", 58, 59)
-    mset(V("d1o"), -1.0)
-    mset(V("d1o", 15, 128, 16), 15.0)
-    lin(V("d1s"), V("d1o"), 16.0, 0.0)
+    ts(V("lu", 50, 66), V("iop", 0, 16), 0.0, A.mult, C("pc", 5), A.add)
+    cp(C("lu", 66), p32)
+    l_pick, l_b, l_n, l_32 = V("lu", 0, 17), V("lu", 34, 49), V("lu", 50, 65), V("lu", 66, 67)
+    act(V("d1o"), V("ones", 0, 240), -1.0)
+    act(V("d1o", 15, 240, 16), V("ones", 0, 15), 15.0)
+    act(V("d1s"), V("d1o", 0, 192), 16.0)
     ts(V("mk"), V("ioc"), q_, A.is_equal)
     act(V("et", 0, 516), V("ones", 0, 516), 0.0)
     act(V("et", 516, 1032), V("ones", 0, 516), 0.0)
@@ -318,40 +384,31 @@ def rank_program(g, core, T, topo):
     for b in range(4):
         o = 516 * (b % 2) + (2 if b < 2 else 0)
         quant(V("qe", 128 * b, 128 * b + 128), V("se", 128 * b, 128 * b + 128), V("et", o, o + 512))
-    lin(C("pc", 6), q_, 1.0, 1.0)
-    lin(C("pc", 7), q_, 80.0, 0.0)
-    lin(C("pc", 8), q_, 5.0, 1204.0)
-    lin(C("pc", 9), q_, 1.0, 240.0)
-    lin(C("pc", 12), q_, 18.0, 16.0)
-    lin(C("pc", 13), q_, 18.0, 17.0)
-    ts(C("pc", 10), q_, 15.0, A.is_equal)
-    ts(C("pc", 11), q_, 15.0, A.not_equal)
-    lin(V("w4", 0, 8), V("iop", 0, 8), 1.0, C("pc", 6))
+    lin(C("pc", 6), q_, 1.0, 1.0, "s")
+    ts(C("pc", 7), q_, 15.0, A.not_equal, 80.0, A.mult)
+    lin(C("pc", 8), q_, 5.0, 1204.0, "s")
+    lin(C("pc", 9), q_, 1.0, 240.0, "s")
+    lin(V("w4", 0, 8), V("iop", 0, 8), 1.0, C("pc", 6), "s")
     ts(V("w4", 8, 16), V("w4", 0, 8), 15.0, A.is_ge, -15.0, A.mult)
     tt(V("tf", 8, 16), V("w4", 0, 8), V("w4", 8, 16), A.add)
-    lin(V("tf", 0, 8), V("iop", 0, 8), 0.0, q_)
-    lin(V("tf", 16, 24), V("iop", 0, 8), 0.0, C("pc", 12))
-    lin(V("tf", 24, 32), V("iop", 0, 8), 0.0, C("pc", 13))
-    lin(V("tf", 32, 40), V("tf", 8, 16), 18.0, 17.0)
-    lin(V("tf", 40, 48), V("tf", 8, 16), 1.0, c16q)
-    lin(V("w4", 32, 48), V("iop"), 5.0, 4.0)
-    lin(V("w4", 16, 32), V("iop"), -80.0, C("pc", 7))
-    ts(V("w5", 0, 16), V("w4", 16, 32), 0.0, A.is_lt, 1200.0, A.mult)
+    lin(V("tf", 0, 8), V("iop", 0, 8), 0.0, q_, "s")
+    lin(V("tf", 16, 24), V("tf", 0, 8), 18.0, 16.0, "s")
+    lin(V("tf", 24, 40), V("tf", 0, 16), 18.0, 17.0, "s")
+    lin(V("tf", 40, 48), V("tf", 8, 16), 1.0, c16q, "s")
+    lin(V("w4", 16, 32), V("iop", 0, 16), -1.0, q_, "s")
+    ts(V("w5", 0, 16), V("w4", 16, 32), 0.0, A.is_lt, 15.0, A.mult)
     tt(V("w5", 0, 16), V("w5", 0, 16), V("w4", 16, 32), A.add)
-    lin(V("w5", 32, 48), V("w4", 32, 48), C("pc", 10), 0.0)
-    lin(V("w5", 16, 32), V("w5", 0, 16), -1.0, C("pc", 8))
+    lin(V("w5", 0, 16), V("w5", 0, 16), C("pc", 7), 0.0, "s")
+    lin(V("w5", 16, 32), V("w5", 0, 16), -1.0, C("pc", 8), "s")
     tt(V("w4", 48, 64), V("w5", 0, 16), V("w4", 32, 48), A.add)
     tt(V("w4", 48, 64), V("w4", 48, 64), V("w5", 16, 32), A.min)
-    ts(V("w4", 48, 64), V("w4", 48, 64), 79.0, A.max, C("pc", 11), A.mult)
-    tt(V("tf", 48, 63), V("w4", 48, 63), V("w5", 32, 47), A.add)
-    lin(C("tf", 63), q_, 5.0, 4.0)
-    cp(V("tu", 0, 48), V("tf", 0, 48))
-    cp(V("tu", 48, 64), V("tf", 48, 64))
-    l_x, l_y, l_cx, l_wx, l_wy, l_xy, l_tab = [V("tu", 8 * k, 8 * k + 7) for k in range(6)] + [V("tu", 48, 64)]
+    ts(C("pc", 10), q_, 15.0, A.not_equal, 79.0, A.mult)
+    ts(V("tf", 48, 64), V("w4", 48, 64), C("pc", 10), A.max)
+    cp(V("tu"), V("tf"))
+    l_x, l_y, l_cx, l_wx, l_wy, l_xy, l_tab = [V("tu", 8 * k, 8 * k + 7) for k in range(6)] + [V("tu", 48, 63)]
     act(V("hm", 0, 560, 5), V("ones", 0, 112), 0.0)
     act(V("hm", 1, 560, 5), V("ones", 0, 112), -1.0)
-    act(V("pa", 80, 640), V("ones"), 0.0)
-    lin(V("rv", 15, 32, 16), V("iop", 0, 2), 0.0, C("pc", 9))
+    lin(V("rv", 15, 32, 16), V("iop", 0, 2), 0.0, C("pc", 9), "s")
     cp(C("offo", 14), q_)
     cp(C("offr", 0), C("pc", 9))
 
@@ -361,7 +418,7 @@ def rank_program(g, core, T, topo):
     quant(V("qu"), V("su"), V("uin"))
     quant(V("qv"), V("sv"), V("vin"))
     ts(V("pa", 84, 640, 5), I(V("trii"), l_xy), LIFT, A.add)
-    lin(V("tab"), I(V("pa"), l_tab), 1.0, -LIFT)
+    cp(V("tab"), V("trii", 0, 240))
 
     def o_(j):
         return C("osn", 16 * j + 15)
@@ -372,7 +429,6 @@ def rank_program(g, core, T, topo):
         last = r == ROUNDS - 1
         qs, ss, qa, sa = "qs%d" % r, "ss%d" % r, "qa%d" % r, "sa%d" % r
         qx, sx, ns = ("qp", "sp", 272) if r == 0 else ("qx", "sx", 256)
-        table = V("trii") if r == 0 else V("tab")
         cur, new = ("pb", "pa") if r % 2 else ("pa", "pb")
 
         def plane(b):
@@ -381,45 +437,39 @@ def rank_program(g, core, T, topo):
         def w_(b):
             return V("wq", 128 * b, 128 * b + 128), V("wsc", 128 * b, 128 * b + 128)
 
-        def order(j0, j1):
-            a, b = 16 * j0, 16 * j1
-            tt(V("ne", a, b), I(V("rs"), V("lu", 50, 50 + j1 - j0)), V("kjp", a, b), A.not_equal)
-            scan(V("o16", a, b), V("ne", a, b), V("d1s", 0, b - a), A.mult, A.add)
-            scan(V("osn", a, b), V("ne", a, b), V("d1o", 0, b - a), A.mult, A.add)
-
-        def third(j):
-            a = 16 * j
-            tt(V("ix", j, j + 6), V("o16", a + 15, a + 96, 16), V("osn", a + 31, a + 112, 16), A.add)
-            cp(V("ixu", j, j + 6), V("ix", j, j + 6))
-            tt(V("lk", a, a + 96), I(table, V("ixu", j, j + 6)), V("mk"), A.mult)
-            scan(V("ms", a, a + 96), V("nm"), V("lk", a, a + 96), A.mult, A.add)
-            ts(V("offm", j, j + 6), V("ms", a + 15, a + 96, 16), 16.0, A.mult, c16, A.add)
-
-        mm(V("psS", 0, ns), V("qu"), V("su"), V(qx, 0, ns), V(sx, 0, ns))
+        for name, a, b in (("psS", 0, 272),) if r == 0 else (("psY", 0, 128), ("psS", 112, 256)):
+            mm(V(name, 0, b - a), V("qu"), V("su"), V(qx, a, b), V(sx, a, b))
         for b in range(4):
             mm(V("psF", 512 * b, 512 * b + 256), V("qe", 128 * b, 128 * b + 128), V("se", 128 * b, 128 * b + 128),
                V(qx, 0, 256), V(sx, 0, 256))
             act(plane(b), V("psF", 512 * b, 512 * b + 256), 0.5)
-        tr(V("tt", 0, 256), V("psS", 0, 256))
-        tr(V("tt", 256, 512), V("psS", 16, 272))
-        act(V("ap", 0, 128), I(V("tt"), V("lu", 18, 26)))
-        cp(V("ap", 128, 240), I(V("tt"), V("lu", 26, 33)))
-        tt(V("gg"), I(V("tt"), l_b), V("ap"), A.is_lt)
-        scan(V("rs"), V("d0r"), V("gg"), A.mult, A.add)
-        order(0, 7)
-        ts(V("offo", 0, 6), V("osn", 31, 112, 16), 16.0, A.mult, c16, A.add)
-        third(0)
+        for o, name, a, b in (((0, "psS", 0, 256), (256, "psS", 16, 272)) if r == 0 else
+                              ((0, "psY", 0, 128), (256, "psY", 16, 112), (128, "psS", 16, 144), (352, "psS", 0, 160))):
+            tr(V("tt", o, o + b - a), V(name, a, b))
+        cp(V("ap", 0, 128), I(V("tt"), V("lu", 18, 26)))
+        act(V("ap", 128, 240), I(V("tt"), V("lu", 26, 33)))
+        for a, b in ((0, 8), (8, 15)):
+            tt(V("gg", 16 * a, 16 * b), I(V("tt"), V("lu", 34 + a, 34 + b)), V("ap", 16 * a, 16 * b), A.is_lt)
+            scan(V("rs", 16 * a, 16 * b), V("d0r", 16 * a, 16 * b), V("gg", 16 * a, 16 * b), A.mult, A.add)
+        for j0, j1, j in ((0, 7, 0), (7, 15, 6)):
+            a, b, e = 16 * j0, 16 * j1, 16 * j
+            tt(V("ne", a, b), I(V("rs"), V("lu", 50, 50 + j1 - j0)), V("kjp", a, b), A.not_equal)
+            scan(V("o16", a, min(b, 192)), V("ne", a, min(b, 192)), V("d1s", a, min(b, 192)), A.mult, A.add)
+            scan(V("osn", a, b), V("ne", a, b), V("d1o", a, b), A.mult, A.add)
+            ts(V("offo", j, j1 - 1), V("osn", e + 31, b, 16), 16.0, A.mult, c16, A.add)
+            tt(V("ix", j, j + 6), V("o16", e + 15, e + 96, 16), V("osn", e + 31, e + 112, 16), A.add)
+            cp(V("ixu", j, j + 6), V("ix", j, j + 6))
+            tt(V("lk", e, e + 96), I(V("tab"), V("ixu", j, j + 6)), V("mk"), A.mult)
+            scan(V("ms", e, e + 96), V("nm"), V("lk", e, e + 96), A.mult, A.add)
+            ts(V("offm", j, j + 6), V("ms", e + 15, e + 96, 16), 16.0, A.mult, c16, A.add)
         for b in range(4):
             act(V("a1", 96 * b, 96 * b + 96), I(plane(b), V("offo", 0, 6)))
             tt(V("zt", b, 384, 4), I(plane(b), V("offm", 0, 6)), V("a1", 96 * b, 96 * b + 96), A.add)
         quant(V(qs), V(ss), V("zt", 0, 512))
-        send(V(qa, 0, 96), V(qs, 0, 96), "arr%d" % r, dt.uint8, CFG["FIRST"] if r == 0 else 0)
+        send(V(qa, 0, 96), V(qs, 0, 96), "arr%d" % r, dt.uint8, r == 0)
         send(V(sa, 0, 96), V(ss, 0, 96), "arr%d" % r)
         ops.append({"kind": "arrive", "q": "a", "r": [], "w": [V(qa, 0, 96), V(sa, 0, 96)], "sem": "arr%d" % r,
-                    "n": 2 * n_in, "after": [len(ops) - 2, len(ops) - 1], "hold": 0, "len": CFG["FLIGHT"]})
-        order(7, 15)
-        ts(V("offo", 6, 14), V("osn", 127, 240, 16), 16.0, A.mult, c16, A.add)
-        third(6)
+                    "n": 2 * n_in, "after": [len(ops) - 2, len(ops) - 1], "hold": lambda u: 0, "more": lambda u: u["flight"]})
         for b in range(4):
             act(V("a2", 144 * b, 144 * b + 144), I(plane(b), V("offo", 6, 15)))
             tt(V("zt", 512 + b, 896, 4), I(plane(b), V("offm", 6, 12)), V("a2", 144 * b, 144 * b + 96), A.add)
@@ -443,17 +493,14 @@ def rank_program(g, core, T, topo):
             mm(V("psF", 512 * b, 512 * b + 128), *w_(b), V(qa, 0, 128), V(sa, 0, 128))
             tt(V("yw", 256 * b, 256 * b + 96), V("psF", 512 * b, 512 * b + 96), V("z32", b, 384, 4), A.add)
         for b in range(4):
-            src = I(V("yw", 256 * b, 256 * b + 256), V("offr"))
-            if b in (0, 2):
-                act(V("xt", b, 1024, 4), src, 0.03125)
-            else:
-                ts(V("xt", b, 1024, 4), src, 0.03125, A.mult)
-        quant(V("qx"), V("sx"), V("xt"))
-        act(V("sq", 0, 240), V("tab", 0, 240), -16.0, F.Square, C("o16", 15))
-        act(V("sq", 256, 496), V("tab", 0, 240), -16.0, F.Square, C("o16", 31))
-        scan(V("ab", 0, 256), V("sq", 0, 256), V("ones", 0, 256), A.min, A.add)
-        scan(V("ab", 256, 512), V("sq", 256, 512), V("ones", 0, 256), A.min, A.add)
-        lin(V("r2", 0, 32, 2), V("ab", 15, 256, 16), -1.0, 16.0)
+            lin(V("xt", b, 1024, 4), I(V("yw", 256 * b, 256 * b + 256), V("offr")), 0.03125, 0.0, "sv"[b % 2])
+        for a, b in ((0, 128), (128, 256)):
+            quant(V("qx", a, b), V("sx", a, b), V("xt", 4 * a, 4 * b))
+        ts(V("sq", 0, 240), V("tab"), o_(0), A.not_equal, 256.0, A.mult)
+        act(V("sq", 256, 496), V("tab"), -16.0, F.Square, C("o16", 31))
+        for a in (0, 256):
+            scan(V("ab", a, a + 256), V("sq", a, a + 256), V("ones", 0, 256), A.min, A.add)
+        lin(V("r2", 0, 32, 2), V("ab", 15, 256, 16), -1.0, 16.0, "s")
         tt(V("df", 0, 15), V("ab", 287, 512, 16), V("ab", 271, 496, 16), A.subtract)
         tt(V("nw", 17, 288, 18), V("ab", 271, 512, 16), V("ab", 15, 256, 16), A.subtract)
         tt(V("do", 0, 3), V("osn", 15, 48, 16), V("osn", 31, 64, 16), A.subtract)
@@ -476,22 +523,24 @@ def rank_program(g, core, T, topo):
         ts(V(cur, 1, 640, 5), V(cur, 4, 640, 5), -LIFT, A.add, o_(0), A.is_equal)
         ts(V(cur, 0, 640, 5), V(cur, 4, 640, 5), -LIFT, A.add, o_(1), A.is_equal)
         tt(V("ev"), V(cur, 1, 80, 5), V(cur, 0, 80, 5), A.subtract)
-        lin(V("hm", 3, 560, 5), I(V("ev"), l_y), BIG, 1.0)
-        lin(V("hm", 4, 560, 5), I(V("ev"), l_x), 1.0, 1.0 / BIG)
-        lin(C("dof", 0), C("do", 0), BIG, 0.0)
-        act(V("hm", 2, 560, 5), I(V("nc"), l_cx), C("dof", 0), F.Identity)
+        lin(V("hm", 3, 560, 5), I(V("ev"), l_y), BIG, 1.0, "s")
+        lin(V("hm", 4, 560, 5), I(V("ev"), l_x), 1.0, 1.0 / BIG, "s")
+        lin(C("dof", 0), C("do", 0), BIG, 0.0, "s")
+        lin(V("hm", 2, 560, 5), I(V("nc"), l_cx), C("dof", 0), 0.0, "s")
         act(V(cur, 82, 640, 5), I(V("nc"), l_wx))
         act(V(cur, 83, 640, 5), I(V("nc"), l_wy))
         scan(V(new, 80, 640), V("hm"), V(cur, 80, 640), A.mult, A.add)
-        lin(V("tabo" if last else "tab"), I(V(new), l_tab), 1.0, -LIFT)
+        lin(V("tabo" if last else "tab", 0, 240), I(V(new), l_tab), 1.0, -LIFT, "s")
 
     store("y", T.ot[:], T.tabo[:], [V("tabo")])
-    mm(V("psS", 0, 256), V("qv"), V("sv"), V("qx"), V("sx"))
-    act(V("yo"), V("psS", 0, 256))
+    for k, q in enumerate("sv"):
+        a = 128 * k
+        mm(V("psY", 4 * a, 4 * a + 128), V("qv"), V("sv"), V("qx", a, a + 128), V("sx", a, a + 128))
+        lin(V("yo", a, a + 128), V("psY", 4 * a, 4 * a + 128), 1.0, 0.0, q)
     store("s", T.y[:], T.yo[:], [V("yo")])
     store("y", T.oc[:], T.qx[:].bitcast(dt.uint8), [V("qx")])
     for k in range(4):
-        store("y", T.osc[4 * k:4 * k + 4, :], T.sx[32 * k:32 * k + 4, :], [V("sx")])
+        store("ys"[k % 2], T.osc[4 * k:4 * k + 4, :], T.sx[32 * k:32 * k + 4, :], [V("sx")], 0)
 
     if not ORDER:
         ORDER.extend(arrange(ops))

@@ -5,14 +5,14 @@ F = ActivationFunctionType
 ROUNDS = 3
 C4, U8, BF, F32, I32, U16 = "float8_e4m3fn_x4", "uint8", "bfloat16", "float32", "int32", "uint16"
 SB = {
-    BF: dict(xin=1024, uin=512, vin=512, et=1032, idn=128, ones=516, xt=1024, ioc=96, d0r=240, kjp=240, d1o=240,
-             mk=96, nm=96, d1s=192, gg=240, rs=240, ne=240, osn=240, o16=192, ix=12, lk=192, ms=192,
+    BF: dict(xin=1024, uin=512, vin=512, et=1032, ones=516, xt=1024, ioc=96, d0r=240, kjp=240, d1o=240,
+             mk=96, nm=96, gg=240, rs=256, ne=240, osn=240, o16=2, lk=192, ms=192,
              fh=1024, a1=384, a2=576, zt=896, z32=896, yw=1024, tab=240, sq=512, ab=512, df=16, t2=2, rk=16,
              nw=288, md=288, nc=288, do=4, wk=80, r2=32, ev=16, hm=560, pa=640, pb=640),
-    F32: dict(pc=16, iop=18, w1=32, w3=32, w4=64, w5=32, lf=18, tf=64, tt=512, ap=240, rv=32, rvt=32,
-              tabo=256, dof=2, yo=256),
-    I32: dict(trii=256, pi=4, w2=32),
-    U16: dict(lu=68, tu=64, ixu=12, offo=16, offm=12, offr=16),
+    F32: dict(pc=16, iop=18, w1=32, w3=32, w4=64, w5=64, w6=64, w8=32, lf=18, tf=64, tt=512, ap=240, rv=32, rvt=32,
+              tabo=256, ix=208, kw=112, ka=16, kb=16, kc=16, dof=2, yo=256),
+    I32: dict(trii=256, pi=4, w2=32, w7=32),
+    U16: dict(lu=76, tu=64, ixu=12, offo=16, offm=12, offr=16),
     C4: dict(wq=512, qu=128, qv=128, qe=512, qn=256, qp=272, qx=256, qs0=128, qs1=128, qs2=128, qa0=224, qa1=224, qa2=224),
     U8: dict(wsc=512, su=128, sv=128, se=512, sn=256, sp=272, sx=256, ss0=128, ss1=128, ss2=128, sa0=224, sa1=224, sa2=224),
 }
@@ -22,10 +22,46 @@ SEMAPHORES = ["cv", "cs", "ct", "cg", "sent"] + ["arr%d" % r for r in range(ROUN
 COUNTER = {"v": "cv", "s": "cs", "t": "ct", "g": "cg"}
 BIG = 1024.0
 LIFT = 128.0
-GUESS = [dict(same=255, other=250, flight=1000, first=2000, fixed=0, least=64, act=80, gather=130),
-         dict(same=215, other=260, flight=1400, first=1500, fixed=25, least=40, act=90, gather=110)]
-CFG = dict(LOCAL=1100, DMA=200, ISSUE=240, SWEEPS=2, REACH=4,
-           PASSES=[(240, 30), (240, 30), (220, 60), (260, 0), (260, 40)])
+FULL = (16 * 105 + 4 * 15 + 244 / 16) * 16 / 15
+
+SPAN, BEGIN, LATE = 8.72, 2.53, 1.3
+ROUND = """
+scores, F, ranks:    .32 psY0 .55 psS0 .65 psF0 .8 psF512 .95 psF1024 1.1 psF1536 .61 tt96 .72 tt0 .85 tt224 .96 tt352
+                     1.0 ap0 1.29 ap96 1.54 gg0 1.74 gg96 2.0 rs0 2.2 rs96 1.53 fh0 1.81 fh256 2.09 fh512 2.37 fh768
+order, third points: 2.46 ne0 2.67 ne112 2.9 ix0 2.99 osn0 3.04 rk0 3.1 osn112 3.19 ixu0 3.24 offo0 3.29 ix112
+                     3.37 offo6 3.44 lk0 3.63 ixu6 3.83 ms0 3.88 lk96 4.08 offm0 4.24 ms96 5.08 offm6
+slots that travel:   3.6 a10 3.8 a196 4.0 a1192 4.2 a1288 4.33 zt0 4.52 zt1 4.7 zt2 4.89 zt3 5.28 qs0
+                     5.6 >qs0 5.8 >ss0 6.0 landed 5.6 z320
+slots that stay:     4.5 a20 4.77 a2144 5.04 a2288 5.31 a2432 5.4 zt512 5.64 zt513 5.88 zt514 6.07 zt515 6.4 qa96
+                     5.98 yw192 6.1 yw448 6.22 yw704 6.83 yw960 6.45 z32512 6.65 offr1 6.66 rv0 6.67 rv16 6.9 rvt0
+                     7.42 offr0 6.7 psS0' 6.79 psY0' 6.88 psY512 6.97 psY1024 7.07 yw96 7.15 yw352 7.23 yw608 7.31 yw864
+new state:           7.2 psF0' 7.29 psF512' 7.38 psF1024' 7.47 psF1536' 7.5 yw0 7.58 yw256 7.66 yw512 7.74 yw768
+                     7.78 xt0 7.82 xt1 8.21 xt2 8.23 xt3 8.46 xt514 8.46 xt515 8.72 qx0 8.96 qx128
+rows, cycle:         3.3 o160 3.4 sq256 3.68 do0 3.73 sq0 4.13 ab0 4.29 t20 4.45 r20 5.12 ab256 5.22 nw1 5.59 df0
+                     5.83 wk16 5.85 wk0 6.26 nw3 6.3 nw2 6.35 nw17 6.55 wk48 6.6 wk32 6.8 nw5 6.85 nw4 7.05 wk64
+                     7.39 nw6 8.84 nc0
+new table:           6.34 dof0 6.7 pt0 6.95 pt1 7.44 ev0 8.75 hm3 8.97 hm4 9.2 hm2 9.42 pt82 9.95 pt83 10.98 pt80
+                     11.4 tab0
+"""
+CHANGED = {0: "7.45 pt0 7.45 pt1 7.7 nc0 7.8 ev0 7.9 hm2 8.0 hm3 8.2 hm4 8.3 pt82 10.05 pt83",
+           ROUNDS - 1: """5.1 pt0 6.0 pt1 6.62 ev0 6.96 hm3 7.2 hm4 7.8 nc0 8.45 hm2 8.7 pt82 8.75 pt83 9.1 pt80
+                          9.5 tabo0 9.5 tabo128"""}
+START = """
+loads:    -9 <xin0 -8 <uin0 1.7 <trii0 1.8 <wq0 1.9 <wsc0 2.0 <vin0
+GpSimd:   0 pi0 .13 iop0 .41 et0 1.44 lf0 1.64 d0r0 2.21 kjp0 2.74 d0r0' 2.9 rs240 3.06 ioc0 3.35 nm0 3.68 zt384
+          4.0 sq240 4.2 sq496 4.4 w432 4.6 r21 4.8 pt0 5.1 md0 5.7 nw0 6.3 md16 6.5 pt0' 6.8 tabo240
+Vector:   0 ones0 .33 pi1 .38 pi2 .44 pi3 .49 ka0 .55 kc0 .63 pc0 .74 kb0 1.01 w10 1.06 w116 1.12 pc4 1.17 lu68
+          1.22 kc1 1.32 w20 1.37 w60 1.42 lu50 1.47 offo14 1.57 w70 1.62 w632 1.67 lu66 1.72 qn0 1.96 lu0 2.01 w30
+          2.06 qe0 2.2 qp0 2.43 w80 2.48 qu0 2.6 qp128 2.85 lu18 2.9 qe256 3.02 qe128 3.63 qe384 4.6 mk0 4.65 pc7
+          4.66 w48 4.8 tab0 5.7 w50 8.0 tf8 8.05 w516 8.7 w448 8.9 pc10 8.95 offr0 9.0 w448' 9.25 tf48 9.45 tu0
+          9.7 pt4 9.9 qv0
+Scalar:   .41 et516 .5 d1o0 .9 pc3 .97 d1o15 1.05 pc6 1.12 pc9 1.19 pc8 1.26 w416 1.33 tf0 1.4 tf40 1.47 w40 1.54 tf16
+          1.64 et517 2.2 sp0 2.45 sp128 2.72 kw0 2.95 hm0 3.11 hm1 3.3 rv15 8.1 w532 8.15 tf24 8.2 tf41 8.45 w548
+"""
+END = "9.12 <qx0 9.17 <sx1 9.22 <sx0 9.32 <sx2 9.37 <sx3 9.32 psY0 9.52 psY512 9.62 yo0 9.82 yo128 10.0 <yo0 10.3 <tabo0"
+GUESS = [dict(same=240, other=240, late=105, flight=960, first=1800, act=80, gather=80, rate=1.7),
+         dict(same=255, other=260, late=0, flight=650, first=1600, act=80, gather=112, rate=1.58)]
+LOCAL, DMA, ISSUE, SWEEPS, REACH = 900, 230, 240, 4, 5
 ORDER = []
 
 
@@ -81,6 +117,28 @@ def depends(ops):
     return deps
 
 
+def planned(ops):
+    def read(text):
+        words = " ".join(line.split(":")[-1] for line in text.split("\n")).split()
+        return {name: float(t) for t, name in zip(words[0::2], words[1::2])}
+
+    out, seen = [], set()
+    for op in ops:
+        r, name = op["round"], op["name"]
+        if (r, name) in seen:
+            name += "'"
+        seen.add((r, name))
+        if r < 0:
+            out.append(read(START)[name])
+            continue
+        k = min(r, ROUNDS - 1)
+        own = read(END if r == ROUNDS else CHANGED.get(r, ""))
+        t = own[name] if name in own else read(ROUND)[name]
+        waits = k > 0 or (name not in own and t >= read(ROUND)["psF0'"])
+        out.append(BEGIN + k * SPAN + t + (LATE if waits else 0))
+    return out
+
+
 def arrange(ops):
     deps = depends(ops)
     for i, op in enumerate(ops):
@@ -90,89 +148,52 @@ def arrange(ops):
         implied = set().union(*[above[j] for j in d])
         above.append(implied | d)
         d -= implied
-    succ = [[] for _ in ops]
-    for i in range(n):
-        for j in deps[i]:
-            succ[j].append(i)
-    holds = [[op["hold"](u) for op in ops] for u in GUESS]
-    spans = [[op["hold"](u) + op["more"](u) for op in ops] for u in GUESS]
-    hold_, span_ = [[sum(x) / len(x) for x in zip(*y)] for y in (holds, spans)]
-    behind = [0.0] * n
-    for i in reversed(range(n)):
-        behind[i] = span_[i] + max([CFG["PASSES"][0][0] + behind[k] for k in succ[i]] + [0])
-
-    def lay(before, after, key, backwards, wait, slack):
-        left = [len(b) for b in before]
-        ready = [i for i in range(n) if not left[i]]
-        start, done, busy = [0.0] * n, [0.0] * n, {}
-        while ready:
-            i = min(ready, key=lambda k: (key[k], k))
-            ready.remove(i)
-            hold = hold_[i]
-            lead = span_[i] - hold if backwards else 0
-            t = max([0] + [done[j] + wait for j in before[i]]) + lead
-            taken = busy.setdefault(ops[i]["q"], [])
-            for a, b in taken:
-                if b > t:
-                    if t < a and t + hold <= a + slack:
-                        break
-                    t = b
-            taken.append((t, t + hold))
-            taken.sort()
-            start[i], done[i] = t - lead, t - lead + span_[i]
-            for k in after[i]:
-                left[k] -= 1
-                if not left[k]:
-                    ready.append(k)
-        return start, done
-
-    def ends(order, k):
-        same, other, hold, span = GUESS[k]["same"], GUESS[k]["other"], holds[k], spans[k]
-        free, done = {}, [0.0] * n
-        for i in order:
-            q = queue[i]
-            t = free.get(q, 0.0)
-            for j in deps[i]:
-                e = done[j] + (same if queue[j] == q else other)
-                if e > t:
-                    t = e
-            free[q] = t + hold[i]
-            done[i] = t + span[i]
-        return done
+    succ = [[k for k in range(i + 1, n) if i in deps[k]] for i in range(n)]
+    key, left, order = planned(ops), [len(d) for d in deps], []
+    ready = [i for i in range(n) if not left[i]]
+    while ready:
+        i = min(ready, key=lambda k: (key[k], k))
+        ready.remove(i)
+        order.append(i)
+        for k in succ[i]:
+            left[k] -= 1
+            if not left[k]:
+                ready.append(k)
+    guesses = [([op["hold"](u) for op in ops], [op["hold"](u) + op["more"](u) for op in ops],
+                [[(j, u["same"] if queue[j] == queue[i] else u["other"]) for j in deps[i]] for i in range(n)])
+               for u in GUESS]
 
     def length(order):
-        return sum(max(done) + sum(done) / n for done in (ends(order, k) for k in range(len(GUESS))))
+        total = 0
+        for hold, span, waits in guesses:
+            free, done = {}, [0.0] * n
+            for i in order:
+                t = free.get(queue[i], 0.0)
+                for j, w in waits[i]:
+                    if done[j] + w > t:
+                        t = done[j] + w
+                free[queue[i]] = t + hold[i]
+                done[i] = t + span[i]
+            total += max(done) + 0.3 * sum(done) / n
+        return total
 
-    def polish(order):
-        now = length(order)
-        for _ in range(CFG["SWEEPS"]):
-            for i in range(n):
-                p, better = order.index(i), None
-                for step, stop in ((-1, deps[i]), (1, succ[i])):
-                    k, passed = p, 0
-                    while passed < CFG["REACH"] and 0 <= k + step < n and order[k + step] not in stop:
-                        k += step
-                        if queue[order[k]] == queue[i]:
-                            passed += 1
-                            moved = order[:p] + order[p + 1:]
-                            moved.insert(k, i)
-                            t = length(moved)
-                            if t < now - 1e-6:
-                                now, better = t, moved
-                order = better or order
-        return order
-
-    best, key = None, [-b for b in behind]
-    for wait, slack in CFG["PASSES"]:
-        if best:
-            done = [a + b for a, b in zip(ends(best[1], 0), ends(best[1], 1))]
-            key = [-d for d in lay(succ, deps, [-d for d in done], True, wait, slack)[1]]
-        start = lay(deps, succ, key, False, wait, slack)[0]
-        order = polish(sorted(range(n), key=lambda i: (start[i], i)))
-        end = sum(max(ends(order, k)) for k in range(len(GUESS)))
-        if best is None or end < best[0]:
-            best = (end, order)
-    return best[1]
+    now = length(order)
+    for _ in range(SWEEPS):
+        for i in range(n):
+            p, better = order.index(i), None
+            for step, stop in ((-1, deps[i]), (1, succ[i])):
+                k, passed = p, 0
+                while passed < REACH and 0 <= k + step < n and order[k + step] not in stop:
+                    k += step
+                    if queue[order[k]] == queue[i]:
+                        passed += 1
+                        moved = order[:p] + order[p + 1:]
+                        moved.insert(k, i)
+                        t = length(moved)
+                        if t < now - 1e-6:
+                            now, better = t, moved
+            order = better or order
+    return order
 
 
 def issue(ops, g, T):
@@ -235,7 +256,7 @@ def rank_program(g, core, T, topo):
     rid, pid, _ = topo.addr(nxt)
     mask = topo.mask(core, nxt)
     n_out, n_in = len(topo.engines(core, nxt)), len(topo.engines(prv, core))
-    ops = []
+    ops, now = [], [-1]
 
     def ap(x, word=None):
         if not is_view(x):
@@ -253,17 +274,21 @@ def rank_program(g, core, T, topo):
                 out += [x[1], x[2]] if x[0] == "@" else [x]
         return out
 
-    def rec(q, f, r, w, kind="compute", hold=None, more=0, slow=1, first=False):
+    def rec(q, f, r, w, kind="compute", hold=None, more=0, slow=1, first=False, name=None):
         def cycles(u):
             if hold is not None:
                 return hold + (u["first"] if first else 0)
             if r and r[0][0] == "@":
-                return (60 if q == "v" else u["gather"]) + 1.6 * size(r[0])
+                return (60 if q == "v" else u["gather"]) + u["rate"] * size(r[0])
             if q == "s":
                 return u["act"] + size(w[0])
             narrow = all(SCRATCH[x[0]][2] in (BF, U16) for x in flat([r[0], w[0]] if r else w))
-            return u["fixed"] + max(u["least"], size(w[0]) * (0.5 if narrow else 1) * slow)
-        ops.append({"q": q, "f": f, "r": flat(r), "w": flat(w), "kind": kind, "hold": cycles, "more": lambda u: more})
+            return max(64, size(w[0]) * (0.5 if narrow else 1) * slow)
+        buf, col = (w or r)[0][:2]
+        buf = {"pa": "pt", "pb": "pt"}.get(buf, buf[:2] if buf[:2] in ("qs", "ss", "qa") and now[0] >= 0 else buf)
+        ops.append({"q": q, "f": f, "r": flat(r), "w": flat(w), "kind": kind, "round": now[0], "hold": cycles,
+                    "more": lambda u: more + (u["late"] if q == "s" and kind == "compute" else 0),
+                    "name": name or {"dma": "<", "remote": ">"}.get(kind, "") + buf + str(col)})
 
     def cp(o, i, word=None):
         rec("v", lambda q: q.tensor_copy(ap(o, word), ap(i, word)), [i], [o])
@@ -277,8 +302,8 @@ def rank_program(g, core, T, topo):
         else:
             rec("v", lambda q: q.tensor_scalar(ap(o), ap(a), ap(s1), ap(s2), op0, op1), [a, s1, s2], [o])
 
-    def scan(o, d0, d1, op0, op1):
-        rec("v", lambda q: q.tensor_tensor_scan(ap(o), ap(d0), ap(d1), 0.0, op0, op1), [d0, d1], [o])
+    def scan(o, d0, d1, op0, op1, first=0.0):
+        rec("v", lambda q: q.tensor_tensor_scan(ap(o), ap(d0), ap(d1), ap(first), op0, op1), [d0, d1, first], [o])
 
     def mset(o, c):
         rec("v", lambda q: q.memset(ap(o), c), [], [o])
@@ -307,52 +332,51 @@ def rank_program(g, core, T, topo):
         rec("t", lambda q: q.matmul_mx(ap(o), ap(lq), ap(ls), ap(rq), ap(rsc), True, True), [lq, ls, rq, rsc], [o],
             hold=0.7 * (size(o) + 16))
 
-    def iota(o, pattern, base, cm, small=True):
+    def iota(o, pattern, base, cm=0, small=True):
         kw = {"allow_small_or_imprecise_dtypes": True} if small else {}
         rec("g", lambda q: q.iota(ap(o), pattern, base, cm, **kw), [], [o], hold=160 + 2 * size(o))
 
     def select(o, i, pattern, op, fill, base=0, cm=0):
         rec("g", lambda q: q.affine_select(ap(o), ap(i), pattern, op, fill, base, cm), [i], [o], hold=200 + 2 * size(o))
 
-    def load(q, o, src, word=None, after=(), more=500):
-        rec(q, lambda e: e.dma_start(ap(o, word), src), list(after), [o], "dma", CFG["DMA"], CFG["LOCAL"] + more)
+    def load(o, src, word=None, after=(), more=500):
+        rec("y", lambda e: e.dma_start(ap(o, word), src), list(after), [o], "dma", DMA, LOCAL + more)
 
-    def store(q, dst, src, reads, more=400):
-        rec(q, lambda e: e.dma_start(dst, src), reads, [], "dma", CFG["DMA"], CFG["LOCAL"] + more)
+    def store(q, dst, src, reads, more=400, name=None):
+        rec(q, lambda e: e.dma_start(dst, src), reads, [], "dma", DMA, LOCAL + more, name=name)
 
     def send(dst, src, sem, word=None, first=False):
         rec("g", lambda q: q.remote_dma(ap(dst, word), ap(src, word), T.sem[sem], T.sem.sent, pid, rid, mask),
-            [src], [], "remote", CFG["ISSUE"], first=first)
+            [src], [], "remote", ISSUE, first=first)
 
-    load("y", V("xin"), T.x[:], more=600)
-    load("y", V("uin"), T.u[:], more=1100)
-    load("y", V("trii"), T.tri[:], None, [C("xin", 0)])
-    load("y", V("wq"), T.wc[:], dt.uint8, [C("xin", 0)])
-    load("y", V("wsc"), T.ws[:], None, [C("xin", 0)])
-    load("y", V("vin"), T.v[:], None, [C("xin", 0)])
+    load(V("xin"), T.x[:], more=600)
+    load(V("uin"), T.u[:], more=1100)
+    load(V("trii"), T.tri[:], None, [C("xin", 0)])
+    load(V("wq"), T.wc[:], dt.uint8, [C("xin", 0)])
+    load(V("wsc"), T.ws[:], None, [C("xin", 0)])
+    load(V("vin"), T.v[:], None, [C("xin", 0)])
 
     q_, h_, p32, c16, c16q = C("pc", 0), C("pc", 1), C("pc", 2), C("pc", 3), C("pc", 4)
     iota(C("pi", 0), [[0, 1]], 0, 1, False)
-    iota(V("iop"), [[1, 18]], 0, 0)
+    iota(V("iop"), [[1, 18]], 0)
     mset(V("ones"), 1.0)
-    select(V("idn"), V("ones", 0, 128), [[-1, 128]], A.is_equal, 0.0, 0, 1)
-    iota(V("ioc"), [[0, 6], [1, 16]], 0, 0)
+    iota(V("ioc"), [[0, 6], [1, 16]], 0)
     select(V("d0r"), V("ones", 0, 240), [[1, 15], [-1, 16]], A.not_equal, -1.0)
-    iota(V("kjp"), [[1, 15], [-1, 16]], 0, 0)
-    iota(V("d0r", 0, 240, 16), [[0, 15]], 0, 0)
-    iota(V("kjp", 15, 240, 16), [[0, 15]], 99, 0)
+    iota(V("kjp"), [[1, 15], [-1, 16]], 0)
+    iota(V("d0r", 0, 240, 16), [[0, 15]], 0)
+    iota(V("rs", 240, 256), [[0, 16]], 99)
     select(V("nm"), V("ones", 0, 96), [[0, 6], [1, 16]], A.is_gt, 0.0)
-    iota(V("sq", 240, 256), [[256, 16]], 0, 0)
-    iota(V("sq", 496, 512), [[256, 16]], 0, 0)
-    iota(V("zt", 384, 512), [[0, 128]], 0, 0)
-    iota(V("r2", 1, 32, 2), [[1, 16]], 0, 0)
+    iota(V("sq", 240, 256), [[256, 16]], 0)
+    iota(V("sq", 496, 512), [[256, 16]], 0)
+    iota(V("zt", 384, 512), [[0, 128]], 0)
+    iota(V("r2", 1, 32, 2), [[1, 16]], 0)
     for p in ("pa", "pb"):
-        iota(V(p, 0, 80), [[1, 16], [0, 5]], int(LIFT), 0)
+        iota(V(p, 0, 80), [[1, 16], [0, 5]], int(LIFT))
     select(V("md"), V("ones", 0, 288), [[0, 16], [1, 18]], A.is_equal, 0.0)
-    iota(V("md", 16, 288, 18), [[0, 16]], -1, 0)
+    iota(V("md", 16, 288, 18), [[0, 16]], -1)
     select(V("nw"), V("ones", 0, 288), [[0, 16], [1, 18]], A.not_equal, 0.0)
-    iota(V("tabo", 240, 256), [[1, 16]], 0, 0)
-    iota(V("w4", 32, 48), [[5, 16]], 4, 0)
+    iota(V("tabo", 240, 256), [[1, 16]], 0)
+    iota(V("w4", 32, 48), [[5, 16]], 4)
     select(V("lf"), V("iop"), [[1, 18]], A.is_gt, 16.0)
     ts(C("pi", 1), C("pi", 0), 15, A.bitwise_and)
     ts(C("pi", 2), C("pi", 0), 4, A.arith_shift_right, 1, A.bitwise_and)
@@ -360,27 +384,30 @@ def rank_program(g, core, T, topo):
     cp(V("pc", 0, 3), V("pi", 1, 4))
     ts(c16q, q_, 16.0, A.mult)
     lin(c16, q_, 1.0, 16.0, "s")
-    ts(V("lu", 0, 16), V("lf", 0, 16), c16q, A.add, -1.0, A.add)
-    mset(V("lu", 16, 18), 0)
-    ts(V("w1", 0, 16), V("iop", 0, 16), q_, A.max, 1.0, A.add)
-    ts(V("w1", 16, 32), V("iop", 0, 16), q_, A.min, 1.0, A.add)
+    ts(V("lu", 0, 18), V("lf"), c16q, A.add, -1.0, A.add)
+    ts(V("w1", 0, 16), V("iop", 0, 16), q_, A.min, 1.0, A.add)
+    ts(V("w1", 16, 32), V("iop", 0, 16), q_, A.max, 1.0, A.add)
     ts(V("w2"), V("w1"), h_, A.add)
-    ts(V("w2"), V("w2"), 1, A.bitwise_and)
-    ts(V("w3"), V("w2"), 15.0, A.mult)
-    tt(V("w3"), V("w3"), V("w1"), A.add)
-    ts(V("lu", 18, 50), V("w3"), 16.0, A.mult)
-    ts(C("pc", 5), c16q, 14.0, A.add, 238.0, A.min)
-    ts(V("lu", 50, 66), V("iop", 0, 16), 0.0, A.mult, C("pc", 5), A.add)
+    ts(V("w6", 0, 32), V("w1"), h_, A.subtract, 7.0, A.is_ge)
+    ts(V("w7"), V("w2"), 1, A.bitwise_and)
+    lin(V("w6", 32, 64), V("w6", 0, 32), 16.0, -7.0)
+    tt(V("w3"), V("w6", 32, 64), V("w7"), A.mult)
+    tt(V("w8"), V("w3"), V("w1"), A.add)
+    lin(V("lu", 18, 50), V("w8"), 16.0, 96.0)
+    ts(V("lu", 68, 76), V("iop", 0, 8), 0.0, A.mult, q_, A.add)
+    lin(V("lu", 50, 58), V("lu", 68, 76), 16.0, 14.0)
     cp(C("lu", 66), p32)
-    l_pick, l_b, l_n, l_32 = V("lu", 0, 17), V("lu", 34, 49), V("lu", 50, 65), V("lu", 66, 67)
     act(V("d1o"), V("ones", 0, 240), -1.0)
     act(V("d1o", 15, 240, 16), V("ones", 0, 15), 15.0)
-    act(V("d1s"), V("d1o", 0, 192), 16.0)
+    lin(V("ka"), V("iop", 0, 16), 4.0, 1.0)
+    rec("v", lambda q: q.reciprocal(ap(V("kb")), ap(V("ka"))), [V("ka")], [V("kb")], hold=330)
+    lin(V("kc", 1, 16), V("kb", 1, 16), -4.0, 1.0)
+    mset(C("kc", 0), 61.0 / 16)
+    act(V("kw"), I(V("kc"), V("lu", 68, 75)))
     ts(V("mk"), V("ioc"), q_, A.is_equal)
-    act(V("et", 0, 516), V("ones", 0, 516), 0.0)
-    act(V("et", 516, 1032), V("ones", 0, 516), 0.0)
-    act(V("et", 2, 514, 4), V("idn"))
-    act(V("et", 519, 1031, 4), V("idn"))
+    select(V("et", 0, 516), V("ones"), [[1, 516]], A.is_equal, 0.0, -2, -4)
+    act(V("et", 517, 1032), V("et", 0, 515))
+    act(V("et", 516, 517), V("ones", 0, 1), 0.0)
     for b in range(4):
         o = 516 * (b % 2) + (2 if b < 2 else 0)
         quant(V("qe", 128 * b, 128 * b + 128), V("se", 128 * b, 128 * b + 128), V("et", o, o + 512))
@@ -394,18 +421,20 @@ def rank_program(g, core, T, topo):
     lin(V("tf", 0, 8), V("iop", 0, 8), 0.0, q_, "s")
     lin(V("tf", 16, 24), V("tf", 0, 8), 18.0, 16.0, "s")
     lin(V("tf", 24, 40), V("tf", 0, 16), 18.0, 17.0, "s")
-    lin(V("tf", 40, 48), V("tf", 8, 16), 1.0, c16q, "s")
+    lin(V("tf", 41, 48), V("tf", 8, 15), 1.0, c16q, "s")
+    lin(C("tf", 40), q_, 16.0, 15.0, "s")
     lin(V("w4", 16, 32), V("iop", 0, 16), -1.0, q_, "s")
     ts(V("w5", 0, 16), V("w4", 16, 32), 0.0, A.is_lt, 15.0, A.mult)
-    tt(V("w5", 0, 16), V("w5", 0, 16), V("w4", 16, 32), A.add)
-    lin(V("w5", 0, 16), V("w5", 0, 16), C("pc", 7), 0.0, "s")
-    lin(V("w5", 16, 32), V("w5", 0, 16), -1.0, C("pc", 8), "s")
-    tt(V("w4", 48, 64), V("w5", 0, 16), V("w4", 32, 48), A.add)
-    tt(V("w4", 48, 64), V("w4", 48, 64), V("w5", 16, 32), A.min)
+    tt(V("w5", 16, 32), V("w5", 0, 16), V("w4", 16, 32), A.add)
+    lin(V("w5", 32, 48), V("w5", 16, 32), C("pc", 7), 0.0, "s")
+    lin(V("w5", 48, 64), V("w5", 32, 48), -1.0, C("pc", 8), "s")
+    tt(V("w4", 48, 64), V("w5", 32, 48), V("w4", 32, 48), A.add)
+    tt(V("w4", 48, 64), V("w4", 48, 64), V("w5", 48, 64), A.min)
     ts(C("pc", 10), q_, 15.0, A.not_equal, 79.0, A.mult)
     ts(V("tf", 48, 64), V("w4", 48, 64), C("pc", 10), A.max)
     cp(V("tu"), V("tf"))
-    l_x, l_y, l_cx, l_wx, l_wy, l_xy, l_tab = [V("tu", 8 * k, 8 * k + 7) for k in range(6)] + [V("tu", 48, 63)]
+    l_x, l_y, l_cx, l_wx, l_wy = [V("tu", 8 * k, 8 * k + 7) for k in range(5)]
+    l_xy = V("tu", 40, 48)
     act(V("hm", 0, 560, 5), V("ones", 0, 112), 0.0)
     act(V("hm", 1, 560, 5), V("ones", 0, 112), -1.0)
     lin(V("rv", 15, 32, 16), V("iop", 0, 2), 0.0, C("pc", 9), "s")
@@ -413,53 +442,60 @@ def rank_program(g, core, T, topo):
     cp(C("offr", 0), C("pc", 9))
 
     quant(V("qn"), V("sn"), V("xin"))
-    cp(V("qp"), I(V("qn"), l_pick), dt.uint32)
-    act(V("sp"), I(V("sn"), l_pick))
+    for a, b in ((0, 8), (8, 17)):
+        cp(V("qp", 16 * a, 16 * b), I(V("qn"), V("lu", a, b)), dt.uint32)
+        act(V("sp", 16 * a, 16 * b), I(V("sn"), V("lu", a, b)))
     quant(V("qu"), V("su"), V("uin"))
     quant(V("qv"), V("sv"), V("vin"))
-    ts(V("pa", 84, 640, 5), I(V("trii"), l_xy), LIFT, A.add)
+    ts(V("pa", 4, 640, 5), I(V("trii"), l_xy), LIFT, A.add)
     cp(V("tab"), V("trii", 0, 240))
 
     def o_(j):
         return C("osn", 16 * j + 15)
 
+    def plane(b):
+        return V("fh", 256 * b, 256 * b + 256)
+
+    def w_(b):
+        return V("wq", 128 * b, 128 * b + 128), V("wsc", 128 * b, 128 * b + 128)
+
+    def mark(i, k):
+        ts(V("nw", 1 + i, 288, 9), V("r2"), k, A.not_equal)
+
+    def hop(s, i, e):
+        scan(V("wk", 16 * s, 16 * s + 15), V("nw", 1 + i + 9 * e, 270, 18), V("df", 0, 15), A.mult, A.add)
+        return C("wk", 16 * s + 14)
+
     ybank = [("psS", 0), ("psY", 0), ("psY", 512), ("psY", 1024)]
 
     for r in range(ROUNDS):
         last = r == ROUNDS - 1
+        now[0] = r
         qs, ss, qa, sa = "qs%d" % r, "ss%d" % r, "qa%d" % r, "sa%d" % r
         qx, sx, ns = ("qp", "sp", 272) if r == 0 else ("qx", "sx", 256)
         cur, new = ("pb", "pa") if r % 2 else ("pa", "pb")
-
-        def plane(b):
-            return V("fh", 256 * b, 256 * b + 256)
-
-        def w_(b):
-            return V("wq", 128 * b, 128 * b + 128), V("wsc", 128 * b, 128 * b + 128)
-
-        for name, a, b in (("psS", 0, 272),) if r == 0 else (("psY", 0, 128), ("psS", 112, 256)):
+        for name, a, b in (("psY", 0, 128), ("psS", 112, ns)):
             mm(V(name, 0, b - a), V("qu"), V("su"), V(qx, a, b), V(sx, a, b))
         for b in range(4):
             mm(V("psF", 512 * b, 512 * b + 256), V("qe", 128 * b, 128 * b + 128), V("se", 128 * b, 128 * b + 128),
                V(qx, 0, 256), V(sx, 0, 256))
             act(plane(b), V("psF", 512 * b, 512 * b + 256), 0.5)
-        for o, name, a, b in (((0, "psS", 0, 256), (256, "psS", 16, 272)) if r == 0 else
-                              ((0, "psY", 0, 128), (256, "psY", 16, 112), (128, "psS", 16, 144), (352, "psS", 0, 160))):
+        for o, name, a, b in ((96, "psY", 0, 128), (0, "psY", 16, 112), (224, "psS", 16, 144), (352, "psS", 0, 160)):
             tr(V("tt", o, o + b - a), V(name, a, b))
-        cp(V("ap", 0, 128), I(V("tt"), V("lu", 18, 26)))
-        act(V("ap", 128, 240), I(V("tt"), V("lu", 26, 33)))
-        for a, b in ((0, 8), (8, 15)):
-            tt(V("gg", 16 * a, 16 * b), I(V("tt"), V("lu", 34 + a, 34 + b)), V("ap", 16 * a, 16 * b), A.is_lt)
+        act(V("ap", 0, 96), I(V("tt", 0, 224), V("lu", 18, 24)))
+        cp(V("ap", 96, 240), I(V("tt"), V("lu", 24, 33)))
+        for a, b in ((0, 6), (6, 15)):
+            tt(V("gg", 16 * a, 16 * b), I(V("tt"), V("lu", 34 + a, 34 + b)), V("ap", 16 * a, 16 * b), A.is_gt)
             scan(V("rs", 16 * a, 16 * b), V("d0r", 16 * a, 16 * b), V("gg", 16 * a, 16 * b), A.mult, A.add)
         for j0, j1, j in ((0, 7, 0), (7, 15, 6)):
             a, b, e = 16 * j0, 16 * j1, 16 * j
             tt(V("ne", a, b), I(V("rs"), V("lu", 50, 50 + j1 - j0)), V("kjp", a, b), A.not_equal)
-            scan(V("o16", a, min(b, 192)), V("ne", a, min(b, 192)), V("d1s", a, min(b, 192)), A.mult, A.add)
+            scan(V("ix", a, min(b, 208)), V("kw", 0, min(b, 208) - a), V("ne", a, min(b, 208)), A.mult, A.add,
+                 C("ix", a - 1) if a else FULL / 244 + 1)
             scan(V("osn", a, b), V("ne", a, b), V("d1o", a, b), A.mult, A.add)
             ts(V("offo", j, j1 - 1), V("osn", e + 31, b, 16), 16.0, A.mult, c16, A.add)
-            tt(V("ix", j, j + 6), V("o16", e + 15, e + 96, 16), V("osn", e + 31, e + 112, 16), A.add)
-            cp(V("ixu", j, j + 6), V("ix", j, j + 6))
-            tt(V("lk", e, e + 96), I(V("tab"), V("ixu", j, j + 6)), V("mk"), A.mult)
+            lin(V("ixu", j, j + 6), V("ix", e + 30, e + 112, 16), -228.0, FULL - 4.72)
+            tt(V("lk", e, e + 96), I(V("tab" if r else "trii"), V("ixu", j, j + 6)), V("mk"), A.mult)
             scan(V("ms", e, e + 96), V("nm"), V("lk", e, e + 96), A.mult, A.add)
             ts(V("offm", j, j + 6), V("ms", e + 15, e + 96, 16), 16.0, A.mult, c16, A.add)
         for b in range(4):
@@ -469,20 +505,21 @@ def rank_program(g, core, T, topo):
         send(V(qa, 0, 96), V(qs, 0, 96), "arr%d" % r, dt.uint8, r == 0)
         send(V(sa, 0, 96), V(ss, 0, 96), "arr%d" % r)
         ops.append({"kind": "arrive", "q": "a", "r": [], "w": [V(qa, 0, 96), V(sa, 0, 96)], "sem": "arr%d" % r,
-                    "n": 2 * n_in, "after": [len(ops) - 2, len(ops) - 1], "hold": lambda u: 0, "more": lambda u: u["flight"]})
+                    "n": 2 * n_in, "after": [len(ops) - 2, len(ops) - 1], "round": r, "name": "landed",
+                    "hold": lambda u: 0, "more": lambda u: u["flight"]})
         for b in range(4):
             act(V("a2", 144 * b, 144 * b + 144), I(plane(b), V("offo", 6, 15)))
             tt(V("zt", 512 + b, 896, 4), I(plane(b), V("offm", 6, 12)), V("a2", 144 * b, 144 * b + 96), A.add)
             act(V("yw", 256 * b + 192, 256 * b + 256), V("a2", 144 * b + 80, 144 * b + 144), 64.0)
         quant(V(qa, 96, 224), V(sa, 96, 224), V("zt", 384, 896))
         act(V("z32", 0, 384), V("zt", 0, 384), 32.0)
-        ts(V("z32", 512, 896), V("zt", 512, 896), 32.0, A.mult)
+        act(V("z32", 512, 896), V("zt", 512, 896), 32.0)
         tt(V("rk", 0, 15), V("rs", 14, 240, 16), V("iop", 0, 15), A.add)
         if last:
             ts(V("rv", 0, 15), V("rk", 0, 15), 16.0, A.mult, q_, A.add)
             ts(V("rv", 16, 31), V("rk", 0, 15), 16.0, A.mult, q_, A.add)
             tr(V("rvt"), V("rv"))
-            cp(V("offr"), I(V("rvt"), l_32))
+            cp(V("offr"), I(V("rvt"), V("lu", 66, 67)))
         else:
             ts(V("offr", 1, 16), V("rk", 0, 15), 16.0, A.mult, q_, A.add)
         for b in range(4):
@@ -493,11 +530,14 @@ def rank_program(g, core, T, topo):
             mm(V("psF", 512 * b, 512 * b + 128), *w_(b), V(qa, 0, 128), V(sa, 0, 128))
             tt(V("yw", 256 * b, 256 * b + 96), V("psF", 512 * b, 512 * b + 96), V("z32", b, 384, 4), A.add)
         for b in range(4):
-            lin(V("xt", b, 1024, 4), I(V("yw", 256 * b, 256 * b + 256), V("offr")), 0.03125, 0.0, "sv"[b % 2])
+            for a, e in ((0, 8), (8, 16)) if b >= 2 else ((0, 16),):
+                lin(V("xt", 64 * a + b, 64 * e, 4), I(V("yw", 256 * b, 256 * b + 256), V("offr", a, e)), 0.03125, 0.0,
+                    "sv"[b % 2])
         for a, b in ((0, 128), (128, 256)):
             quant(V("qx", a, b), V("sx", a, b), V("xt", 4 * a, 4 * b))
         ts(V("sq", 0, 240), V("tab"), o_(0), A.not_equal, 256.0, A.mult)
-        act(V("sq", 256, 496), V("tab"), -16.0, F.Square, C("o16", 31))
+        lin(C("o16", 0), o_(1), 16.0, 0.0, "s")
+        act(V("sq", 256, 496), V("tab"), -16.0, F.Square, C("o16", 0))
         for a in (0, 256):
             scan(V("ab", a, a + 256), V("sq", a, a + 256), V("ones", 0, 256), A.min, A.add)
         lin(V("r2", 0, 32, 2), V("ab", 15, 256, 16), -1.0, 16.0, "s")
@@ -505,14 +545,6 @@ def rank_program(g, core, T, topo):
         tt(V("nw", 17, 288, 18), V("ab", 271, 512, 16), V("ab", 15, 256, 16), A.subtract)
         tt(V("do", 0, 3), V("osn", 15, 48, 16), V("osn", 31, 64, 16), A.subtract)
         ts(C("t2", 0), C("ms", 15), o_(2), A.is_equal, C("do", 2), A.mult)
-
-        def mark(i, k):
-            ts(V("nw", 1 + i, 288, 9), V("r2"), k, A.not_equal)
-
-        def hop(s, i, e):
-            scan(V("wk", 16 * s, 16 * s + 15), V("nw", 1 + i + 9 * e, 270, 18), V("df", 0, 15), A.mult, A.add)
-            return C("wk", 16 * s + 14)
-
         ts(V("nw", 1, 288, 9), V("r2"), C("t2", 0), A.add, o_(2), A.not_equal)
         mark(2, hop(1, 0, 1))
         mark(1, hop(0, 0, 0))
@@ -520,27 +552,28 @@ def rank_program(g, core, T, topo):
         mark(3, hop(2, 1, 0))
         mark(5, hop(4, 4, 0))
         scan(V("nc"), V("nw"), V("md"), A.mult, A.add)
-        ts(V(cur, 1, 640, 5), V(cur, 4, 640, 5), -LIFT, A.add, o_(0), A.is_equal)
+        act(V(cur, 1, 640, 5), I(V("sq", 0, 256), l_xy), -1.0, F.Relu, 1.0)
         ts(V(cur, 0, 640, 5), V(cur, 4, 640, 5), -LIFT, A.add, o_(1), A.is_equal)
         tt(V("ev"), V(cur, 1, 80, 5), V(cur, 0, 80, 5), A.subtract)
         lin(V("hm", 3, 560, 5), I(V("ev"), l_y), BIG, 1.0, "s")
         lin(V("hm", 4, 560, 5), I(V("ev"), l_x), 1.0, 1.0 / BIG, "s")
         lin(C("dof", 0), C("do", 0), BIG, 0.0, "s")
         lin(V("hm", 2, 560, 5), I(V("nc"), l_cx), C("dof", 0), 0.0, "s")
-        act(V(cur, 82, 640, 5), I(V("nc"), l_wx))
+        lin(V(cur, 82, 640, 5), I(V("nc"), l_wx), 1.0, 0.0, "v" if last else "s")
         act(V(cur, 83, 640, 5), I(V("nc"), l_wy))
         scan(V(new, 80, 640), V("hm"), V(cur, 80, 640), A.mult, A.add)
-        lin(V("tabo" if last else "tab", 0, 240), I(V(new), l_tab), 1.0, -LIFT, "s")
+        for a, b, q in ((0, 8, "v"), (8, 15, "s")) if last else ((0, 15, "s"),):
+            lin(V("tabo" if last else "tab", 16 * a, 16 * b), I(V(new), V("tu", 48 + a, 48 + b)), 1.0, -LIFT, q)
 
+    now[0] = ROUNDS
     store("y", T.ot[:], T.tabo[:], [V("tabo")])
-    for k, q in enumerate("sv"):
-        a = 128 * k
+    for a in (0, 128):
         mm(V("psY", 4 * a, 4 * a + 128), V("qv"), V("sv"), V("qx", a, a + 128), V("sx", a, a + 128))
-        lin(V("yo", a, a + 128), V("psY", 4 * a, 4 * a + 128), 1.0, 0.0, q)
+        cp(V("yo", a, a + 128), V("psY", 4 * a, 4 * a + 128))
     store("s", T.y[:], T.yo[:], [V("yo")])
     store("y", T.oc[:], T.qx[:].bitcast(dt.uint8), [V("qx")])
     for k in range(4):
-        store("ys"[k % 2], T.osc[4 * k:4 * k + 4, :], T.sx[32 * k:32 * k + 4, :], [V("sx")], 0)
+        store("ys"[k % 2], T.osc[4 * k:4 * k + 4, :], T.sx[32 * k:32 * k + 4, :], [V("sx")], 0, "<sx%d" % k)
 
     if not ORDER:
         ORDER.extend(arrange(ops))

from concourse.mybir import dt, AluOpType, ActivationFunctionType

A = AluOpType
F = ActivationFunctionType
ROUNDS = 3
C4, U8, BF, F32, I32, U16 = "float8_e4m3fn_x4", "uint8", "bfloat16", "float32", "int32", "uint16"
SB = {
    BF: dict(xin=1024, uin=512, vin=512, et=1032, ones=516, xt=1024, ioc=96, d0r=240, kjp=240, d1o=240,
             mk=96, nm=96, gg=240, rs=256, ne=240, osn=240, o16=2, lk=192, ms=192,
             fh=1024, a1=384, a2=576, zt=896, z32=896, yw=1024, tab=240, sq=512, ab=512, df=16, t2=2, rk=16,
             nw=288, md=288, nc=288, do=4, wk=80, r2=32, ev=16, hm=560, pa=640, pb=640),
    F32: dict(pc=16, iop=18, w1=32, w3=32, w4=64, w5=64, w6=64, w8=32, lf=18, tf=64, tt=512, ap=240, rv=32, rvt=32,
              tabo=256, ix=208, kw=112, ka=16, kb=16, kc=16, dof=2, yo=256),
    I32: dict(trii=256, pi=4, w2=32, w7=32),
    U16: dict(lu=76, tu=64, ixu=12, offo=16, offm=12, offr=16),
    C4: dict(wq=512, qu=128, qv=128, qe=512, qn=256, qp=272, qx=256, qs0=128, qs1=128, qs2=128, qa0=224, qa1=224, qa2=224),
    U8: dict(wsc=512, su=128, sv=128, se=512, sn=256, sp=272, sx=256, ss0=128, ss1=128, ss2=128, sa0=224, sa1=224, sa2=224),
}
SCRATCH = {name: ("sbuf", [128, n], t) for t, d in SB.items() for name, n in d.items()}
SCRATCH.update({"psS": ("psum", [128, 512], F32), "psF": ("psum", [128, 2048], F32), "psY": ("psum", [128, 1536], F32)})
SEMAPHORES = ["cv", "cs", "ct", "cg", "sent"] + ["arr%d" % r for r in range(ROUNDS)] + ["dm%d" % k for k in range(16)]
COUNTER = {"v": "cv", "s": "cs", "t": "ct", "g": "cg"}
BIG = 1024.0
LIFT = 128.0
FULL = (16 * 105 + 4 * 15 + 244 / 16) * 16 / 15

SPAN, BEGIN, LATE = 8.72, 2.53, 1.3
ROUND = """
scores, F, ranks:    .32 psY0 .55 psS0 .65 psF0 .8 psF512 .95 psF1024 1.1 psF1536 .61 tt96 .72 tt0 .85 tt224 .96 tt352
                     1.0 ap0 1.29 ap96 1.54 gg0 1.74 gg96 2.0 rs0 2.2 rs96 1.53 fh0 1.81 fh256 2.09 fh512 2.37 fh768
order, third points: 2.46 ne0 2.67 ne112 2.9 ix0 2.99 osn0 3.04 rk0 3.1 osn112 3.19 ixu0 3.24 offo0 3.29 ix112
                     3.37 offo6 3.44 lk0 3.63 ixu6 3.83 ms0 3.88 lk96 4.08 offm0 4.24 ms96 5.08 offm6
slots that travel:   3.6 a10 3.8 a196 4.0 a1192 4.2 a1288 4.33 zt0 4.52 zt1 4.7 zt2 4.89 zt3 5.28 qs0
                     5.6 >qs0 5.8 >ss0 6.0 landed 5.6 z320
slots that stay:     4.5 a20 4.77 a2144 5.04 a2288 5.31 a2432 5.4 zt512 5.64 zt513 5.88 zt514 6.07 zt515 6.4 qa96
                     5.98 yw192 6.1 yw448 6.22 yw704 6.83 yw960 6.45 z32512 6.65 offr1 6.66 rv0 6.67 rv16 6.9 rvt0
                     7.42 offr0 6.7 psS0' 6.79 psY0' 6.88 psY512 6.97 psY1024 7.07 yw96 7.15 yw352 7.23 yw608 7.31 yw864
new state:           7.2 psF0' 7.29 psF512' 7.38 psF1024' 7.47 psF1536' 7.5 yw0 7.58 yw256 7.66 yw512 7.74 yw768
                     7.78 xt0 7.82 xt1 8.21 xt2 8.23 xt3 8.46 xt514 8.46 xt515 8.72 qx0 8.96 qx128
rows, cycle:         3.3 o160 3.4 sq256 3.68 do0 3.73 sq0 4.13 ab0 4.29 t20 4.45 r20 5.12 ab256 5.22 nw1 5.59 df0
                     5.83 wk16 5.85 wk0 6.26 nw3 6.3 nw2 6.35 nw17 6.55 wk48 6.6 wk32 6.8 nw5 6.85 nw4 7.05 wk64
                     7.39 nw6 8.84 nc0
new table:           6.34 dof0 6.7 pt0 6.95 pt1 7.44 ev0 8.75 hm3 8.97 hm4 9.2 hm2 9.42 pt82 9.95 pt83 10.98 pt80
                     11.4 tab0
"""
CHANGED = {0: "7.45 pt0 7.45 pt1 7.7 nc0 7.8 ev0 7.9 hm2 8.0 hm3 8.2 hm4 8.3 pt82 10.05 pt83",
           ROUNDS - 1: """5.1 pt0 6.0 pt1 6.62 ev0 6.96 hm3 7.2 hm4 7.8 nc0 8.45 hm2 8.7 pt82 8.75 pt83 9.1 pt80
                          9.5 tabo0 9.5 tabo128"""}
START = """
loads:    -9 <xin0 -8 <uin0 1.7 <trii0 1.8 <wq0 1.9 <wsc0 2.0 <vin0
GpSimd:   0 pi0 .13 iop0 .41 et0 1.44 lf0 1.64 d0r0 2.21 kjp0 2.74 d0r0' 2.9 rs240 3.06 ioc0 3.35 nm0 3.68 zt384
          4.0 sq240 4.2 sq496 4.4 w432 4.6 r21 4.8 pt0 5.1 md0 5.7 nw0 6.3 md16 6.5 pt0' 6.8 tabo240
Vector:   0 ones0 .33 pi1 .38 pi2 .44 pi3 .49 ka0 .55 kc0 .63 pc0 .74 kb0 1.01 w10 1.06 w116 1.12 pc4 1.17 lu68
          1.22 kc1 1.32 w20 1.37 w60 1.42 lu50 1.47 offo14 1.57 w70 1.62 w632 1.67 lu66 1.72 qn0 1.96 lu0 2.01 w30
          2.06 qe0 2.2 qp0 2.43 w80 2.48 qu0 2.6 qp128 2.85 lu18 2.9 qe256 3.02 qe128 3.63 qe384 4.6 mk0 4.65 pc7
          4.66 w48 4.8 tab0 5.7 w50 8.0 tf8 8.05 w516 8.7 w448 8.9 pc10 8.95 offr0 9.0 w448' 9.25 tf48 9.45 tu0
          9.7 pt4 9.9 qv0
Scalar:   .41 et516 .5 d1o0 .9 pc3 .97 d1o15 1.05 pc6 1.12 pc9 1.19 pc8 1.26 w416 1.33 tf0 1.4 tf40 1.47 w40 1.54 tf16
          1.64 et517 2.2 sp0 2.45 sp128 2.72 kw0 2.95 hm0 3.11 hm1 3.3 rv15 8.1 w532 8.15 tf24 8.2 tf41 8.45 w548
"""
END = "9.12 <qx0 9.17 <sx1 9.22 <sx0 9.32 <sx2 9.37 <sx3 9.32 psY0 9.52 psY512 9.62 yo0 9.82 yo128 10.0 <yo0 10.3 <tabo0"
GUESS = [dict(same=240, other=240, late=105, flight=960, first=1800, act=80, gather=80, rate=1.7),
         dict(same=255, other=260, late=0, flight=650, first=1600, act=80, gather=112, rate=1.58)]
LOCAL, DMA, ISSUE, SWEEPS, REACH = 900, 230, 240, 4, 5
ORDER = []


def V(name, a=0, b=None, s=1):
    return (name, a, SCRATCH[name][1][1] if b is None else b, s)


def C(name, a):
    return (name, a, a + 1, 1)


def I(win, off):
    return ("@", win, off)


def is_view(x):
    return isinstance(x, tuple)


def size(v):
    return 16 * size(v[2]) if v[0] == "@" else len(range(v[1], v[2], v[3]))


def depends(ops):
    writer, readers, deps = {}, {}, []

    def cells(v):
        name, a, b, s = v
        if SCRATCH[name][0] == "psum":
            return [(name, k) for k in range(a // 512, (b - 1) // 512 + 1)]
        return [(name, k) for k in range(a, b, s)]

    for i, op in enumerate(ops):
        d = set()
        rd = [c for v in op["r"] for c in cells(v)]
        wr = [c for v in op["w"] for c in cells(v)]
        for c in rd:
            if c in writer:
                d.add(writer[c])
            if SCRATCH[c[0]][0] == "psum":
                d.update(j for j in readers.get(c, ()) if ops[j]["q"] != op["q"])
        for c in wr:
            if c in writer:
                d.add(writer[c])
            d.update(readers.get(c, ()))
        for c in rd:
            readers.setdefault(c, set()).add(i)
        for c in wr:
            writer[c] = i
            readers[c] = set()
        d.discard(i)
        deps.append(d)
    return deps


def planned(ops):
    def read(text):
        words = " ".join(line.split(":")[-1] for line in text.split("\n")).split()
        return {name: float(t) for t, name in zip(words[0::2], words[1::2])}

    out, seen = [], set()
    for op in ops:
        r, name = op["round"], op["name"]
        if (r, name) in seen:
            name += "'"
        seen.add((r, name))
        if r < 0:
            out.append(read(START)[name])
            continue
        k = min(r, ROUNDS - 1)
        own = read(END if r == ROUNDS else CHANGED.get(r, ""))
        t = own[name] if name in own else read(ROUND)[name]
        waits = k > 0 or (name not in own and t >= read(ROUND)["psF0'"])
        out.append(BEGIN + k * SPAN + t + (LATE if waits else 0))
    return out


def arrange(ops):
    deps = depends(ops)
    for i, op in enumerate(ops):
        deps[i].update(op.get("after", ()))
    n, queue, above = len(ops), [op["q"] for op in ops], []
    for d in deps:
        implied = set().union(*[above[j] for j in d])
        above.append(implied | d)
        d -= implied
    succ = [[k for k in range(i + 1, n) if i in deps[k]] for i in range(n)]
    key, left, order = planned(ops), [len(d) for d in deps], []
    ready = [i for i in range(n) if not left[i]]
    while ready:
        i = min(ready, key=lambda k: (key[k], k))
        ready.remove(i)
        order.append(i)
        for k in succ[i]:
            left[k] -= 1
            if not left[k]:
                ready.append(k)
    guesses = [([op["hold"](u) for op in ops], [op["hold"](u) + op["more"](u) for op in ops],
                [[(j, u["same"] if queue[j] == queue[i] else u["other"]) for j in deps[i]] for i in range(n)])
               for u in GUESS]

    def length(order):
        total = 0
        for hold, span, waits in guesses:
            free, done = {}, [0.0] * n
            for i in order:
                t = free.get(queue[i], 0.0)
                for j, w in waits[i]:
                    if done[j] + w > t:
                        t = done[j] + w
                free[queue[i]] = t + hold[i]
                done[i] = t + span[i]
            total += max(done) + 0.3 * sum(done) / n
        return total

    now = length(order)
    for _ in range(SWEEPS):
        for i in range(n):
            p, better = order.index(i), None
            for step, stop in ((-1, deps[i]), (1, succ[i])):
                k, passed = p, 0
                while passed < REACH and 0 <= k + step < n and order[k + step] not in stop:
                    k += step
                    if queue[order[k]] == queue[i]:
                        passed += 1
                        moved = order[:p] + order[p + 1:]
                        moved.insert(k, i)
                        t = length(moved)
                        if t < now - 1e-6:
                            now, better = t, moved
            order = better or order
    return order


def issue(ops, g, T):
    queue = {"v": g.vector, "s": g.scalar, "t": g.tensor, "g": g, "y": g.sync}
    deps = depends(ops)
    known = {q: set() for q in queue}
    clock, waits = [], []
    for i, op in enumerate(ops):
        if op["kind"] == "arrive":
            clock.append(set())
            waits.append([])
            continue
        k = known[op["q"]]
        mine = []
        for j in sorted(deps[i], reverse=True):
            if j in k:
                continue
            mine.append(j)
            k.add(j)
            k.update(clock[j])
            if ops[j]["kind"] == "compute":
                for e in range(j):
                    if ops[e]["kind"] == "compute" and ops[e]["q"] == ops[j]["q"] and e not in k:
                        k.add(e)
                        k.update(clock[e])
        waits.append(mine)
        clock.append(set(k))
    needed = set(j for w in waits for j in w)
    token, count, ndma, open_dma = {}, {q: 0 for q in COUNTER}, [0], []
    for i, op in enumerate(ops):
        if op["kind"] == "arrive":
            token[i] = (op["sem"], op["n"])
        elif op["kind"] == "compute" and i in needed:
            count[op["q"]] += 1
            token[i] = (COUNTER[op["q"]], count[op["q"]])
        elif op["kind"] == "dma":
            token[i] = ("dm%d" % ndma[0], 16)
            ndma[0] += 1
            if i not in needed:
                open_dma.append(i)
    for i, op in enumerate(ops):
        if op["kind"] == "arrive":
            continue
        q = queue[op["q"]]
        for j in waits[i]:
            q.wait_ge(T.sem[token[j][0]], token[j][1])
        ins = op["f"](q)
        if i in token:
            ins.then_inc(T.sem[token[i][0]], 16 if op["kind"] == "dma" else 1)
    for i in open_dma:
        queue[ops[i]["q"]].wait_ge(T.sem[token[i][0]], 16)


def rank_program(g, core, T, topo):
    rank = T.rank_of(core)
    if rank is None:
        return
    n = len(T.cores)
    nxt, prv = T.cores[(rank + 1) % n], T.cores[(rank - 1) % n]
    rid, pid, _ = topo.addr(nxt)
    mask = topo.mask(core, nxt)
    n_out, n_in = len(topo.engines(core, nxt)), len(topo.engines(prv, core))
    ops, now = [], [-1]

    def ap(x, word=None):
        if not is_view(x):
            return x
        if x[0] == "@":
            return ap(x[1], word).indirect(ap(x[2]))
        name, a, b, s = x
        v = T[name][:, a:b] if s == 1 else T[name][:, a:b:s]
        return v.bitcast(word) if word is not None else v

    def flat(xs):
        out = []
        for x in xs:
            if is_view(x):
                out += [x[1], x[2]] if x[0] == "@" else [x]
        return out

    def rec(q, f, r, w, kind="compute", hold=None, more=0, slow=1, first=False, name=None):
        def cycles(u):
            if hold is not None:
                return hold + (u["first"] if first else 0)
            if r and r[0][0] == "@":
                return (60 if q == "v" else u["gather"]) + u["rate"] * size(r[0])
            if q == "s":
                return u["act"] + size(w[0])
            narrow = all(SCRATCH[x[0]][2] in (BF, U16) for x in flat([r[0], w[0]] if r else w))
            return max(64, size(w[0]) * (0.5 if narrow else 1) * slow)
        buf, col = (w or r)[0][:2]
        buf = {"pa": "pt", "pb": "pt"}.get(buf, buf[:2] if buf[:2] in ("qs", "ss", "qa") and now[0] >= 0 else buf)
        ops.append({"q": q, "f": f, "r": flat(r), "w": flat(w), "kind": kind, "round": now[0], "hold": cycles,
                    "more": lambda u: more + (u["late"] if q == "s" and kind == "compute" else 0),
                    "name": name or {"dma": "<", "remote": ">"}.get(kind, "") + buf + str(col)})

    def cp(o, i, word=None):
        rec("v", lambda q: q.tensor_copy(ap(o, word), ap(i, word)), [i], [o])

    def tt(o, a, b, op):
        rec("v", lambda q: q.tensor_tensor(ap(o), ap(a), ap(b), op), [a, b], [o], slow=1 if a[0][:2] == "ps" else 2)

    def ts(o, a, s1, op0, s2=None, op1=None):
        if op1 is None:
            rec("v", lambda q: q.tensor_scalar(ap(o), ap(a), ap(s1), None, op0), [a, s1], [o])
        else:
            rec("v", lambda q: q.tensor_scalar(ap(o), ap(a), ap(s1), ap(s2), op0, op1), [a, s1, s2], [o])

    def scan(o, d0, d1, op0, op1, first=0.0):
        rec("v", lambda q: q.tensor_tensor_scan(ap(o), ap(d0), ap(d1), ap(first), op0, op1), [d0, d1, first], [o])

    def mset(o, c):
        rec("v", lambda q: q.memset(ap(o), c), [], [o])

    def tr(o, i):
        rec("v", lambda q: q.transpose(ap(o), ap(i)), [i], [o])

    def quant(qc, sc, i):
        rec("v", lambda q: q.quantize_mx(ap(qc), ap(sc), ap(i)), [i], [qc, sc], hold=15 + 0.27 * size(i))

    def act(o, i, scale=None, func=F.Copy, bias=None):
        kw = {}
        if scale is not None:
            kw["scale"] = ap(scale)
        if bias is not None:
            kw["bias"] = ap(bias)
        rec("s", lambda q: q.activation(ap(o), ap(i), func, **kw), [i, bias, scale], [o])

    def lin(o, i, scale, bias, q="v"):
        if q == "s":
            act(o, i, scale, F.Identity, bias)
        else:
            ts(o, i, scale, A.mult, bias, A.add)

    def mm(o, lq, ls, rq, rsc):
        rec("t", lambda q: q.matmul_mx(ap(o), ap(lq), ap(ls), ap(rq), ap(rsc), True, True), [lq, ls, rq, rsc], [o],
            hold=0.7 * (size(o) + 16))

    def iota(o, pattern, base, cm=0, small=True):
        kw = {"allow_small_or_imprecise_dtypes": True} if small else {}
        rec("g", lambda q: q.iota(ap(o), pattern, base, cm, **kw), [], [o], hold=160 + 2 * size(o))

    def select(o, i, pattern, op, fill, base=0, cm=0):
        rec("g", lambda q: q.affine_select(ap(o), ap(i), pattern, op, fill, base, cm), [i], [o], hold=200 + 2 * size(o))

    def load(o, src, word=None, after=(), more=500):
        rec("y", lambda e: e.dma_start(ap(o, word), src), list(after), [o], "dma", DMA, LOCAL + more)

    def store(q, dst, src, reads, more=400, name=None):
        rec(q, lambda e: e.dma_start(dst, src), reads, [], "dma", DMA, LOCAL + more, name=name)

    def send(dst, src, sem, word=None, first=False):
        rec("g", lambda q: q.remote_dma(ap(dst, word), ap(src, word), T.sem[sem], T.sem.sent, pid, rid, mask),
            [src], [], "remote", ISSUE, first=first)

    load(V("xin"), T.x[:], more=600)
    load(V("uin"), T.u[:], more=1100)
    load(V("trii"), T.tri[:], None, [C("xin", 0)])
    load(V("wq"), T.wc[:], dt.uint8, [C("xin", 0)])
    load(V("wsc"), T.ws[:], None, [C("xin", 0)])
    load(V("vin"), T.v[:], None, [C("xin", 0)])

    q_, h_, p32, c16, c16q = C("pc", 0), C("pc", 1), C("pc", 2), C("pc", 3), C("pc", 4)
    iota(C("pi", 0), [[0, 1]], 0, 1, False)
    iota(V("iop"), [[1, 18]], 0)
    mset(V("ones"), 1.0)
    iota(V("ioc"), [[0, 6], [1, 16]], 0)
    select(V("d0r"), V("ones", 0, 240), [[1, 15], [-1, 16]], A.not_equal, -1.0)
    iota(V("kjp"), [[1, 15], [-1, 16]], 0)
    iota(V("d0r", 0, 240, 16), [[0, 15]], 0)
    iota(V("rs", 240, 256), [[0, 16]], 99)
    select(V("nm"), V("ones", 0, 96), [[0, 6], [1, 16]], A.is_gt, 0.0)
    iota(V("sq", 240, 256), [[256, 16]], 0)
    iota(V("sq", 496, 512), [[256, 16]], 0)
    iota(V("zt", 384, 512), [[0, 128]], 0)
    iota(V("r2", 1, 32, 2), [[1, 16]], 0)
    for p in ("pa", "pb"):
        iota(V(p, 0, 80), [[1, 16], [0, 5]], int(LIFT))
    select(V("md"), V("ones", 0, 288), [[0, 16], [1, 18]], A.is_equal, 0.0)
    iota(V("md", 16, 288, 18), [[0, 16]], -1)
    select(V("nw"), V("ones", 0, 288), [[0, 16], [1, 18]], A.not_equal, 0.0)
    iota(V("tabo", 240, 256), [[1, 16]], 0)
    iota(V("w4", 32, 48), [[5, 16]], 4)
    select(V("lf"), V("iop"), [[1, 18]], A.is_gt, 16.0)
    ts(C("pi", 1), C("pi", 0), 15, A.bitwise_and)
    ts(C("pi", 2), C("pi", 0), 4, A.arith_shift_right, 1, A.bitwise_and)
    ts(C("pi", 3), C("pi", 0), 31, A.bitwise_and)
    cp(V("pc", 0, 3), V("pi", 1, 4))
    ts(c16q, q_, 16.0, A.mult)
    lin(c16, q_, 1.0, 16.0, "s")
    ts(V("lu", 0, 18), V("lf"), c16q, A.add, -1.0, A.add)
    ts(V("w1", 0, 16), V("iop", 0, 16), q_, A.min, 1.0, A.add)
    ts(V("w1", 16, 32), V("iop", 0, 16), q_, A.max, 1.0, A.add)
    ts(V("w2"), V("w1"), h_, A.add)
    ts(V("w6", 0, 32), V("w1"), h_, A.subtract, 7.0, A.is_ge)
    ts(V("w7"), V("w2"), 1, A.bitwise_and)
    lin(V("w6", 32, 64), V("w6", 0, 32), 16.0, -7.0)
    tt(V("w3"), V("w6", 32, 64), V("w7"), A.mult)
    tt(V("w8"), V("w3"), V("w1"), A.add)
    lin(V("lu", 18, 50), V("w8"), 16.0, 96.0)
    ts(V("lu", 68, 76), V("iop", 0, 8), 0.0, A.mult, q_, A.add)
    lin(V("lu", 50, 58), V("lu", 68, 76), 16.0, 14.0)
    cp(C("lu", 66), p32)
    act(V("d1o"), V("ones", 0, 240), -1.0)
    act(V("d1o", 15, 240, 16), V("ones", 0, 15), 15.0)
    lin(V("ka"), V("iop", 0, 16), 4.0, 1.0)
    rec("v", lambda q: q.reciprocal(ap(V("kb")), ap(V("ka"))), [V("ka")], [V("kb")], hold=330)
    lin(V("kc", 1, 16), V("kb", 1, 16), -4.0, 1.0)
    mset(C("kc", 0), 61.0 / 16)
    act(V("kw"), I(V("kc"), V("lu", 68, 75)))
    ts(V("mk"), V("ioc"), q_, A.is_equal)
    select(V("et", 0, 516), V("ones"), [[1, 516]], A.is_equal, 0.0, -2, -4)
    act(V("et", 517, 1032), V("et", 0, 515))
    act(V("et", 516, 517), V("ones", 0, 1), 0.0)
    for b in range(4):
        o = 516 * (b % 2) + (2 if b < 2 else 0)
        quant(V("qe", 128 * b, 128 * b + 128), V("se", 128 * b, 128 * b + 128), V("et", o, o + 512))
    lin(C("pc", 6), q_, 1.0, 1.0, "s")
    ts(C("pc", 7), q_, 15.0, A.not_equal, 80.0, A.mult)
    lin(C("pc", 8), q_, 5.0, 1204.0, "s")
    lin(C("pc", 9), q_, 1.0, 240.0, "s")
    lin(V("w4", 0, 8), V("iop", 0, 8), 1.0, C("pc", 6), "s")
    ts(V("w4", 8, 16), V("w4", 0, 8), 15.0, A.is_ge, -15.0, A.mult)
    tt(V("tf", 8, 16), V("w4", 0, 8), V("w4", 8, 16), A.add)
    lin(V("tf", 0, 8), V("iop", 0, 8), 0.0, q_, "s")
    lin(V("tf", 16, 24), V("tf", 0, 8), 18.0, 16.0, "s")
    lin(V("tf", 24, 40), V("tf", 0, 16), 18.0, 17.0, "s")
    lin(V("tf", 41, 48), V("tf", 8, 15), 1.0, c16q, "s")
    lin(C("tf", 40), q_, 16.0, 15.0, "s")
    lin(V("w4", 16, 32), V("iop", 0, 16), -1.0, q_, "s")
    ts(V("w5", 0, 16), V("w4", 16, 32), 0.0, A.is_lt, 15.0, A.mult)
    tt(V("w5", 16, 32), V("w5", 0, 16), V("w4", 16, 32), A.add)
    lin(V("w5", 32, 48), V("w5", 16, 32), C("pc", 7), 0.0, "s")
    lin(V("w5", 48, 64), V("w5", 32, 48), -1.0, C("pc", 8), "s")
    tt(V("w4", 48, 64), V("w5", 32, 48), V("w4", 32, 48), A.add)
    tt(V("w4", 48, 64), V("w4", 48, 64), V("w5", 48, 64), A.min)
    ts(C("pc", 10), q_, 15.0, A.not_equal, 79.0, A.mult)
    ts(V("tf", 48, 64), V("w4", 48, 64), C("pc", 10), A.max)
    cp(V("tu"), V("tf"))
    l_x, l_y, l_cx, l_wx, l_wy = [V("tu", 8 * k, 8 * k + 7) for k in range(5)]
    l_xy = V("tu", 40, 48)
    act(V("hm", 0, 560, 5), V("ones", 0, 112), 0.0)
    act(V("hm", 1, 560, 5), V("ones", 0, 112), -1.0)
    lin(V("rv", 15, 32, 16), V("iop", 0, 2), 0.0, C("pc", 9), "s")
    cp(C("offo", 14), q_)
    cp(C("offr", 0), C("pc", 9))

    quant(V("qn"), V("sn"), V("xin"))
    for a, b in ((0, 8), (8, 17)):
        cp(V("qp", 16 * a, 16 * b), I(V("qn"), V("lu", a, b)), dt.uint32)
        act(V("sp", 16 * a, 16 * b), I(V("sn"), V("lu", a, b)))
    quant(V("qu"), V("su"), V("uin"))
    quant(V("qv"), V("sv"), V("vin"))
    ts(V("pa", 4, 640, 5), I(V("trii"), l_xy), LIFT, A.add)
    cp(V("tab"), V("trii", 0, 240))

    def o_(j):
        return C("osn", 16 * j + 15)

    def plane(b):
        return V("fh", 256 * b, 256 * b + 256)

    def w_(b):
        return V("wq", 128 * b, 128 * b + 128), V("wsc", 128 * b, 128 * b + 128)

    def mark(i, k):
        ts(V("nw", 1 + i, 288, 9), V("r2"), k, A.not_equal)

    def hop(s, i, e):
        scan(V("wk", 16 * s, 16 * s + 15), V("nw", 1 + i + 9 * e, 270, 18), V("df", 0, 15), A.mult, A.add)
        return C("wk", 16 * s + 14)

    ybank = [("psS", 0), ("psY", 0), ("psY", 512), ("psY", 1024)]

    for r in range(ROUNDS):
        last = r == ROUNDS - 1
        now[0] = r
        qs, ss, qa, sa = "qs%d" % r, "ss%d" % r, "qa%d" % r, "sa%d" % r
        qx, sx, ns = ("qp", "sp", 272) if r == 0 else ("qx", "sx", 256)
        cur, new = ("pb", "pa") if r % 2 else ("pa", "pb")
        for name, a, b in (("psY", 0, 128), ("psS", 112, ns)):
            mm(V(name, 0, b - a), V("qu"), V("su"), V(qx, a, b), V(sx, a, b))
        for b in range(4):
            mm(V("psF", 512 * b, 512 * b + 256), V("qe", 128 * b, 128 * b + 128), V("se", 128 * b, 128 * b + 128),
               V(qx, 0, 256), V(sx, 0, 256))
            act(plane(b), V("psF", 512 * b, 512 * b + 256), 0.5)
        for o, name, a, b in ((96, "psY", 0, 128), (0, "psY", 16, 112), (224, "psS", 16, 144), (352, "psS", 0, 160)):
            tr(V("tt", o, o + b - a), V(name, a, b))
        act(V("ap", 0, 96), I(V("tt", 0, 224), V("lu", 18, 24)))
        cp(V("ap", 96, 240), I(V("tt"), V("lu", 24, 33)))
        for a, b in ((0, 6), (6, 15)):
            tt(V("gg", 16 * a, 16 * b), I(V("tt"), V("lu", 34 + a, 34 + b)), V("ap", 16 * a, 16 * b), A.is_gt)
            scan(V("rs", 16 * a, 16 * b), V("d0r", 16 * a, 16 * b), V("gg", 16 * a, 16 * b), A.mult, A.add)
        for j0, j1, j in ((0, 7, 0), (7, 15, 6)):
            a, b, e = 16 * j0, 16 * j1, 16 * j
            tt(V("ne", a, b), I(V("rs"), V("lu", 50, 50 + j1 - j0)), V("kjp", a, b), A.not_equal)
            scan(V("ix", a, min(b, 208)), V("kw", 0, min(b, 208) - a), V("ne", a, min(b, 208)), A.mult, A.add,
                 C("ix", a - 1) if a else FULL / 244 + 1)
            scan(V("osn", a, b), V("ne", a, b), V("d1o", a, b), A.mult, A.add)
            ts(V("offo", j, j1 - 1), V("osn", e + 31, b, 16), 16.0, A.mult, c16, A.add)
            lin(V("ixu", j, j + 6), V("ix", e + 30, e + 112, 16), -228.0, FULL - 4.72)
            tt(V("lk", e, e + 96), I(V("tab" if r else "trii"), V("ixu", j, j + 6)), V("mk"), A.mult)
            scan(V("ms", e, e + 96), V("nm"), V("lk", e, e + 96), A.mult, A.add)
            ts(V("offm", j, j + 6), V("ms", e + 15, e + 96, 16), 16.0, A.mult, c16, A.add)
        for b in range(4):
            act(V("a1", 96 * b, 96 * b + 96), I(plane(b), V("offo", 0, 6)))
            tt(V("zt", b, 384, 4), I(plane(b), V("offm", 0, 6)), V("a1", 96 * b, 96 * b + 96), A.add)
        quant(V(qs), V(ss), V("zt", 0, 512))
        send(V(qa, 0, 96), V(qs, 0, 96), "arr%d" % r, dt.uint8, r == 0)
        send(V(sa, 0, 96), V(ss, 0, 96), "arr%d" % r)
        ops.append({"kind": "arrive", "q": "a", "r": [], "w": [V(qa, 0, 96), V(sa, 0, 96)], "sem": "arr%d" % r,
                    "n": 2 * n_in, "after": [len(ops) - 2, len(ops) - 1], "round": r, "name": "landed",
                    "hold": lambda u: 0, "more": lambda u: u["flight"]})
        for b in range(4):
            act(V("a2", 144 * b, 144 * b + 144), I(plane(b), V("offo", 6, 15)))
            tt(V("zt", 512 + b, 896, 4), I(plane(b), V("offm", 6, 12)), V("a2", 144 * b, 144 * b + 96), A.add)
            act(V("yw", 256 * b + 192, 256 * b + 256), V("a2", 144 * b + 80, 144 * b + 144), 64.0)
        quant(V(qa, 96, 224), V(sa, 96, 224), V("zt", 384, 896))
        act(V("z32", 0, 384), V("zt", 0, 384), 32.0)
        act(V("z32", 512, 896), V("zt", 512, 896), 32.0)
        tt(V("rk", 0, 15), V("rs", 14, 240, 16), V("iop", 0, 15), A.add)
        if last:
            ts(V("rv", 0, 15), V("rk", 0, 15), 16.0, A.mult, q_, A.add)
            ts(V("rv", 16, 31), V("rk", 0, 15), 16.0, A.mult, q_, A.add)
            tr(V("rvt"), V("rv"))
            cp(V("offr"), I(V("rvt"), V("lu", 66, 67)))
        else:
            ts(V("offr", 1, 16), V("rk", 0, 15), 16.0, A.mult, q_, A.add)
        for b in range(4):
            name, o = ybank[b]
            mm(V(name, o, o + 128), *w_(b), V(qa, 96, 224), V(sa, 96, 224))
            tt(V("yw", 256 * b + 96, 256 * b + 192), V(name, o + 32, o + 128), V("z32", 512 + b, 896, 4), A.add)
        for b in range(4):
            mm(V("psF", 512 * b, 512 * b + 128), *w_(b), V(qa, 0, 128), V(sa, 0, 128))
            tt(V("yw", 256 * b, 256 * b + 96), V("psF", 512 * b, 512 * b + 96), V("z32", b, 384, 4), A.add)
        for b in range(4):
            for a, e in ((0, 8), (8, 16)) if b >= 2 else ((0, 16),):
                lin(V("xt", 64 * a + b, 64 * e, 4), I(V("yw", 256 * b, 256 * b + 256), V("offr", a, e)), 0.03125, 0.0,
                    "sv"[b % 2])
        for a, b in ((0, 128), (128, 256)):
            quant(V("qx", a, b), V("sx", a, b), V("xt", 4 * a, 4 * b))
        ts(V("sq", 0, 240), V("tab"), o_(0), A.not_equal, 256.0, A.mult)
        lin(C("o16", 0), o_(1), 16.0, 0.0, "s")
        act(V("sq", 256, 496), V("tab"), -16.0, F.Square, C("o16", 0))
        for a in (0, 256):
            scan(V("ab", a, a + 256), V("sq", a, a + 256), V("ones", 0, 256), A.min, A.add)
        lin(V("r2", 0, 32, 2), V("ab", 15, 256, 16), -1.0, 16.0, "s")
        tt(V("df", 0, 15), V("ab", 287, 512, 16), V("ab", 271, 496, 16), A.subtract)
        tt(V("nw", 17, 288, 18), V("ab", 271, 512, 16), V("ab", 15, 256, 16), A.subtract)
        tt(V("do", 0, 3), V("osn", 15, 48, 16), V("osn", 31, 64, 16), A.subtract)
        ts(C("t2", 0), C("ms", 15), o_(2), A.is_equal, C("do", 2), A.mult)
        ts(V("nw", 1, 288, 9), V("r2"), C("t2", 0), A.add, o_(2), A.not_equal)
        mark(2, hop(1, 0, 1))
        mark(1, hop(0, 0, 0))
        mark(4, hop(3, 2, 0))
        mark(3, hop(2, 1, 0))
        mark(5, hop(4, 4, 0))
        scan(V("nc"), V("nw"), V("md"), A.mult, A.add)
        act(V(cur, 1, 640, 5), I(V("sq", 0, 256), l_xy), -1.0, F.Relu, 1.0)
        ts(V(cur, 0, 640, 5), V(cur, 4, 640, 5), -LIFT, A.add, o_(1), A.is_equal)
        tt(V("ev"), V(cur, 1, 80, 5), V(cur, 0, 80, 5), A.subtract)
        lin(V("hm", 3, 560, 5), I(V("ev"), l_y), BIG, 1.0, "s")
        lin(V("hm", 4, 560, 5), I(V("ev"), l_x), 1.0, 1.0 / BIG, "s")
        lin(C("dof", 0), C("do", 0), BIG, 0.0, "s")
        lin(V("hm", 2, 560, 5), I(V("nc"), l_cx), C("dof", 0), 0.0, "s")
        lin(V(cur, 82, 640, 5), I(V("nc"), l_wx), 1.0, 0.0, "v" if last else "s")
        act(V(cur, 83, 640, 5), I(V("nc"), l_wy))
        scan(V(new, 80, 640), V("hm"), V(cur, 80, 640), A.mult, A.add)
        for a, b, q in ((0, 8, "v"), (8, 15, "s")) if last else ((0, 15, "s"),):
            lin(V("tabo" if last else "tab", 16 * a, 16 * b), I(V(new), V("tu", 48 + a, 48 + b)), 1.0, -LIFT, q)

    now[0] = ROUNDS
    store("y", T.ot[:], T.tabo[:], [V("tabo")])
    for a in (0, 128):
        mm(V("psY", 4 * a, 4 * a + 128), V("qv"), V("sv"), V("qx", a, a + 128), V("sx", a, a + 128))
        cp(V("yo", a, a + 128), V("psY", 4 * a, 4 * a + 128))
    store("s", T.y[:], T.yo[:], [V("yo")])
    store("y", T.oc[:], T.qx[:].bitcast(dt.uint8), [V("qx")])
    for k in range(4):
        store("ys"[k % 2], T.osc[4 * k:4 * k + 4, :], T.sx[32 * k:32 * k + 4, :], [V("sx")], 0, "<sx%d" % k)

    if not ORDER:
        ORDER.extend(arrange(ops))
    issue([ops[i] for i in ORDER], g, T)
    g.wait_ge(T.sem.sent, 2 * ROUNDS * n_out)
